import numpy as np, ml_dtypes
CORES = [5,29,101,125,133,157,229,253]
N = 8
BF = ml_dtypes.bfloat16
def gentries(a):
    return np.ascontiguousarray(a.reshape(8, 16, -1).transpose(0, 2, 1)).reshape(8, -1)
def gtable(e):
    e = np.asarray(e); return np.ascontiguousarray(e.reshape(8, -1, 16).transpose(0, 2, 1)).reshape(128, -1).astype(np.int32)
CN, Q0, S, H, RO, EPS, RHO = 1280, 384, 192, 64, 4, 44, 60
LN = S + H
def pick4(w, ix):
    return np.take_along_axis(w, ix[:, :, None, :], 3)
def noise(rng, m, shape):
    return np.rint((2 * rng.random(shape) - 1) * m).astype(np.int64)
def clip(v):
    return np.minimum(np.maximum(v, 0), 15)
def pos(rng, lo, hi, *shape):
    return (lo + (hi - lo) * rng.random(shape, dtype=np.float32)).astype(BF)
def split(rng, T, m, c):
    r = rng.random(T.shape + (m * c,)); lim = np.take_along_axis(np.sort(r, axis=-1), (T - 1)[..., None], -1)
    return np.moveaxis(np.add.reduce((r <= lim).astype(np.int64).reshape(T.shape + (m, c)), axis=-1), -1, -2)
def parts(rng):
    K = rng.integers(0, 16, (N, 8, 16, Q0)); nb = rng.integers(0, Q0, (N, 8, 16, Q0))
    me = (np.arange(16)[:, None] == rng.integers(0, 16, (N, 8, 1, Q0))) & (rng.random((N, 8, 1, Q0)) < 0.75)
    nb = np.where(me, np.arange(Q0), nb)
    pm = np.argsort(rng.random((N, 8, Q0)), axis=-1); inv = np.argsort(pm, axis=-1)
    home = np.ascontiguousarray(np.tile(pm, (1, 1, CN // Q0 + 1))[..., :CN])
    C = clip(pick4(K, home) + noise(rng, rng.integers(0, 4, (N, 8, 1, CN)), (N, 8, 16, CN)))
    near = inv[:, :, None, :] + Q0 * rng.integers(0, CN // Q0, (N, 8, 16, Q0))
    dl = np.where(rng.random((N, 8, 16, Q0)) < 0.45, near, rng.integers(0, CN, (N, 8, 16, Q0)))
    st = np.take_along_axis(np.argsort(rng.random((N, 8, Q0)), axis=-1), (Q0 * rng.random((N, 8, LN)) ** 2).astype(np.int64), 2)
    j = st[..., :S]; xs = np.zeros((N, 8, 16, RO, S), np.int64); x = None
    for t in range(RO):
        go = np.take_along_axis(pick4(nb, j), rng.integers(0, 16, (N, 8, 1, S)), 2)[:, :, 0]
        stay = (rng.random((N, 8, S)) < 0.5) & (t > 0); j = np.where(stay, j, go)
        z = clip(pick4(K, j) + noise(rng, rng.choice(np.array([1, 3, 5, 8, 12]), (N, 8, 1, S)), (N, 8, 16, S)))
        x = z if x is None else np.where(stay[:, :, None, :], clip(x + noise(rng, 1, x.shape)), z)
        xs[:, :, :, t] = x
    return {"kq": K, "nb": nb, "dl": dl, "cc": C, "aa": pos(rng, 16, 128, N, 8, 16, CN), "xs": xs, "ys": pos(rng, 64, 1024, N, 8, 16, RO, S), "st": st}
def pack(p):
    d = {}
    for k in ("kq", "nb", "dl", "cc", "aa", "xs", "ys"):
        d[k] = np.ascontiguousarray(p[k].reshape(N, 128, -1)).astype(np.int32 if k in ("nb", "dl") else BF)
    d["st"] = np.stack([gtable(a) for a in p["st"]]); return d
def setup_inputs(rng):
    return pack(parts(rng))
def relay(rng, p, pat, g):
    m = H // 3; n = H - 2 * m; X = p["xs"][:, g]
    for a in range(N):
        c = np.zeros((RO, S), np.int64); c[0, :m] = 1; c[1:, :m] = 2; c[:2, m:H] = 4 + a; c[2:, m:H] = 4 + (a - 1) % N
        X[a] = pat[:, c] + rng.integers(-1, 2, (16, RO, S)); X[a, :, 2, :m] = rng.integers(14, 16, (16, m))
    for a in range(N):
        st = rng.permutation(Q0)[:LN]; own, gst = st[:S], st[S:]; p["st"][a, g] = st
        nb = p["nb"][a, g]; nb[:] = np.arange(Q0); nb[1::2][:, own[:H]] = gst
        o = rng.permutation(CN); h = CN // 4; be, b2, b1, b0 = o[:n], o[n:h], o[h:2 * h], o[2 * h:]
        c = p["cc"][a, g]; c[:, b0] = 2 + rng.integers(-1, 2, (16, b0.size)); c[:, b1] = rng.integers(14, 16, (16, b1.size))
        c[:, b2] = pat[:, 2:3] + rng.integers(-1, 2, (16, b2.size))
        x = X[(a - 1) % N, :, 0, 2 * m:H]; z = split(rng, np.full(n, EPS), 16, 4); c[:, be] = np.where(x > 7, x - z, x + z)
        w = np.concatenate([rng.choice(b1, (8, H)), rng.choice(b2, (2, H)), rng.choice(b0, (6, H))]); w[15, 2 * m:] = be
        dl = p["dl"][a, g]; dl[:, own] = rng.choice(b0, (16, S)); dl[:, gst] = rng.permuted(w, axis=0)
        k = p["kq"][a, g]; k[:, own[:m]] = 2; k[:, gst[:m]] = 15
        k[:, own[m:H]] = pat[:, 4 + a][:, None]; k[:, gst[m:]] = pat[:, 4 + (a - 1) % N][:, None]
def far(rng, p, g):
    v = np.exp(-0.015625 * np.arange(EPS + 1, EPS + 9)); far_d = EPS + 1 + int(np.argmax(np.abs(v.astype(BF).astype(np.float64) - v)))
    u = rng.integers(0, 16, (N, 16, 4)); b = np.arange(H) % 4; n = CN // 8
    for a in range(N):
        me, up = u[a], u[(a - 1) % N]
        st = rng.permutation(Q0)[:LN]; own, gst = st[:H], st[S:]; p["st"][a, g] = st
        nb = p["nb"][a, g]; nb[:] = np.arange(Q0); nb[1::2][:, own] = gst
        k = p["kq"][a, g]; k[:, own] = me[:, b]; k[:, gst] = up[:, b]
        X = p["xs"][a, g]; X[:, :2, :H] = me[:, b][:, None, :]; X[:, 2:, :H] = up[:, b][:, None, :]
        Y = p["ys"][a, g]; Y[:, 0, :H] = pos(rng, 1800, 2048, 16, H).astype(np.float32); Y[:, 1:, :H] = pos(rng, 128, 1024, 16, RO - 1, H).astype(np.float32)
        o = rng.permutation(CN)
        for i in range(4):
            c1, c2 = o[2 * i * n:(2 * i + 1) * n], o[(2 * i + 1) * n:(2 * i + 2) * n]
            for x, ix, T, q, lo, hi in ((me[:, i:i + 1], c1, np.full(n, far_d), own[i::4], 124, 128), (up[:, i:i + 1], c2, rng.integers(EPS + 1, 61, n), gst[i::4], 16, 32)):
                z = split(rng, T, 16, 4); p["cc"][a, g][:, ix] = np.where(x > 7, x - z, x + z)
                p["aa"][a, g][:, ix] = pos(rng, lo, hi, 16, n).astype(np.float32)
                p["dl"][a, g][:, q] = rng.choice(ix, (16, q.size))
def setup_inputs_corners(rng):
    p = parts(rng); off = int(rng.integers(0, 8)); vals = (0, 1, 2, 3, H - 1, H, H + 1, S)
    pat = 2 + 10 * np.array([[bin(f & j).count("1") & 1 for j in range(16)] for f in range(16)])
    for a in range(N):
        for g in range(8):
            st = rng.permutation(Q0)[:LN]; own, gst = st[:S], st[S:]; p["st"][a, g] = st
            nb = p["nb"][a, g]; nb[:] = np.arange(Q0); nb[1::2][:, own[:H]] = gst
            o = rng.permutation(CN); h = CN // 2; b0, b1, b2 = o[:h], o[h:h + h // 2], o[h + h // 2:]
            c = p["cc"][a, g]; c[:, b0] = 2 + rng.integers(-1, 2, (16, b0.size)); c[:, b1] = rng.integers(14, 16, (16, b1.size))
            c[:, b2] = pat[:, 1 + np.arange(b2.size) % (RO - 1)] + rng.integers(-1, 2, (16, b2.size))
            dl = p["dl"][a, g]; dl[:, own] = rng.choice(b0, (16, S))
            w = [rng.choice(b1, (8, H))] + [rng.choice(b2[t::RO - 1], (1, H)) for t in range(RO - 1)] + [rng.choice(b0, (9 - RO, H))]
            dl[:, gst] = rng.permuted(np.concatenate(w), axis=0)
            k = p["kq"][a, g]; k[:, own[:H]] = 2; k[:, gst] = 15
            k[:, own[H:]] = pat[:, rng.integers(0, RO, S - H)] + rng.integers(-1, 2, (16, S - H))
            for t in range(RO):
                new = rng.permutation(S) < vals[(a + g + 3 * t + off) % 8]
                x = pat[:, np.where(new & (t < RO - 1), t + 1, 0)] + rng.integers(-1, 2, (16, S))
                if t == RO - 1: x[:, :H] = rng.integers(14, 16, (16, H))
                p["xs"][a, g, :, t] = x
    relay(rng, p, pat, int(rng.integers(0, 8)))
    return pack(p)
def setup_inputs_crowd(rng):
    p = parts(rng)
    for a in range(N):
        for g in range(8):
            o = rng.permutation(Q0); st, nb = p["st"][a, g], p["nb"][a, g]; kind = g // 2
            if (a + g) % 2 == 1:
                st[:] = o[:LN]; nb[:] = np.arange(Q0); p["xs"][a, g] = rng.integers(0, 16, (16, RO, S)); continue
            z = o[:4] if kind == 2 else o[:1]
            nb[:, z] = rng.choice(z, (16, z.size)); st[:] = rng.choice(z, LN)
            if kind == 1 or kind == 3:
                st[LN - 1 if kind == 1 else int(rng.integers(1, S))] = o[5]; nb[:, o[5]] = o[5]
            if kind != 2: p["xs"][a, g][:, :2, 0] = p["cc"][a, g][:, p["dl"][a, g, 0, z[0]]][:, None]
    return pack(p)
def setup_inputs_ends(rng):
    p = parts(rng); sw = (np.arange(N)[:, None] + np.arange(8)) % 2
    hs = 15 * (np.argsort(rng.random((N, 8, 16, 3)), axis=2) < 8)
    pr = np.zeros((N, 8, 16, 8), np.int64); pr[..., 1] = 15; pr[..., 2::2] = hs; pr[..., 3::2] = 15 - hs
    ki = rng.integers(0, 8, (N, 8, Q0)); ci = rng.integers(0, 8, (N, 8, CN)); xi = rng.integers(0, 8, (N, 8, RO, S))
    ci[..., 0] = sw; ci[..., CN - 1] = 1 - sw; ki[..., 0] = 1 - sw; ki[..., Q0 - 1] = sw
    ci[:, 7, 0] = 0; ci[:, 7, CN - 1] = 0; ki[:, 7, 0] = 0; ki[:, 7, Q0 - 1] = 0
    xi[..., 0] = rng.integers(0, 2, (N, 8, RO)); xi[..., S - 1] = rng.integers(0, 2, (N, 8, RO)); xi[:, 7, 0, 0] = 1; xi[:, 7, 0, S - 1] = 1
    p["kq"] = pick4(pr, ki); p["cc"] = pick4(pr, ci); p["xs"] = pick4(pr, xi.reshape(N, 8, RO * S))
    for k, top in (("nb", Q0 - 1), ("dl", CN - 1)):
        v = rng.integers(0, top + 1, (N, 8, 16, Q0)); v[:, :, :6] = 0; v[:, :, 6:11] = top
        v[:, :, :11] = np.where(rng.random((N, 8, 1, Q0)) < 0.5, top - v[:, :, :11], v[:, :, :11])
        v = rng.permuted(v, axis=2)
        for a in range(N):
            for c in (0, Q0 - 1): v[a, 7, :, c] = rng.permutation(np.repeat(np.array([0, top]), 8))
        p[k] = v
    st = np.where(rng.random((N, 8, LN)) < 0.72, (Q0 - 1) * rng.integers(0, 2, (N, 8, LN)), rng.integers(0, Q0, (N, 8, LN)))
    st[..., 0] = 0; st[..., S - 1] = Q0 - 1; st[..., LN - 1] = Q0 - 1; st[:, 7, 0] = Q0 - 1; p["st"] = st
    aa = pos(rng, 64, 128, N, 8, 16, CN).astype(np.float32)
    aa[:, 7, :, CN - 1] = 0.5 * aa[:, 7, :, 0]; p["aa"] = aa
    return pack(p)
def setup_inputs_spread(rng):
    p = parts(rng)
    for k, lo, hi in (("aa", 32, 64), ("ys", 128, 1024)):
        s = (N, 8, 1) + p[k].shape[3:]
        p[k] = pos(rng, lo, hi, *p[k].shape).astype(np.float32) * np.exp2(rng.integers(-1, 2, s))
    far(rng, p, int(rng.integers(0, 8)))
    return pack(p)
def setup_inputs_ties(rng):
    p = parts(rng)
    st = np.argsort(rng.random((N, 4, Q0)), axis=-1)[..., :LN]; p["st"][:, ::2] = st; p["nb"][:, ::2] = np.arange(Q0); p["cc"][:, ::2] = 7
    for t in range(RO):
        h = 8 * ((t // 2) % 2); x = np.full((N, 4, 16, S), 7)
        x[:, :, h:h + 8] += (1 - 2 * (t % 2)) * split(rng, EPS + rng.integers(0, 2, (N, 4, S)), 8, 7)
        p["xs"][:, ::2, :, t] = x
        if t == 0:
            z = split(rng, RHO + rng.integers(0, 2, (N, 4, S)), 16, 8); K = np.where(x > 7, x - z, x + z)
            for a in range(N):
                for g in range(4): p["kq"][a, 2 * g][:, st[a, g, :S]] = K[a, g]
    p["dl"][:, 2, 8:] = p["dl"][:, 2, :8]; p["dl"][:, 6, 8:] = p["dl"][:, 6, :8]
    pr = rng.integers(0, 16, (N, 4, 16, 6)); p["kq"][:, 1::2] = pick4(pr, rng.integers(0, 6, (N, 4, Q0)))
    p["cc"][:, 1::2] = np.where(rng.random((N, 4, 1, CN)) < 0.6, pick4(pr, rng.integers(0, 6, (N, 4, CN))), p["cc"][:, 1::2])
    for t in range(RO):
        m = rng.choice(np.array([0, 0, 1, 4, 9]), (N, 4, 1, S))
        p["xs"][:, 1::2, :, t] = clip(pick4(pr, rng.integers(0, 6, (N, 4, S))) + noise(rng, m, (N, 4, 16, S)))
    return pack(p)
def check_ranges(d):
    bad = []
    for k, hi in (("kq", 15), ("cc", 15), ("xs", 15), ("nb", Q0 - 1), ("dl", CN - 1), ("st", Q0 - 1)):
        v = np.asarray(d[k]).astype(np.float64)
        if not (np.min(v) >= 0 and np.max(v) <= hi): bad.append("range of " + k)
        elif np.any(v != np.floor(v)): bad.append("whole numbers of " + k)
    for k, lo, hi in (("aa", 16, 128), ("ys", 64, 2048)):
        v = np.asarray(d[k]).astype(np.float64)
        if not np.all((v >= lo) & (v <= hi)): bad.append("range of " + k)
    return bad
def pick(w, ix):
    return np.take_along_axis(w, ix[:, None, :], 2)
def entry(v, k):
    return np.take_along_axis(v, k[:, None, :], 1)[:, 0]
def dist(w, ix, x):
    v = pick(w, ix.reshape(8, -1)).reshape(8, 16, 16, -1)
    return np.add.reduce(np.abs(v - x[:, :, None, :]), axis=1)
def reference(kq, nb, dl, cc, aa, xs, ys, st):
    QT, CT = Q0 + LN * (RO - 1), CN + LN * (RO - 1)
    kk = np.zeros((N, 8, 16, QT), np.int32); nn = np.zeros((N, 8, 16, QT), np.int64); ll = np.zeros((N, 8, 16, QT), np.int64)
    ce = np.zeros((N, 8, 16, CT), np.int32); ac = np.zeros((N, 8, 16, CT), np.float64)
    kk[..., :Q0] = kq.astype(np.float32).astype(np.int32).reshape(N, 8, 16, Q0); nn[..., :Q0] = nb.reshape(N, 8, 16, Q0); ll[..., :Q0] = dl.reshape(N, 8, 16, Q0)
    ce[..., :CN] = cc.astype(np.float32).astype(np.int32).reshape(N, 8, 16, CN); ac[..., :CN] = aa.astype(np.float64).reshape(N, 8, 16, CN)
    x0 = xs.astype(np.float32).astype(np.int32).reshape(N, 8, 16, RO, S); y0 = ys.astype(np.float64).reshape(N, 8, 16, RO, S)
    cl = np.stack([gentries(a) for a in st]).astype(np.int64)
    gx = np.zeros((N, 8, 16, H), np.int32); ga = np.zeros((N, 8, 16, H), np.float64); gn = np.zeros((N, 8), np.int64)
    out = np.zeros((N, 8, 16, RO, S), np.float64); lane = np.arange(LN); rows = np.arange(16)[:, None]; before = np.tri(LN, LN, -1, dtype=bool)
    for t in range(RO):
        hx, ha, hn = np.zeros_like(gx), np.zeros_like(ga), np.zeros_like(gn)
        for a in range(N):
            x = np.concatenate([x0[a, :, :, t], gx[a]], axis=2); live = (lane < S) | (lane - S < gn[a][:, None])
            cand = pick(nn[a], cl[a]); d = dist(kk[a], cand, x)
            q = entry(cand, np.argmin(d, axis=1)); dq = np.min(d, axis=1)
            li = pick(ll[a], q); D = dist(ce[a], li, x)
            w = np.exp(-0.015625 * D[:, None, :, :S])
            P = np.add.reduce(w * pick(ac[a], li[:, :, :S].reshape(8, -1)).reshape(8, 16, 16, S), axis=2)
            out[a, :, :, t] = P
            if t == RO - 1: continue
            win = live & ~np.any((q[:, :, None] == q[:, None, :]) & live[:, None, :] & before, axis=2)
            ks, kl = np.argmin(D, axis=1), np.argmax(D, axis=1)
            upd = np.min(D, axis=1) <= EPS; fork = ~upd & (dq > RHO)
            cs = entry(li, ks); lo, ql = CN + LN * t, Q0 + LN * t
            cn = np.where(upd[:, None, :], pick(ce[a], cs), x)
            an = np.concatenate([np.where(upd[:, None, :S], pick(ac[a], cs[:, :S]), 0.0) + 0.25 * (y0[a, :, :, t] - P), ga[a]], axis=2)
            nl = np.where(rows == np.where(upd, ks, kl)[:, None, :], lo + lane, li)
            nq = np.where(rows == t, q[:, None, :], pick(nn[a], q))
            ce[a][:, :, lo:lo + LN] = cn; ac[a][:, :, lo:lo + LN] = an
            b = (a + 1 + t % (N - 1)) % N
            for g in range(8):
                i = np.nonzero(win[g] & ~fork[g])[0]; ll[a, g][:, q[g, i]] = nl[g][:, i]
                i = np.nonzero(win[g] & fork[g])[0]
                ll[a, g][:, ql + i] = nl[g][:, i]; nn[a, g][:, ql + i] = nq[g][:, i]; kk[a, g][:, ql + i] = x[g][:, i]; nn[a, g][8 + t, q[g, i]] = ql + i
                i = np.nonzero(win[g, :S] & ~upd[g, :S])[0][:H]
                hx[b, g][:, :i.size] = x[g][:, i]; ha[b, g][:, :i.size] = an[g][:, i]; hn[b, g] = i.size
            cl[a] = np.where(live, q, cl[a])
        gx, ga, gn = hx, ha, hn
    return {"yp": out.reshape(N, 128, RO * S).astype(np.float32)}

def check_inputs(d):
    bad = list(check_ranges(d))
    if not bad:
        for name, y in reference(**d).items():
            for q in range(N):
                v = np.abs(np.asarray(y[q], np.float64)); s = np.sqrt(np.mean(v * v))
                if v.max() > 5 * s or s < 2.0 ** 7: bad.append('%s of rank %d is uneven or too small' % (name, q))
    return bad

@@ -1,0 +1,733 @@
+import math
+from concourse.mybir import AluOpType as ALU, ActivationFunctionType as ACT
+
+CN, Q0, S, H, RO, EPS, RHO = 1280, 384, 192, 64, 4, 44, 60
+LN = S + H
+XS_SLOT = 16 + H + S
+C0 = 3 * XS_SLOT
+CT = CN + 3 * LN
+QT = Q0 + 3 * LN
+PAD = 16
+FD = 320
+LO = LN + 4 * FD
+B1 = (RHO + 1) * 65536
+B2 = EPS * 65536 + 32768
+LNR = 0.668
+F, BF, I32, U16 = "float32", "bfloat16", "int32", "uint16"
+
+_SB = {
+    "XS": (768, BF), "YS": (768, BF), "I4": (128, BF), "DR": (4096, BF), "SL2": (72, BF), "SLN": (72, BF), "NBI": (Q0, I32), "DLI": (Q0, I32),
+    "STI": (16, I32), "KK": (QT, BF), "CE": (C0 + CT, BF), "AC": (C0 + CT, F), "NL": (LO + QT, F),
+    "IOTA": (QT, F), "XREP": (768 * 16, BF), "GREP": (H * 16, BF), "D1": (4096, BF), "D20": (PAD + 4096, BF),
+    "D21": (PAD + 4096, BF), "AG": (3072, F), "RR0": (3072, F), "RR1": (3072, F), "SC": (3072, F), "O1": (LN, U16),
+    "O20": (LN, U16), "O21": (LN, U16), "CANDF": (LN, F), "SD": (FD + LN, F), "DAT": (LN, F),
+    "LIF": (LN, F), "RQF": (LN, F), "RQ16": (LN, U16), "E": (16 * LN, BF),
+    "WM": (LN, BF), "WS": (LN, BF), "MN": (256, F), "MX": (256, F), "XP": (256, F), "OHT": (256, F),
+    "P4": (S, F), "GG": (S, F), "YO": (768, F), "IB": (128, BF), "NIB": (128, BF), "LANE4": (16, F), "LANEO": (16, F),
+    "GI": (8 + LN + S, F), "GD": (H, F), "GS": (H, F), "GL0": (4, U16), "GL1": (4, U16),
+    "OBD": (128, BF), "NBD": (128, BF), "TRI": (128, BF), "TRB": (128, BF), "IDF": (128, F), "SL": (72, BF),
+    "DM": (128, F), "BSEL": (8, F), "KC1": (128, BF), "KC2": (128, BF), "ONE2": (128, BF), "RB": (32, BF),
+    "KPAT": (128, F), "GPAT": (128, F), "RMIN": (128, F), "RMAX": (128, F), "RSUM": (256, BF), "MD": (768, F),
+    "WL": (16, F), "THR": (256, F), "PI": (8, I32), "CF": (8, F), "IU": (64, U16), "BL": (8, U16),
+    "LANEL": (16, F), "LANEX": (16, F), "LG": (16, F), "MCOL": (8, F), "ONES": (16, BF),
+    "ST16": (16, U16), "QL0": (16, U16), "QL1": (16, U16), "QL2": (16, U16), "QL3": (16, U16), "CLF": (8, F),
+    "K1I": (16, I32), "QI": (16, I32), "QF": (16, F), "TI": (16, I32), "T2": (16, I32), "SEL": (16, I32), "RI": (16, I32),
+    "LVF": (16, F), "WINF": (16, F), "FK": (16, F), "WF": (16, F), "QD": (16, F), "QB": (16, F), "QA": (16, F),
+    "NV": (16, F), "MM": (16, F), "TB1": (16, F), "TB16": (16, U16), "TA1": (16, F),
+    "TA16": (16, U16), "SI": (16, I32), "CI": (16, I32), "U2": (16, F), "U3": (16, F), "U4": (16, F),
+    "CN16": (16, U16), "NW": (16, BF), "CUM": (16, BF), "GP": (16, F), "GP0": (16, U16),
+    "PU1": (8, F), "PU2": (8, F), "PU3": (8, F),
+    "SX0": (8 + H, U16), "SX1": (8 + H, U16), "LU0": (8 + H, U16), "LU1": (8 + H, U16), "XR0": (S, BF), "XR1": (S, BF), "SA0": (H, F), "SA1": (H, F),
+}
+_PS = ["K0", "K1", "R0", "R1", "CM", "TR", "OH", "F0"]
+CFG = {"direct": {(0, 1, 0), (1, 1, 0), (2, 1, 0), (3, 1, 0)}, "off": set(), "agv": set(), "iters": 4,
+       "gc": 1.5, "sc": 3.8, "pe": 0.6, "sem": 60.0, "look": 120.0, "gpe": False, "relu": set(), "merge": False, "lean": True, "ggrep": set(), "nldma": False, "f2": False, "seed": 0, "noise": 0.0, "f": 1.0}
+SCRATCH = {}
+POOL = {}
+for _n in _SB:
+    _w, _d = _SB[_n]
+    if _w <= 16 and _n != "STI":
+        POOL[_n] = ("SM" + _d, 16 * len([1 for _v in POOL.values() if _v[0] == "SM" + _d]))
+        SCRATCH["SM" + _d] = ("sbuf", [128, POOL[_n][1] + 16], _d)
+    else:
+        SCRATCH[_n] = ("sbuf", [128, _w], _d)
+for _n in _PS:
+    SCRATCH[_n] = ("psum", [128, 512], F)
+NDMA = 36
+SEMAPHORES = (["sv", "ss", "st_", "sg", "sent", "hsent"] + ["dm%d" % i for i in range(NDMA)]
+              + [a + b + c for a in "gh" for b in "exa" for c in "01"])
+
+CFG.update({'direct': [(0, 1, 0), (1, 1, 0), (1, 2, 0), (1, 2, 1), (3, 1, 0), (3, 2, 0), (3, 2, 1)], 'off': [(0, 1, 1, 0), (0, 1, 1, 1), (0, 1, 2, 0), (0, 2, 0, 1), (0, 2, 1, 1), (0, 2, 2, 1), (1, 1, 3, 1), (1, 2, 2, 1), (2, 1, 1, 0), (2, 1, 3, 0), (2, 2, 0, 0), (2, 2, 0, 1), (3, 1, 3, 1)], 'agv': [(3, 4), (3, 5)], 'iters': 8, 'gc': 1.6, 'sc': 3.8, 'pe': 0.75, 'sem': 80.0, 'look': 30, 'nldma': True, 'seed': 873, 'noise': 250, 'f': 1.2})
+CYC = 0.83
+
+
+def R(name, lo=0, hi=None, step=1, p0=0, p1=128, ps=1):
+    if hi is None:
+        hi = _SB[name][0] if name in _SB else 512
+    return (name, lo, hi, step, p0, p1, ps)
+
+
+def width(r):
+    return len(range(r[1], r[2], r[3]))
+
+
+def two_byte(r):
+    return r[0] in _SB and _SB[r[0]][1] in (BF, U16)
+
+
+def overlap(a, b):
+    if a[0] in _PS:
+        return True
+    if a[2] <= b[1] or b[2] <= a[1]:
+        return False
+    if a[3] == b[3] and a[3] > 1 and (a[1] - b[1]) % a[3] != 0:
+        return False
+    return True
+
+
+def route(T, topo, rank, t):
+    n = len(T.cores)
+    src, dst = T.cores[rank], T.cores[(rank + 1 + t % (n - 1)) % n]
+    if topo.may_write(src, dst):
+        return dst, None
+    cand = [h for h in topo.cores_of(src) if T.rank_of(h) is None and topo.may_write(h, dst) and topo.may_write(src, h)]
+    cand.sort(key=lambda h: (topo.die(h) != topo.die(src), h))
+    return dst, cand[0]
+
+
+def few_engines(topo, src, far):
+    es = topo.engines(src, far)[::2][:4]
+    return sum(1 << e for e in es), len(es)
+
+
+def far_core(T, topo, src):
+    return [d for d in T.cores if topo.chip(d) != topo.chip(src) and topo.may_write(src, d)][0]
+
+
+def landing(kind, t):
+    if kind == "e":
+        return R("XR%d" % t)
+    if kind == "x":
+        return R("LU%d" % t)
+    a = C0 + CN + LN * (t + 1) + S
+    return R("AC", a, a + H)
+
+
+def relay_program(g, core, T, topo):
+    total = 0
+    for t in range(2):
+        for r in range(len(T.cores)):
+            dst, via = route(T, topo, r, t)
+            if via != core:
+                continue
+            src = T.cores[r]
+            _, n_in = few_engines(topo, src, far_core(T, topo, src))
+            mask, n = few_engines(topo, core, dst)
+            rid, pid = topo.addr(dst, core)
+            for kind in "exa":
+                r_ = landing(kind, t)
+                ap = T[r_[0]][:, r_[1]:r_[2]]
+                g.wait_ge(T.sem["h%s%d" % (kind, t)], n_in)
+                g.remote_dma(ap, ap, T.sem["g%s%d" % (kind, t)], T.sem.hsent, pid, rid, mask)
+                total += n
+    if total:
+        g.wait_ge(T.sem.hsent, total)
+
+
+def build(g, core, T, topo, rank):
+    ops = []
+    PEC, GC, SCC = CFG["pe"], CFG["gc"], CFG["sc"]
+    V, SE, PE, SY = g.vector, g.scalar, g.tensor, g.sync
+
+    def A(r):
+        name, b = POOL.get(r[0], (r[0], 0))
+        return T[name][slice(r[4], r[5], r[6]) if r[6] > 1 else slice(r[4], r[5]),
+                       slice(b + r[1], b + r[2], r[3]) if r[3] > 1 else slice(b + r[1], b + r[2])]
+
+    def IND(w, o):
+        return A(w).indirect(A(o))
+
+    def op(eng, fn, rd, wr, cost, lat=0.0, kind="c", extra=None):
+        ops.append({"eng": eng, "fn": fn, "rd": rd, "wr": wr, "cost": cost, "lat": lat, "kind": kind, "x": extra})
+
+    def vcost(n, c):
+        return max(64, n * c) * CYC * CFG["f"]
+
+    def sc(x):
+        return A(x) if isinstance(x, tuple) else x
+
+    def refs(*xs):
+        return [x for x in xs if isinstance(x, tuple)]
+
+    def vcopy(o, i):
+        op("v", lambda: V.tensor_copy(A(o), A(i)), [i], [o], vcost(width(o), 0.5 if two_byte(o) and two_byte(i) else 1))
+
+    def vts(o, i, s1, s2, o0, o1=None):
+        if o1 is None:
+            fn = lambda: V.tensor_scalar(A(o), A(i), sc(s1), None, o0)
+        else:
+            fn = lambda: V.tensor_scalar(A(o), A(i), sc(s1), sc(s2), o0, o1)
+        op("v", fn, [i] + refs(s1, s2), [o], vcost(width(o), 0.5 if two_byte(o) and two_byte(i) else 1))
+
+    def vtt(o, a, b, alu):
+        op("v", lambda: V.tensor_tensor(A(o), A(a), A(b), alu), [a, b], [o],
+           vcost(width(o), 1 if a[0] in _PS or b[0] in _PS else 2))
+
+    def vset(o, c):
+        op("v", lambda: V.memset(A(o), c), [], [o], vcost(width(o), 0.5 if two_byte(o) else 1))
+
+    def vscan(o, d0, d1, o0, o1):
+        op("v", lambda: V.tensor_tensor_scan(A(o), A(d0), A(d1), 0.0, o0, o1), [d0, d1], [o],
+           vcost(width(o), 0.5 if two_byte(o) and two_byte(d0) and two_byte(d1) else 1))
+
+    def vgather(o, w, l):
+        op("v", lambda: V.tensor_copy(A(o), IND(w, l)), [w, l], [o], 50 + width(o) * GC * CYC)
+
+    def vgtt(o, w, l, b, alu):
+        op("v", lambda: V.tensor_tensor(A(o), IND(w, l), A(b), alu), [w, l, b], [o], 50 + width(o) * GC * CYC)
+
+    def vscat(w, l, i):
+        op("v", lambda: V.tensor_copy(IND(w, l), A(i)), [l, i], [w], 50 + width(i) * SCC * CYC)
+
+    def vscat_tt(w, l, a, b, alu):
+        op("v", lambda: V.tensor_tensor(IND(w, l), A(a), A(b), alu), [l, a, b], [w], 50 + width(a) * SCC * CYC)
+
+    def act(o, i, func, bias=0.0, scale=1.0):
+        op("s", lambda: SE.activation(A(o), A(i), func, bias=sc(bias), scale=sc(scale)), [i] + refs(bias, scale), [o],
+           vcost(width(o), 1))
+
+    def sgather(o, w, l):
+        op("s", lambda: SE.activation(A(o), IND(w, l), ACT.Copy), [w, l], [o], 65 + width(o) * GC * CYC)
+
+    def mms(lst):
+        def fn():
+            ins = None
+            for o, l, r, st, sp in lst:
+                ins = PE.matmul(A(o), A(l), A(r), st, sp)
+            return ins
+        c = sum(max(min(64, width(l)), width(r)) * (1 if two_byte(l) else 4) for o, l, r, st, sp in lst) * PEC
+        rd = []
+        for o, l, r, st, sp in lst:
+            rd += [l, r]
+        op("t", fn, rd, [lst[0][0]], c, 40)
+
+    def giota(o, pat, base, cm):
+        if _SB[o[0]][1] == I32:
+            fn = lambda: g.iota(A(o), pat, base, cm)
+        else:
+            fn = lambda: g.iota(A(o), pat, base, cm, allow_small_or_imprecise_dtypes=True)
+        op("g", fn, [], [o], 130 + 2 * width(o) * CYC)
+
+    def gsel(o, i, pat, cmp_, base, cm):
+        op("g", lambda: g.affine_select(A(o), A(i), pat, cmp_, 0.0, base, cm), [i], [o], 170 + 2 * width(o) * CYC)
+
+    ndma = [0]
+
+    def dma(q, out, in_, rd, wr, lat=2000.0):
+        k = ndma[0]
+        ndma[0] += 1
+        eng = {"y": SY, "s": SE, "g": g}[q]
+        op(q, lambda: eng.dma_start(out(), in_()), rd, wr, 1000 if q == "g" else 60, lat, "dma", "dm%d" % k)
+
+    def load(q, o, src, lo, hi, lat=2000.0):
+        dma(q, lambda: A(o), lambda: T[src][:, lo:hi], [], [o], lat)
+
+    def copy_dma(o, i):
+        dma("y", lambda: A(o), lambda: A(i), [i], [o])
+
+    mask, neng = few_engines(topo, core, far_core(T, topo, core))
+    n = len(T.cores)
+
+    def send(t, kind, src):
+        dst, via = route(T, topo, rank, t)
+        to = dst if via is None else via
+        rid, pid = topo.addr(to, core)
+        sem = T.sem[("g%s%d" if via is None else "h%s%d") % (kind, t)]
+        land = landing(kind, t)
+        op("g", lambda: g.remote_dma(A(land), A(src), sem, T.sem.sent, pid, rid, mask), [src], [],
+           1500 if kind == "e" else 500, 0, "send")
+        me = len(ops) - 1
+        frm = (rank - 1 - t % (n - 1)) % n
+        _, v2 = route(T, topo, frm, t)
+        if v2 is None:
+            cnt = few_engines(topo, T.cores[frm], far_core(T, topo, T.cores[frm]))[1]
+        else:
+            cnt = few_engines(topo, v2, core)[1]
+        op(None, None, [], [land], 0, 3000.0 if via is None else 6000.0, "arr", ("g%s%d" % (kind, t), cnt, me))
+
+    load("y", R("STI"), "st", 0, 16)
+    load("s", R("NBI"), "nb", 0, Q0)
+    load("y", R("XS"), "xs", 0, 768)
+    load("s", R("KK", 0, Q0), "kq", 0, Q0)
+    load("y", R("DLI"), "dl", 0, Q0)
+    load("y", R("CE", C0, C0 + CN), "cc", 0, CN, 2500)
+    load("g", R("AC", C0, C0 + CN), "aa", 0, CN, 4000)
+    load("y", R("YS"), "ys", 0, 768)
+    for t in range(2):
+        send(t, "e", R("XS", S * t, S * t + S))
+    for t in range(3):
+        a = (2 - t) * XS_SLOT + 16 + H
+        load("y", R("CE", a, a + S), "xs", S * t, S * t + S)
+        load("y", R("KK", Q0 + LN * t, Q0 + LN * t + S), "xs", S * t, S * t + S)
+
+    giota(R("PI", 0, 1), [[0, 1]], 0, 1)
+    giota(R("IOTA", 0, 256), [[1, 256]], 0, 0)
+    giota(R("KPAT"), [[0, 8], [1, 16]], 0, 0)
+    giota(R("GPAT"), [[1, 8], [0, 16]], 0, 0)
+    giota(R("IOTA", 256, QT), [[1, QT - 256]], 256, 0)
+    giota(R("MD", 0, 256), [[96, 2], [1, 128]], CN, 0)
+    giota(R("MD", 256, 768), [[1, 512]], CN + LN, 0)
+    for j in range(6):
+        gsel(R("MD", 128 * j, 128 * j + 128), R("MD", 128 * j, 128 * j + 128), [[-1, 128]], ALU.is_equal, 0, 1)
+    vts(R("PI", 1, 2), R("PI", 0, 1), 15, None, ALU.bitwise_and)
+    vts(R("PI", 2, 3), R("PI", 0, 1), 4, None, ALU.arith_shift_right)
+    vcopy(R("CF", 0, 3), R("PI", 0, 3))
+    p_, pm, pg = R("CF", 0, 1), R("CF", 1, 2), R("CF", 2, 3)
+    vts(R("CF", 3, 4), pg, 8.0, 7.0, ALU.mult, ALU.add)
+    vts(R("CF", 4, 5), p_, 0.0, 2048.0, ALU.is_equal, ALU.mult)
+    vts(R("CF", 5, 6), p_, 1.0, -float(B1), ALU.is_equal, ALU.mult)
+    vts(R("CF", 6, 7), p_, 1.0, -float(B2), ALU.is_equal, ALU.mult)
+    vts(R("KC1"), R("KPAT"), R("CF", 4, 5), R("CF", 5, 6), ALU.mult, ALU.add)
+    vts(R("KC2"), R("KPAT"), R("CF", 4, 5), R("CF", 6, 7), ALU.mult, ALU.add)
+    vts(R("DM"), R("KPAT"), pm, None, ALU.is_equal)
+    vts(R("OBD"), R("GPAT"), pg, None, ALU.is_equal)
+    act(R("NBD"), R("OBD"), ACT.Copy, scale=-1.0)
+    vts(R("BSEL"), R("IOTA", 0, 8), pg, None, ALU.is_equal)
+    vts(R("IDF"), R("IOTA", 0, 128), p_, None, ALU.is_equal)
+    vts(R("SL"), R("IOTA", 0, 72), R("CF", 3, 4), 65536.0, ALU.is_equal, ALU.mult)
+    gsel(R("TRI"), R("OBD"), [[1, 128]], ALU.is_gt, 0, -1)
+    act(R("TRB"), R("IDF"), ACT.Copy, scale=-1024.0)
+    act(R("IB"), R("IDF"), ACT.Copy)
+    act(R("NIB"), R("IDF"), ACT.Copy, scale=-1.0)
+    vts(R("RMIN"), R("KPAT"), 0.0, 2.0 ** 25, ALU.is_equal, ALU.mult)
+    act(R("RMAX"), R("RMIN"), ACT.Identity, bias=R("CF", 7, 8), scale=-1.0)
+    for j in range(2):
+        act(R("RSUM", 128 * j, 128 * j + 128), R("RMIN"), ACT.Identity, bias=R("MCOL", 7, 8), scale=-2.0 ** -25)
+    act(R("MN"), R("IOTA", 0, 256), ACT.Copy, scale=0.0)
+    vcopy(R("IU"), R("IOTA", 0, 64))
+    vts(R("BL"), R("IOTA", 0, 8), 16.0, 15.0, ALU.mult, ALU.add)
+    vts(R("LANEL"), R("IOTA", 0, 16), 16.0, pm, ALU.mult, ALU.add)
+    vts(R("LANEX", 0, 12), R("LANEL", 0, 12), float(16 + H), None, ALU.add)
+    vts(R("LANEX", 12, 16), R("LANEL", 12, 16), float(16 - S), None, ALU.add)
+    vts(R("LG"), R("LANEL"), float(LN - 1024), None, ALU.add)
+    vts(R("LANEO"), R("LANEL"), -float(LO), None, ALU.add)
+    vset(R("MCOL", 4, 5), 84.0)
+    vset(R("MCOL", 5, 6), 84.0 + math.log(2.5))
+    vset(R("MCOL", 6, 7), math.log(0.25))
+    act(R("WL"), R("LANEL"), ACT.Exp, bias=R("MCOL", 4, 5), scale=-LNR)
+    act(R("F0", 0, 256), R("IOTA", 0, 256), ACT.Exp, bias=R("MCOL", 5, 6), scale=-LNR)
+    for j in range(2):
+        vtt(R("THR", 128 * j, 128 * j + 128), R("F0", 128 * j, 128 * j + 128), R("DM"), ALU.mult)
+    act(R("LANE4"), R("LANEL"), ACT.Copy, scale=4.0)
+    return_fill = [(R("ONE2"), 1.0), (R("RB"), -8192.0), (R("ONES"), 1.0), (R("LVF"), 1.0), (R("D20", 0, PAD), 0.0), (R("D21", 0, PAD), 0.0),
+                   (R("NW"), 0.0), (R("CUM"), 0.0), (R("AC", 2 * XS_SLOT, C0), 0.0), (R("MCOL", 7, 8), 1.0),
+                   (R("NL", LO + Q0 + S, LO + Q0 + LN), 0.0), (R("SD", S, FD), 0.0), (R("GI", 0, 8 + H), 0.0),
+                   (R("NL", LN + Q0 + S, LN + Q0 + LN), 0.0), (R("KK", Q0 + S, Q0 + LN), 0.0),
+                   (R("CE", 2 * XS_SLOT, 2 * XS_SLOT + 16 + H), 0.0), (R("CE", C0 + CN + S, C0 + CN + LN), 0.0),
+                   (R("AC", C0 + CN + S, C0 + CN + LN), 0.0), (R("CE", 0, 16), 0.0), (R("CE", XS_SLOT, XS_SLOT + 16), 0.0)]
+    pre = len(ops)
+    vset(R("CF", 7, 8), 4096.0)
+    for r, c in return_fill:
+        vset(r, c)
+    vset(R("SEL"), 0)
+    vset(R("RI"), 0)
+    fills = ops[pre:]
+    del ops[pre:]
+    ops[0:0] = fills
+    for j in range(2):
+        copy_dma(R("AC", j * XS_SLOT, (j + 1) * XS_SLOT), R("AC", 2 * XS_SLOT, C0))
+    vcopy(R("ST16"), R("STI"))
+    vcopy(R("NL", LN, LN + Q0), R("NBI"))
+    vcopy(R("NL", LO, LO + Q0), R("DLI"))
+    vcopy(R("QL0", 12, 16), R("STI", 12, 16))
+    vcopy(R("CLF", 0, 4), R("STI", 12, 16))
+    act(R("I4"), R("IDF"), ACT.Copy, scale=0.25)
+    if CFG["relu"]:
+        act(R("SL2"), R("SL"), ACT.Copy, scale=2.0)
+        act(R("SLN"), R("SL"), ACT.Copy, scale=-1.0)
+
+    def xrep(t):
+        for k in range(16):
+            o, i = R("XREP", S * 16 * t + k, S * 16 * (t + 1), 16), R("XS", S * t, S * t + S)
+            if t > 0:
+                gsel(o, i, [[0, S]], ALU.is_ge, 0, 0)
+            elif k < 11:
+                vcopy(o, i)
+            else:
+                act(o, i, ACT.Copy)
+
+    for t in range(RO):
+        xrep(t)
+
+    nf = [0]
+
+    def oh(a, b, p1=128):
+        return R("CM", 256 + a, 256 + b) if CFG["f2"] else R("OH", a, b)
+
+    def xr(t, l0, cnt):
+        if l0 >= S:
+            return R("GREP", (l0 - S) * 16, (l0 - S + cnt) * 16)
+        return R("XREP", (S * t + l0) * 16, (S * t + l0 + cnt) * 16)
+
+    def lists(t, ph, c, o16, of, win, lst, want_f):
+        if (t, ph, c) in CFG["direct"]:
+            vgather(o16, R("NBI") if (t, ph) == (0, 1) else win, lst)
+            if want_f:
+                sgather(of, win, lst)
+        else:
+            sgather(of, win, lst)
+            vcopy(o16, of)
+
+    def diffs(t, ph, s, dname, pad, win, oname, s0, cnt):
+        h = cnt // 2
+        off = [u for u in range(2) if ((t, ph, s, u) in CFG["off"] and (t, ph, s // 2) not in CFG["relu"])
+               or (s0 >= S and CFG["gpe"])]
+        if not off:
+            parts = [(s0, cnt, False)]
+        else:
+            parts = [(s0 + u * h, h, u in off) for u in range(2)]
+        for a, m, by_s in parts:
+            d = R(dname, pad + a * 16, pad + (a + m) * 16)
+            if by_s:
+                nf[0] += 1
+                fb = "OH" if CFG["f2"] and nf[0] % 2 else "F0"
+                f = R(fb, 0, m * 16)
+                sgather(d, win, R(oname, a, a + m))
+                if a >= S and CFG["gpe"]:
+                    x0 = (2 - t) * XS_SLOT + 16 + a - S
+                    mms([(f, R("IB"), d, True, False)]
+                        + [(R(fb, k, m * 16, 16), R("NIB"), R("CE", x0, x0 + m), False, k == 15) for k in range(16)])
+                else:
+                    mms([(f, R("IB"), d, True, False), (f, R("NIB"), xr(t, a, m), False, True)])
+                act(d, f, ACT.Abs)
+            else:
+                vgtt(d, win, R(oname, a, a + m), xr(t, a, m), ALU.subtract)
+                if (t, ph, s // 2) in CFG["relu"]:
+                    vts(R("DR", a * 16, (a + m) * 16), d, 0.0, None, ALU.max)
+                else:
+                    act(d, d, ACT.Abs)
+
+    def keys(bank, CH, l0, idf, kc, dname, pad, relu=False):
+        full = R(bank, 0, 128, 1, 0, CH)
+        row = (full, R("ONE2", 0, CH, 1, 0, 2), R(kc, 0, 128, 1, 0, 2), False, relu)
+        mms([(full, R(idf, l0, l0 + CH), R("IDF"), True, False)] + ([] if relu else [row]))
+        for nm, sl, end in ([(dname, "SLN", False), ("DR", "SL2", True)] if relu else [(dname, "SL", True)]):
+            lst = []
+            for k in range(16):
+                a = pad + l0 * 16 + k
+                lst.append((R(bank, k % 2, 128, 2, 0, CH), R(nm, a, pad + (l0 + CH) * 16, 16),
+                            R(sl, 7 - k // 2, 71 - k // 2), False, end and k == 15 and not relu))
+            mms(lst + ([row] if relu and end else []))
+
+    for t in range(RO):
+        last = t == RO - 1
+        L = LN if t in (1, 2) else S
+        CH, NB = L // 2, L // 16
+        hb, SUB = NB // 2, L // 4
+        ql, lo = Q0 + LN * t, CN + LN * t
+        CL = ["ST16", "QL0", "QL1", "QL2"][t]
+        QL = "QL%d" % t
+        slot = (2 - t) * XS_SLOT
+
+        O2, D2 = "O2%d" % (t % 2), "D2%d" % (t % 2)
+        if L == LN:
+            lu = "LU%d" % (t - 1)
+            sgather(R("GREP"), R("XR%d" % (t - 1)), R(lu, 8, 8 + H))
+            gsel(R("CE", slot + 16, slot + 16 + H), R("GREP", 0, H * 16, 16), [[0, H]], ALU.is_ge, 0, 0)
+            gsel(R("KK", ql + S, ql + LN), R("GREP", 0, H * 16, 16), [[0, H]], ALU.is_ge, 0, 0)
+            vcopy(R("CLF", 4, 5), R(lu, 0, 1))
+            vts(R("LVF", 12, 16), R("LANEL", 0, 4), R("CLF", 4, 5), None, ALU.is_lt)
+        nnw, llw = R("NL", LN, LN + ql), R("NL", LO, LO + ql)
+        for c in range(2):
+            l0, b0 = c * CH, c * hb
+            bank = "K%d" % c
+            lists(t, 1, c, R("O1", l0, l0 + CH), R("CANDF", l0, l0 + CH), nnw, R(CL, b0, b0 + hb), True)
+            for s in range(2):
+                diffs(t, 1, 2 * c + s, "D1", 0, R("KK", 0, ql), "O1", l0 + s * SUB, SUB)
+            keys(bank, CH, l0, "CANDF", "KC1", "D1", 0, (t, 1, c) in CFG["relu"])
+            vscan(R("MN", 128 * c, 128 * c + 128, 1, 0, CH), R("RMIN", 0, 128, 1, 0, CH), R(bank, 0, 128, 1, 0, CH),
+                  ALU.add, ALU.min)
+            vgtt(R("XP", 128 * c, 128 * c + 128), R("MN", 128 * c, 128 * c + 128), R("BL"), R("DM"), ALU.mult)
+            mms([(R("TR", b0, b0 + hb), R("XP", 128 * c, 128 * c + 128, 1, 0, CH), R("BSEL", 0, hb, 1, 0, CH), True, True)])
+            vcopy(R("K1I", b0, b0 + hb), R("TR", b0, b0 + hb))
+            vts(R("QI", b0, b0 + hb), R("K1I", b0, b0 + hb), 2047, None, ALU.bitwise_and)
+            vcopy(R(QL, b0, b0 + hb), R("QI", b0, b0 + hb))
+        for c in range(2):
+            l0, b0 = c * CH, c * hb
+            bank = "K%d" % c
+            lists(t, 2, c, R(O2, l0, l0 + CH), R("LIF", l0, l0 + CH), llw, R(QL, b0, b0 + hb), not last)
+            for s in range(2):
+                diffs(t, 2, 2 * c + s, D2, PAD, R("CE", C0, C0 + lo), O2, l0 + s * SUB, SUB)
+            if last:
+                continue
+            keys(bank, CH, l0, "LIF", "KC2", D2, PAD)
+            kb = R(bank, 0, 128, 1, 0, CH)
+            vscan(R("MN", 128 * c, 128 * c + 128, 1, 0, CH), R("RMIN", 0, 128, 1, 0, CH), kb, ALU.add, ALU.min)
+            vscan(R("MX", 128 * c, 128 * c + 128, 1, 0, CH), R("RMAX", 0, 128, 1, 0, CH), kb, ALU.add, ALU.max)
+            if CFG["merge"] and c == 0:
+                continue
+            c0, c1 = (0 if CFG["merge"] else c), c + 1
+            e8 = lambda nm: R(nm, 8 * c0, 8 * c1, 1, 0, CH)
+            vts(e8("TI"), R("MX", 128 * c0 + 15, 128 * c1, 16, 0, CH), -1.0, float(30 * 2048 + 2047), ALU.mult, ALU.add)
+            vts(e8("T2"), e8("TI"), 32767, None, ALU.bitwise_and)
+            vtt(e8("SEL"), R("MN", 128 * c0 + 15, 128 * c1, 16, 0, CH), e8("T2"), ALU.min)
+            vts(e8("RI"), e8("SEL"), 11, 15, ALU.arith_shift_right, ALU.bitwise_and)
+            for u in range(c0, c1):
+                vgtt(R("XP", 128 * u, 128 * u + 128), R("SEL", 8 * u, 8 * u + 8), R("IU", 0, 8), R("DM"), ALU.mult)
+                mms([(R("TR", 16 + u * hb, 16 + u * hb + hb), R("XP", 128 * u, 128 * u + 128, 1, 0, CH),
+                      R("BSEL", 0, hb, 1, 0, CH), True, True)])
+                vgtt(R("OHT", 128 * u, 128 * u + 128), R("RI", 8 * u, 8 * u + 8), R("IU", 0, 8), R("KPAT"), ALU.is_equal)
+                m0 = 128 * (2 * t + u)
+                mms([(oh(u * CH, u * CH + CH), R("OHT", 128 * u, 128 * u + 128, 1, 0, CH),
+                      R("MD", m0, m0 + CH, 1, 0, CH), True, True)])
+        nb_ = lambda nm: R(nm, 0, NB)
+        if not last:
+            vcopy(nb_("QF"), nb_("QI"))
+            sgather(R("RQF", 0, L), R("IOTA", 0, ql), nb_(QL))
+            sgather(R("SD", FD, FD + L), nnw, nb_(QL))
+            vcopy(R("RQ16", 0, L), R("RQF", 0, L))
+            for b in range(NB):
+                e = R("E", LN * b + 16 * b, LN * b + L)
+                vts(e, R("RQ16", 16 * b, L), R("QF", b, b + 1), R("WL", b, b + 1), ALU.is_equal, ALU.mult)
+            for b0 in range(0, NB, 4):
+                mms([(R("CM", 16 * b, L), R("OBD"), R("E", LN * b + 16 * b, LN * b + L), b == 0, b == NB - 1)
+                     for b in range(b0, b0 + 4)])
+            vtt(R("WM", 0, L), R("CM", 0, L), R("THR", 0, L), ALU.is_lt)
+            vscan(R("WS", 0, L), R("RSUM", 0, L), R("WM", 0, L), ALU.mult, ALU.add)
+            vtt(nb_("WINF"), R("WS", 15, L, 16), nb_("LVF"), ALU.mult)
+            vts(nb_("FK"), nb_("K1I"), 0.0, -float(LO - LN), ALU.is_ge, ALU.mult)
+            vtt(nb_("WF"), nb_("FK"), nb_("WINF"), ALU.mult)
+            vtt(nb_("QD"), nb_("QF"), nb_("LANEO"), ALU.subtract)
+            vtt(nb_("QB"), nb_("QD"), nb_("WINF"), ALU.mult)
+            vtt(nb_("QA"), nb_("QB"), nb_("LANEL"), ALU.add)
+            if CFG["nldma"]:
+                copy_dma(R("NL", LN + ql, LN + ql + L), R("SD", FD, FD + L))
+            else:
+                act(R("NL", LN + ql, LN + ql + L), R("SD", FD, FD + L), ACT.Copy)
+            copy_dma(R("NL", LN + ql, LN + ql + L, 1, t, 128, 16), R("RQF", 0, L, 1, t, 128, 16))
+            copy_dma(R("SD", FD, FD + L, 1, 8 + t, 128, 16), R("IOTA", ql, ql + L, 1, 8 + t, 128, 16))
+            if t == 1:
+                vtt(R("PU1", 0, 4), R("QF", 12, 16), R("CLF", 0, 4), ALU.subtract)
+                vtt(R("PU2", 0, 4), R("PU1", 0, 4), R("LVF", 12, 16), ALU.mult)
+                vtt(R("PU3", 0, 4), R("PU2", 0, 4), R("CLF", 0, 4), ALU.add)
+                vcopy(R(QL, 12, 16), R("PU3", 0, 4))
+            sel = R("TR", 16, 16 + NB)
+            vts(nb_("NV"), sel, 0.0, None, ALU.is_ge)
+            vcopy(nb_("SI"), sel)
+            vtt(nb_("MM"), nb_("NV"), nb_("WF"), ALU.mult)
+            vtt(nb_("TB1"), nb_("LANE4"), nb_("MM"), ALU.subtract)
+            vts(nb_("TB16"), nb_("TB1"), 0.25, None, ALU.mult)
+            vtt(R("SD", 0, L), oh(0, L), R("LIF", 0, L), ALU.max)
+            sgather(R("DAT", 0, L), R("SD", 0, FD + L), nb_("TB16"))
+            vtt(nb_("TA1"), nb_("QA"), nb_("MM"), ALU.add)
+            vcopy(nb_("TA16"), nb_("TA1"))
+            vscat(R("NL", 0, LO + ql), nb_("TA16"), R("DAT", 0, L))
+            copy_dma(R("NL", LO + ql, LO + ql + L), R("SD", 0, L))
+            if t < 2:
+                sx, gp, gl = "SX%d" % t, R("GP0", 0, 12), R("GL%d" % t, 0, 4)
+                vtt(R("NW", 0, 12), R("NV", 0, 12), R("WINF", 0, 12), ALU.mult)
+                vscan(R("CUM", 1, 13), R("ONES", 0, 12), R("NW", 0, 12), ALU.mult, ALU.add)
+                mms([(R("TR", 32, 45), R("TRI"), R("NW", 0, 13), True, False),
+                     (R("TR", 32, 45), R("TRB"), R("NW", 0, 13), False, False),
+                     (R("TR", 32, 45), R("OBD"), R("CUM", 0, 13), False, True)])
+                vtt(R("GP", 0, 12), R("TR", 32, 44), R("LG", 0, 12), ALU.min)
+                vcopy(R("GI", 0, 1), R("TR", 44, 45))
+                vts(gp, R("GP", 0, 12), 1024.0, None, ALU.add)
+                vscat(R("GI", 8, 8 + LN + S), gp, R("IOTA", 0, S))
+                vcopy(R(sx), R("GI", 0, 8 + H))
+                send(t, "x", R(sx))
+                vtt(R("GD"), R("GI", 8, 8 + H), R("DM", 0, H), ALU.mult)
+                vscan(R("GS"), R("RSUM", 0, H), R("GD"), ALU.mult, ALU.add)
+                vcopy(gl, R("GS", 15, H, 16))
+            vts(nb_("CI"), nb_("SI"), 2047, None, ALU.bitwise_and)
+            vts(nb_("U2"), nb_("NV"), -8192.0, float((t + 1) * XS_SLOT), ALU.mult, ALU.add)
+            vtt(nb_("U3"), nb_("U2"), nb_("CI"), ALU.add)
+            vtt(nb_("U4"), nb_("U3"), nb_("LANEX"), ALU.max)
+            vcopy(nb_("CN16"), nb_("U4"))
+            sgather(R("CE", C0 + lo, C0 + lo + L), R("CE", slot, C0 + lo), nb_("CN16"))
+            sgather(R("GG"), R("AC", slot, C0 + lo), R("CN16", 0, 12))
+        rr = "RR%d" % (t % 2)
+        for j in range(6):
+            (vgather if (t, j) in CFG["agv"] else sgather)(R("AG", 512 * j, 512 * j + 512), R("AC", C0, C0 + lo),
+                                                           R(O2, 32 * j, 32 * j + 32))
+        for j in range(6):
+            bank = "R%d" % (j % 2)
+            a = PAD + 512 * j
+            mms([(R(bank), R("OBD"), R(D2, a, a + 512), True, False),
+                 (R(bank, 0, 512, 16), R("ONE2", 0, 128, 1, 0, 2), R("RB", 0, 32, 1, 0, 2), False, False),
+                 (R(bank), R("NBD"), R(D2, a - 1, a + 511), False, True)])
+            act(R(rr, 512 * j, 512 * j + 512), R(bank), ACT.Exp, scale=1.0 / 64)
+            vscan(R("SC", 512 * j, 512 * j + 512), R(rr, 512 * j, 512 * j + 512), R("AG", 512 * j, 512 * j + 512),
+                  ALU.mult, ALU.add)
+        wb = R("TR", 64, 64 + S) if CFG["f2"] else R("CM", 256, 256 + S)
+        mms([(wb, R("OBD"), R(D2, PAD + 15, PAD + S * 16, 16), True, True)])
+        yo = R("YO", S * t, S * t + S)
+        if last:
+            act(wb, wb, ACT.Exp, scale=-1.0 / 64)
+            vtt(yo, R("SC", 15, 3072, 16), wb, ALU.mult)
+        else:
+            act(wb, wb, ACT.Exp, bias=R("MCOL", 6, 7), scale=-1.0 / 64)
+            vtt(R("P4"), R("SC", 15, 3072, 16), wb, ALU.mult)
+            xb = R("TR" if CFG["f2"] else "OH", 256, 256 + S)
+            mms([(xb, R("I4"), R("YS", S * t, S * t + S), True, False), (xb, R("IDF"), R("GG"), False, True)])
+            vtt(R("AC", C0 + lo, C0 + lo + S), xb, R("P4"), ALU.subtract)
+            act(yo, R("P4"), ACT.Copy, scale=4.0)
+            if t < 2:
+                sgather(R("SA%d" % t), R("AC", C0 + lo, C0 + lo + S), R("GL%d" % t, 0, 4))
+                send(t, "a", R("SA%d" % t))
+        dma("y", (lambda tt=t: T.yp[:, S * tt:S * tt + S]), (lambda i=yo: A(i)), [yo], [])
+    return ops, neng
+
+
+def dependences(ops):
+    hist = {}
+    for i, o in enumerate(ops):
+        deps = {}
+        acc = [(r, False) for r in o["rd"]] + [(r, True) for r in o["wr"]]
+        for r, w in acc:
+            psum = r[0] in _PS
+            for (j, r2, w2) in hist.get(r[0], []):
+                if j == i or not overlap(r, r2):
+                    continue
+                if psum:
+                    same = ops[j]["eng"] == o["eng"]
+                    if same and not (w or w2):
+                        continue
+                    deps[j] = deps.get(j, False) or not (same and (o["eng"] == "t" or (w and CFG["lean"])))
+                elif w or w2:
+                    inorder = (w and CFG["lean"] and ops[j]["eng"] == o["eng"] and o["kind"] == "c"
+                               and ops[j]["kind"] == "c")
+                    deps[j] = deps.get(j, False) or not inorder
+        for r, w in acc:
+            lst = hist.setdefault(r[0], [])
+            if w and r[3] == 1 and r[4] == 0 and r[5] == 128 and r[6] == 1 and r[0] not in _PS:
+                lst[:] = [e for e in lst if not (r[1] <= e[1][1] and e[1][2] <= r[2])]
+            if w and r[0] in _PS and any(ops[e[0]]["eng"] != o["eng"] for e in lst):
+                lst[:] = []
+            lst.append((i, r, w))
+        o["deps"] = deps
+    for i, o in enumerate(ops):
+        if o["kind"] == "arr":
+            snd = [j for j in range(i) if ops[j]["kind"] == "send"][-1]
+            o["after"] = snd
+
+
+def one_pass(ops, preds, succ, pri, back):
+    n = len(ops)
+    sem, look = CFG["sem"], CFG["look"]
+    left = [len(p) for p in preds]
+    rdy = [ops[i]["lat"] if back else 0.0 for i in range(n)]
+    start, fin = [0.0] * n, [0.0] * n
+    free = {}
+    ready = [i for i in range(n) if left[i] == 0]
+    order = []
+    while ready:
+        est = {i: max(rdy[i], free.get(ops[i]["eng"], 0.0)) if ops[i]["eng"] else rdy[i] for i in ready}
+        first = min(ready, key=lambda i: (est[i], -pri[i]))
+        e = ops[first]["eng"]
+        pick = max([i for i in ready if ops[i]["eng"] == e and est[i] <= est[first] + look], key=lambda i: (pri[i], -i))
+        ready.remove(pick)
+        order.append(pick)
+        end = est[pick] + ops[pick]["cost"]
+        if e:
+            free[e] = end
+        start[pick] = est[pick]
+        fin[pick] = end + (0.0 if back else ops[pick]["lat"])
+        for k in succ[pick]:
+            hard = ops[pick]["deps"].get(k, True) if back else ops[k]["deps"].get(pick, True)
+            rdy[k] = max(rdy[k], fin[pick] + (sem if hard else 0.0) + (ops[k]["lat"] if back else 0.0))
+            left[k] -= 1
+            if left[k] == 0:
+                ready.append(k)
+    return order, start, fin
+
+
+PLAN = {}
+
+
+def schedule(ops):
+    n = len(ops)
+    if n not in PLAN:
+        preds = [list(o["deps"]) + ([o["after"]] if o["kind"] == "arr" else []) for o in ops]
+        succ = [[] for _ in ops]
+        for i in range(n):
+            for j in preds[i]:
+                succ[j].append(i)
+        pri = [0.0] * n
+        for i in range(n - 1, -1, -1):
+            pri[i] = ops[i]["cost"] + ops[i]["lat"] + CFG["sem"] + max([pri[k] for k in succ[i]] + [0.0])
+        best = None
+        for it in range(CFG["iters"]):
+            order, start, fin = one_pass(ops, preds, succ, pri, False)
+            if best is None or max(fin) < best[0]:
+                best = (max(fin), order, start)
+            pri = one_pass(ops, succ, preds, fin, True)[2]
+            x = CFG["seed"] * 7919 + it
+            for i in range(n):
+                x = (x * 1103515245 + 12345) % 2147483648
+                pri[i] += CFG["noise"] * x / 2147483648
+        PLAN[n] = best
+    for i in range(n):
+        ops[i]["t0"] = PLAN[n][2][i]
+    return PLAN[n][1]
+
+
+def emit(g, T, ops, order, neng):
+    queue = {"v": g.vector, "s": g.scalar, "t": g.tensor, "g": g, "y": g.sync}
+    csem = {"v": "sv", "s": "ss", "t": "st_", "g": "sg"}
+    needed = set()
+    for o in ops:
+        if o["kind"] != "arr":
+            needed.update(j for j in o["deps"] if o["deps"][j])
+    count = {}
+    known = {e: {} for e in queue}
+    totals = {}
+    for i in order:
+        o = ops[i]
+        if o["kind"] == "arr":
+            o["tok"] = (o["x"][0], o["x"][1])
+            o["clock"] = {o["x"][0]: o["x"][1]}
+            totals[o["x"][0]] = o["x"][1]
+            continue
+        e = o["eng"]
+        kn = known[e]
+        want = sorted([j for j in o["deps"] if o["deps"][j]], key=lambda j: -ops[j]["t0"])
+        for j in want:
+            s, v = ops[j]["tok"]
+            if kn.get(s, 0) >= v:
+                continue
+            v = max(ops[k]["tok"][1] for k in want if ops[k]["tok"][0] == s)
+            queue[e].wait_ge(T.sem[s], v)
+            for k in want:
+                if ops[k]["tok"][0] == s:
+                    for s2, v2 in ops[k]["clock"].items():
+                        kn[s2] = max(kn.get(s2, 0), v2)
+        ins = o["fn"]()
+        if o["kind"] == "dma":
+            ins.then_inc(T.sem[o["x"]], 16)
+            o["tok"] = (o["x"], 16)
+        elif o["kind"] == "send":
+            totals["sent"] = totals.get("sent", 0) + neng
+            continue
+        elif i in needed:
+            count[e] = count.get(e, 0) + 1
+            ins.then_inc(T.sem[csem[e]], 1)
+            o["tok"] = (csem[e], count[e])
+        else:
+            continue
+        o["clock"] = dict(kn)
+        o["clock"][o["tok"][0]] = o["tok"][1]
+        totals[o["tok"][0]] = o["tok"][1]
+    for s in totals:
+        if not any(known[e].get(s, 0) >= totals[s] for e in known):
+            g.wait_ge(T.sem[s], totals[s])
+
+
+def rank_program(g, core, T, topo):
+    rank = T.rank_of(core)
+    if rank is None:
+        relay_program(g, core, T, topo)
+        return
+    ops, neng = build(g, core, T, topo, rank)
+    dependences(ops)
+    emit(g, T, ops, schedule(ops), neng)

@@ -3,45 +3,48 @@ from concourse.mybir import AluOpType as ALU, ActivationFunctionType as ACT
 
 CN, Q0, S, H, RO, EPS, RHO = 1280, 384, 192, 64, 4, 44, 60
 LN = S + H
-XS_SLOT = 16 + H + S
-C0 = 3 * XS_SLOT
+C0 = LN
 CT = CN + 3 * LN
 QT = Q0 + 3 * LN
-PAD = 16
-FD = 320
-LO = LN + 4 * FD
-B1 = (RHO + 1) * 65536
+PAD = 0
+LO = 2 * LN + QT
+FD = (LO - LN) // 4
+B1 = RHO * 65536 + 32768
 B2 = EPS * 65536 + 32768
 LNR = 0.668
+GW = H + LN + S - 64
+HL = S // 2
 F, BF, I32, U16 = "float32", "bfloat16", "int32", "uint16"
 
 _SB = {
-    "XS": (768, BF), "YS": (768, BF), "I4": (128, BF), "DR": (4096, BF), "SL2": (72, BF), "SLN": (72, BF), "NBI": (Q0, I32), "DLI": (Q0, I32),
-    "STI": (16, I32), "KK": (QT, BF), "CE": (C0 + CT, BF), "AC": (C0 + CT, F), "NL": (LO + QT, F),
-    "IOTA": (QT, F), "XREP": (768 * 16, BF), "GREP": (H * 16, BF), "D1": (4096, BF), "D20": (PAD + 4096, BF),
+    "XS": (768, BF), "YS": (768, BF), "I4": (128, BF), "I4F": (128, F), "D1R": (3072, BF), "D20R": (3072, BF), "D21R": (3072, BF),
+    "NBI": (Q0, I32), "DLI": (Q0, I32), "STI": (16, I32), "KK": (QT, BF), "CE": (C0 + CT, BF), "AC": (C0 + CT, F),
+    "NL": (LO + QT, F), "IOTA": (QT, F), "XREP": (768 * 16, BF), "D1": (4096, BF), "D20": (PAD + 4096, BF),
     "D21": (PAD + 4096, BF), "AG": (3072, F), "RR0": (3072, F), "RR1": (3072, F), "SC": (3072, F), "O1": (LN, U16),
     "O20": (LN, U16), "O21": (LN, U16), "CANDF": (LN, F), "SD": (FD + LN, F), "DAT": (LN, F),
-    "LIF": (LN, F), "RQF": (LN, F), "RQ16": (LN, U16), "E": (16 * LN, BF),
-    "WM": (LN, BF), "WS": (LN, BF), "MN": (256, F), "MX": (256, F), "XP": (256, F), "OHT": (256, F),
-    "P4": (S, F), "GG": (S, F), "YO": (768, F), "IB": (128, BF), "NIB": (128, BF), "LANE4": (16, F), "LANEO": (16, F),
-    "GI": (8 + LN + S, F), "GD": (H, F), "GS": (H, F), "GL0": (4, U16), "GL1": (4, U16),
+    "LIF": (LN, F), "RQF": (LN, F), "RQ16": (LN, U16), "E": (16 * LN, BF), "CMB": (LN, BF),
+    "WM": (LN, BF), "WS": (LN, BF), "THR": (256, F), "RSUM": (256, BF),
+    "MN": (384, F), "MB": (384, F), "MX": (384, F), "XP": (384, F), "XQ": (384, F), "OHT": (384, BF),
+    "P4": (S, F), "GG": (S, F), "YO": (768, F), "IB": (128, BF), "NIB": (128, BF), "LANE4": (16, F),
+    "GI": (2 * (GW + 64), BF), "RH": (384, BF), "RS": (1024, BF), "RZ": (128, BF), "IOM": (LN, F), "Y4": (3 * S, BF), "ZP": (192, BF), "ZN": (136, BF),
+    "ZPN": (136, BF), "ZS": (144, BF), "ZM": (128, BF),
     "OBD": (128, BF), "NBD": (128, BF), "TRI": (128, BF), "TRB": (128, BF), "IDF": (128, F), "SL": (72, BF),
-    "DM": (128, F), "BSEL": (8, F), "KC1": (128, BF), "KC2": (128, BF), "ONE2": (128, BF), "RB": (32, BF),
-    "KPAT": (128, F), "GPAT": (128, F), "RMIN": (128, F), "RMAX": (128, F), "RSUM": (256, BF), "MD": (768, F),
-    "WL": (16, F), "THR": (256, F), "PI": (8, I32), "CF": (8, F), "IU": (64, U16), "BL": (8, U16),
-    "LANEL": (16, F), "LANEX": (16, F), "LG": (16, F), "MCOL": (8, F), "ONES": (16, BF),
+    "DM": (128, F), "BSEL": (8, F), "KC1": (128, BF), "KC2": (128, BF), "ONE2": (144, BF), "RB": (32, BF),
+    "KPAT": (256, F), "GPAT": (128, F), "RMIN": (128, F), "RMAX": (128, F), "RMC": (128, F), "MD": (512, BF), "MT": (384, BF),
+    "TI": (24, I32), "T2": (24, I32), "SEL": (24, I32), "RI": (24, I32),
+    "WL": (16, F), "THL": (16, F), "THX": (16, F), "PI": (8, I32), "CF": (16, F), "IU": (16, U16), "BL": (8, U16),
+    "LANEL": (16, F), "LX": (16, F), "LG": (16, F), "MCOL": (8, F),
     "ST16": (16, U16), "QL0": (16, U16), "QL1": (16, U16), "QL2": (16, U16), "QL3": (16, U16), "CLF": (8, F),
-    "K1I": (16, I32), "QI": (16, I32), "QF": (16, F), "TI": (16, I32), "T2": (16, I32), "SEL": (16, I32), "RI": (16, I32),
-    "LVF": (16, F), "WINF": (16, F), "FK": (16, F), "WF": (16, F), "QD": (16, F), "QB": (16, F), "QA": (16, F),
-    "NV": (16, F), "MM": (16, F), "TB1": (16, F), "TB16": (16, U16), "TA1": (16, F),
-    "TA16": (16, U16), "SI": (16, I32), "CI": (16, I32), "U2": (16, F), "U3": (16, F), "U4": (16, F),
+    "K1I": (16, I32), "QI": (16, I32), "QF": (16, F),
+    "LVF": (16, F), "WINF": (16, F), "HD": (16, F), "HF": (16, F), "HM": (16, F), "HM2": (16, F), "YY": (16, F),
+    "FF": (16, F), "TB1": (16, F), "TB16": (16, U16), "TA1": (16, F), "WTH": (16, F),
+    "TA16": (16, U16), "SI": (16, I32), "CI": (16, I32), "U4": (16, F),
     "CN16": (16, U16), "NW": (16, BF), "CUM": (16, BF), "GP": (16, F), "GP0": (16, U16),
     "PU1": (8, F), "PU2": (8, F), "PU3": (8, F),
-    "SX0": (8 + H, U16), "SX1": (8 + H, U16), "LU0": (8 + H, U16), "LU1": (8 + H, U16), "XR0": (S, BF), "XR1": (S, BF), "SA0": (H, F), "SA1": (H, F),
+    "SX0": (17, U16), "SX1": (17, U16), "LU0": (17, U16), "LU1": (17, U16), "XR0": (S + 16, BF), "XR1": (S + 16, BF),
+    "SA0": (H, F), "SA1": (H, F),
 }
-_PS = ["K0", "K1", "R0", "R1", "CM", "TR", "OH", "F0"]
-CFG = {"direct": {(0, 1, 0), (1, 1, 0), (2, 1, 0), (3, 1, 0)}, "off": set(), "agv": set(), "iters": 4,
-       "gc": 1.5, "sc": 3.8, "pe": 0.6, "sem": 60.0, "look": 120.0, "gpe": False, "relu": set(), "merge": False, "lean": True, "ggrep": set(), "nldma": False, "f2": False, "seed": 0, "noise": 0.0, "f": 1.0}
+_PS = ["K0", "K1", "R0", "R1", "CM", "TR", "F0", "F1"]
 SCRATCH = {}
 POOL = {}
 for _n in _SB:
@@ -53,11 +56,46 @@ for _n in _SB:
         SCRATCH[_n] = ("sbuf", [128, _w], _d)
 for _n in _PS:
     SCRATCH[_n] = ("psum", [128, 512], F)
-NDMA = 36
+NDMA = 60
 SEMAPHORES = (["sv", "ss", "st_", "sg", "sent", "hsent"] + ["dm%d" % i for i in range(NDMA)]
               + [a + b + c for a in "gh" for b in "exa" for c in "01"])
 
-CFG.update({'direct': [(0, 1, 0), (1, 1, 0), (1, 2, 0), (1, 2, 1), (3, 1, 0), (3, 2, 0), (3, 2, 1)], 'off': [(0, 1, 1, 0), (0, 1, 1, 1), (0, 1, 2, 0), (0, 2, 0, 1), (0, 2, 1, 1), (0, 2, 2, 1), (1, 1, 3, 1), (1, 2, 2, 1), (2, 1, 1, 0), (2, 1, 3, 0), (2, 2, 0, 0), (2, 2, 0, 1), (3, 1, 3, 1)], 'agv': [(3, 4), (3, 5)], 'iters': 8, 'gc': 1.6, 'sc': 3.8, 'pe': 0.75, 'sem': 80.0, 'look': 30, 'nldma': True, 'seed': 873, 'noise': 250, 'f': 1.2})
+CFG = {
+    "direct": [(0, 1, 0), (1, 1, 0), (2, 1, 0), (3, 1, 0)],
+    "off": [(0, 1, 2), (0, 1, 5), (0, 2, 2), (0, 2, 5), (3, 1, 5)],
+    "f1": [(0, 1, 5)],
+    "em": [],
+    "agv": [],
+    "cx": [(t, h) for t in range(3) for h in range(2)],
+    "g3": [1],
+    "gv": [],
+    "gx": [], "dfm": 5, "dg": [], "ga": False, "m1": [], "gm": [], "ohm": False, "agm": 1, "eg": 4, "vm": 2, "two": False, "wsel": True, "pe4": False, "xq": True, "xr0": (10, 5), "xr1": (6, 0), "split": [3],
+    "iters": 8, "look": 30, "seed": 1, "noise": 250,
+    "cost": {"f": 1.1, "gc": 1.56, "sc": 3.8, "pe": 0.5, "sem": 120.0, "ov": 20.0, "dl": 1500.0, "rl": 2000.0},
+}
+CFG.update({'direct': [(0, 1, 0), (0, 2, 0), (1, 1, 0), (1, 2, 0), (2, 1, 0), (2, 2, 0), (3, 1, 0), (3, 2, 0)], 'off': [(0, 1, 2), (0, 1, 5), (0, 2, 2), (0, 2, 5), (1, 1, 3), (1, 2, 0), (2, 2, 0), (3, 1, 5)], 'f1': [(0, 1, 5), (1, 1, 3), (1, 1, 7), (1, 2, 1), (1, 2, 7), (2, 1, 2), (2, 1, 3), (2, 1, 7), (2, 2, 0)], 'relu': {}, 'agv': [(3, 1), (3, 3)], 'cx': [(0, 0), (0, 1), (1, 0), (1, 1), (2, 0), (2, 1)], 'g3': [], 'gv': [], 'eg': 8, 'vm': 1, 'two': False, 'wsel': True, 'pe4': False, 'xq': False, 'xr0': (10, 5), 'xr1': (6, 0), 'split': [2, 3], 'iters': 4, 'look': 0.1, 'seed': 378, 'noise': 250, 'cost': {'f': 1.1, 'gc': 1.56, 'sc': 3.8, 'pe': 0.5, 'sem': 80.0, 'ov': 0.0, 'dl': 1500.0, 'rl': 2000.0}})
+CFG.update({'off': [(0, 1, 2), (0, 1, 5), (0, 2, 2), (0, 2, 5), (1, 2, 0), (2, 2, 0), (3, 1, 5)], 'f1': [(0, 1, 5), (1, 1, 7), (1, 2, 7), (2, 1, 7), (2, 2, 0)], 'cx': [(0, 0), (0, 1), (1, 0), (1, 1), (2, 1)], 'gv': [(1, 1, 6)], 'xr1': (12, 0), 'split': [0, 2], 'seed': 2868, 'noise': 100})
+CFG.update({"tabu": 0, "tries": 12, "moves": 0, "back": 1.0, "reach": 40, "slack": 0.0005, "figs": [
+    {"f": 1.0, "gc": 1.56, "sc": 3.8, "pe": 0.45, "sem": 200.0, "ov": 0.0, "dl": 1500.0, "rl": 2000.0},
+    {"f": 1.4, "gc": 2.2, "sc": 5.0, "pe": 0.62, "sem": 120.0, "ov": 20.0, "dl": 2200.0, "rl": 3500.0}]})
+MID = {"f": 1.15, "gc": 1.75, "sc": 4.2, "pe": 0.52, "sem": 160.0, "ov": 0.0, "dl": 1700.0, "rl": 2500.0}
+CFG.update(m1=[1, 2, 3], ohm=True, agm=1, em=[], cx=[(t, h) for t in range(3) for h in range(2)], split=[3], gv=[],
+           two=True, xq=True, xr1=(4, 0), cost=MID, tabu=0, moves=70000, slack=.004, figs=[MID], iters=20, back=.02,
+           noise=400, look=.2, agv=[(3, 0), (3, 1)],
+           direct=[(t, 1, 0) for t in range(4)] + [(t, 2, k) for t in range(4) for k in range(2)],
+           off=[(0, 1, 2), (0, 2, 2), (0, 1, 5), (0, 2, 5), (0, 1, 1), (0, 2, 4), (1, 2, 0), (1, 1, 0), (2, 2, 0), (2, 1, 0),
+                (3, 1, 5), (3, 1, 2)],
+           f1=[(0, 1, 5), (0, 2, 5), (1, 1, 7), (1, 2, 7), (2, 1, 7), (2, 2, 7), (3, 1, 2)])
+CFG.update(moves=70000, slack=.005, ga=False, wsel=False, agv=[(3, 0)], look=.1, iters=60, noise=200, seed=3,
+           off=[(0, 1, 2), (0, 2, 2), (0, 1, 5), (0, 2, 5), (1, 2, 0), (2, 2, 0), (1, 1, 0), (3, 1, 5), (2, 1, 0), (0, 1, 1)],
+           cost=dict(f=1.15, gc=1.65, sc=4.6, pe=.65, sem=150, ov=0, dl=1900, rl=3000),
+           figs=[dict(f=1.15, gc=1.75, sc=4.2, pe=.52, sem=170, ov=0, dl=1700, rl=2500),
+                 dict(f=1.1, gc=1.5, sc=5, pe=.78, sem=130, ov=0, dl=2000, rl=3500)])
+CFG.update(moves=60000, gx=[0, 1, 2], wsel=True, agv=[(3, 0), (3, 1)],
+           off=[(0, 1, 2), (0, 2, 2), (0, 1, 5), (0, 2, 5), (0, 1, 1), (0, 2, 4), (1, 2, 0), (1, 1, 0), (2, 2, 0), (2, 1, 0),
+                (3, 1, 5), (3, 1, 2)],
+           figs=[dict(f=1.1, gc=1.65, sc=4.0, pe=.5, sem=190, ov=0, dl=1600, rl=2200),
+                 dict(f=1.15, gc=1.5, sc=4.5, pe=.64, sem=150, ov=0, dl=3500, rl=5000)])
 CYC = 0.83
 
 
@@ -75,9 +113,11 @@ def two_byte(r):
     return r[0] in _SB and _SB[r[0]][1] in (BF, U16)
 
 
+def psum(r):
+    return r[0] not in _SB
+
+
 def overlap(a, b):
-    if a[0] in _PS:
-        return True
     if a[2] <= b[1] or b[2] <= a[1]:
         return False
     if a[3] == b[3] and a[3] > 1 and (a[1] - b[1]) % a[3] != 0:
@@ -96,7 +136,7 @@ def route(T, topo, rank, t):
 
 
 def few_engines(topo, src, far):
-    es = topo.engines(src, far)[::2][:4]
+    es = topo.engines(src, far)
     return sum(1 << e for e in es), len(es)
 
 
@@ -106,11 +146,29 @@ def far_core(T, topo, src):
 
 def landing(kind, t):
     if kind == "e":
-        return R("XR%d" % t)
+        return R("XR%d" % t, 0, S)
     if kind == "x":
-        return R("LU%d" % t)
+        return R("LU%d" % t, 0, 4)
     a = C0 + CN + LN * (t + 1) + S
     return R("AC", a, a + H)
+
+
+def chunks(t):
+    if t in (0, RO - 1):
+        return [(0, HL), (HL, HL)]
+    return [(0, HL), (HL, HL), (S, H)] if t in CFG["g3"] else [(0, 128), (128, 128)]
+
+
+def signed(t, ph, u):
+    return (t, ph, u) in CFG["em"] and (t, ph, u) not in CFG["off"] and 32 * u < S
+
+
+def xlanes(t):
+    return 32 + 32 * max(u for ph in (1, 2) for u in range(S // 32) if (t, ph, u) not in CFG["off"])
+
+
+DIFF_ROWS = ([(0, "ZN", 1)] + [(k, "ZPN", k) for k in range(1, 7)] + [(7, "ZP", 7)],
+             [(7, "ZN", 0)] + [(k, "ZPN", k - 8) for k in range(8, 15)] + [(15, "ZP", 7)])
 
 
 def relay_program(g, core, T, topo):
@@ -136,22 +194,25 @@ def relay_program(g, core, T, topo):
 
 def build(g, core, T, topo, rank):
     ops = []
-    PEC, GC, SCC = CFG["pe"], CFG["gc"], CFG["sc"]
     V, SE, PE, SY = g.vector, g.scalar, g.tensor, g.sync
 
+    leases = [0]
+
+    def lease(bank):
+        leases[0] += 1
+        return "%s#%d" % (bank, leases[0])
+
     def A(r):
-        name, b = POOL.get(r[0], (r[0], 0))
+        name, b = POOL.get(r[0], (r[0].split("#")[0], 0))
         return T[name][slice(r[4], r[5], r[6]) if r[6] > 1 else slice(r[4], r[5]),
                        slice(b + r[1], b + r[2], r[3]) if r[3] > 1 else slice(b + r[1], b + r[2])]
 
     def IND(w, o):
         return A(w).indirect(A(o))
 
-    def op(eng, fn, rd, wr, cost, lat=0.0, kind="c", extra=None):
-        ops.append({"eng": eng, "fn": fn, "rd": rd, "wr": wr, "cost": cost, "lat": lat, "kind": kind, "x": extra})
-
-    def vcost(n, c):
-        return max(64, n * c) * CYC * CFG["f"]
+    def op(eng, fn, rd, wr, work, kind="c", extra=None):
+        ops.append({"eng": eng, "fn": fn, "rd": rd, "wr": wr, "work": work, "kind": kind, "x": extra,
+                    "banks": sorted(set(r[0][:2] for r in rd + wr if psum(r))), "starts": False, "group": 0})
 
     def sc(x):
         return A(x) if isinstance(x, tuple) else x
@@ -159,45 +220,44 @@ def build(g, core, T, topo, rank):
     def refs(*xs):
         return [x for x in xs if isinstance(x, tuple)]
 
+    def plain(o, *ins):
+        return ("plain", width(o) * (0.5 if all(two_byte(r) for r in (o,) + ins) else 1))
+
     def vcopy(o, i):
-        op("v", lambda: V.tensor_copy(A(o), A(i)), [i], [o], vcost(width(o), 0.5 if two_byte(o) and two_byte(i) else 1))
+        op("v", lambda: V.tensor_copy(A(o), A(i)), [i], [o], plain(o, i))
 
     def vts(o, i, s1, s2, o0, o1=None):
         if o1 is None:
             fn = lambda: V.tensor_scalar(A(o), A(i), sc(s1), None, o0)
         else:
             fn = lambda: V.tensor_scalar(A(o), A(i), sc(s1), sc(s2), o0, o1)
-        op("v", fn, [i] + refs(s1, s2), [o], vcost(width(o), 0.5 if two_byte(o) and two_byte(i) else 1))
+        op("v", fn, [i] + refs(s1, s2), [o], plain(o, i))
 
     def vtt(o, a, b, alu):
         op("v", lambda: V.tensor_tensor(A(o), A(a), A(b), alu), [a, b], [o],
-           vcost(width(o), 1 if a[0] in _PS or b[0] in _PS else 2))
+           ("plain", width(o) * (1 if psum(a) or psum(b) else 2)))
 
     def vset(o, c):
-        op("v", lambda: V.memset(A(o), c), [], [o], vcost(width(o), 0.5 if two_byte(o) else 1))
+        op("v", lambda: V.memset(A(o), c), [], [o], plain(o))
 
     def vscan(o, d0, d1, o0, o1):
-        op("v", lambda: V.tensor_tensor_scan(A(o), A(d0), A(d1), 0.0, o0, o1), [d0, d1], [o],
-           vcost(width(o), 0.5 if two_byte(o) and two_byte(d0) and two_byte(d1) else 1))
+        op("v", lambda: V.tensor_tensor_scan(A(o), A(d0), A(d1), 0.0, o0, o1), [d0, d1], [o], plain(o, d0, d1))
 
     def vgather(o, w, l):
-        op("v", lambda: V.tensor_copy(A(o), IND(w, l)), [w, l], [o], 50 + width(o) * GC * CYC)
+        op("v", lambda: V.tensor_copy(A(o), IND(w, l)), [w, l], [o], ("gather", width(o)))
 
     def vgtt(o, w, l, b, alu):
-        op("v", lambda: V.tensor_tensor(A(o), IND(w, l), A(b), alu), [w, l, b], [o], 50 + width(o) * GC * CYC)
+        op("v", lambda: V.tensor_tensor(A(o), IND(w, l), A(b), alu), [w, l, b], [o], ("gather", width(o)))
 
     def vscat(w, l, i):
-        op("v", lambda: V.tensor_copy(IND(w, l), A(i)), [l, i], [w], 50 + width(i) * SCC * CYC)
-
-    def vscat_tt(w, l, a, b, alu):
-        op("v", lambda: V.tensor_tensor(IND(w, l), A(a), A(b), alu), [l, a, b], [w], 50 + width(a) * SCC * CYC)
+        op("v", lambda: V.tensor_copy(IND(w, l), A(i)), [l, i], [w], ("scatter", width(i)))
 
     def act(o, i, func, bias=0.0, scale=1.0):
         op("s", lambda: SE.activation(A(o), A(i), func, bias=sc(bias), scale=sc(scale)), [i] + refs(bias, scale), [o],
-           vcost(width(o), 1))
+           ("plain", width(o)))
 
     def sgather(o, w, l):
-        op("s", lambda: SE.activation(A(o), IND(w, l), ACT.Copy), [w, l], [o], 65 + width(o) * GC * CYC)
+        op("s", lambda: SE.activation(A(o), IND(w, l), ACT.Copy), [w, l], [o], ("gather", width(o)))
 
     def mms(lst):
         def fn():
@@ -205,32 +265,35 @@ def build(g, core, T, topo, rank):
             for o, l, r, st, sp in lst:
                 ins = PE.matmul(A(o), A(l), A(r), st, sp)
             return ins
-        c = sum(max(min(64, width(l)), width(r)) * (1 if two_byte(l) else 4) for o, l, r, st, sp in lst) * PEC
+        c = sum(max(min(64, width(l)), width(r)) * (1 if two_byte(l) else 4) for o, l, r, st, sp in lst)
         rd = []
         for o, l, r, st, sp in lst:
-            rd += [l, r]
-        op("t", fn, rd, [lst[0][0]], c, 40)
+            rd += [x for x in (l, r) if x not in rd]
+        op("t", fn, rd, [R(lst[0][0][0], min(m[0][1] for m in lst), max(m[0][2] for m in lst))], ("tensor", c))
+        ops[-1]["starts"] = any(m[3] for m in lst)
+        ops[-1]["group"] = (1 if lst[0][3] and not lst[-1][4] else 0) - (1 if lst[-1][4] and not ops[-1]["starts"] else 0)
 
     def giota(o, pat, base, cm):
         if _SB[o[0]][1] == I32:
             fn = lambda: g.iota(A(o), pat, base, cm)
         else:
             fn = lambda: g.iota(A(o), pat, base, cm, allow_small_or_imprecise_dtypes=True)
-        op("g", fn, [], [o], 130 + 2 * width(o) * CYC)
+        op("g", fn, [], [o], ("pool", 130 + 2 * width(o) * CYC))
 
     def gsel(o, i, pat, cmp_, base, cm):
-        op("g", lambda: g.affine_select(A(o), A(i), pat, cmp_, 0.0, base, cm), [i], [o], 170 + 2 * width(o) * CYC)
+        op("g", lambda: g.affine_select(A(o), A(i), pat, cmp_, 0.0, base, cm), [i], [o],
+           ("pool", 170 + 2 * width(o) * CYC))
 
     ndma = [0]
 
-    def dma(q, out, in_, rd, wr, lat=2000.0):
+    def dma(q, out, in_, rd, wr, more=0.0):
         k = ndma[0]
         ndma[0] += 1
         eng = {"y": SY, "s": SE, "g": g}[q]
-        op(q, lambda: eng.dma_start(out(), in_()), rd, wr, 1000 if q == "g" else 60, lat, "dma", "dm%d" % k)
+        op(q, lambda: eng.dma_start(out(), in_()), rd, wr, ("dma", 1000 if q == "g" else 60, more), "dma", "dm%d" % k)
 
-    def load(q, o, src, lo, hi, lat=2000.0):
-        dma(q, lambda: A(o), lambda: T[src][:, lo:hi], [], [o], lat)
+    def load(q, o, src, lo, hi, more=0.0):
+        dma(q, lambda: A(o), lambda: T[src][:, lo:hi], [], [o], more)
 
     def copy_dma(o, i):
         dma("y", lambda: A(o), lambda: A(i), [i], [o])
@@ -245,7 +308,7 @@ def build(g, core, T, topo, rank):
         sem = T.sem[("g%s%d" if via is None else "h%s%d") % (kind, t)]
         land = landing(kind, t)
         op("g", lambda: g.remote_dma(A(land), A(src), sem, T.sem.sent, pid, rid, mask), [src], [],
-           1500 if kind == "e" else 500, 0, "send")
+           ("send", 1500 if kind == "e" else 500), "send")
         me = len(ops) - 1
         frm = (rank - 1 - t % (n - 1)) % n
         _, v2 = route(T, topo, frm, t)
@@ -253,121 +316,140 @@ def build(g, core, T, topo, rank):
             cnt = few_engines(topo, T.cores[frm], far_core(T, topo, T.cores[frm]))[1]
         else:
             cnt = few_engines(topo, v2, core)[1]
-        op(None, None, [], [land], 0, 3000.0 if via is None else 6000.0, "arr", ("g%s%d" % (kind, t), cnt, me))
+        op(None, None, [], [land], ("arrive", 1 if via is None else 2), "arr", ("g%s%d" % (kind, t), cnt, me))
+
+    compact = len(CFG["cx"]) > 0
+    plainp = len(CFG["cx"]) < 2 * RO
+    QOFF = LN if CFG["two"] else LO
 
     load("y", R("STI"), "st", 0, 16)
     load("s", R("NBI"), "nb", 0, Q0)
     load("y", R("XS"), "xs", 0, 768)
     load("s", R("KK", 0, Q0), "kq", 0, Q0)
     load("y", R("DLI"), "dl", 0, Q0)
-    load("y", R("CE", C0, C0 + CN), "cc", 0, CN, 2500)
-    load("g", R("AC", C0, C0 + CN), "aa", 0, CN, 4000)
+    load("y", R("CE", C0, C0 + CN), "cc", 0, CN, 500)
+    load("g", R("AC", C0, C0 + CN), "aa", 0, CN, 2000)
     load("y", R("YS"), "ys", 0, 768)
     for t in range(2):
         send(t, "e", R("XS", S * t, S * t + S))
     for t in range(3):
-        a = (2 - t) * XS_SLOT + 16 + H
-        load("y", R("CE", a, a + S), "xs", S * t, S * t + S)
         load("y", R("KK", Q0 + LN * t, Q0 + LN * t + S), "xs", S * t, S * t + S)
 
+    vset(R("ZM"), 0.0)
+    vset(R("ONE2"), 1.0)
+    for r in ([R("AC", 0, 128), R("AC", 128, C0), R("CE", 0, H), R("CE", C0 + CN + S, C0 + CN + LN),
+               R("KK", Q0 + S, Q0 + LN), R("XR0", S, S + 16), R("XR1", S, S + 16), R("AC", C0 + CN + S, C0 + CN + LN),
+               R("NL", LO + Q0 + S, LO + Q0 + LN), R("NL", LN + Q0 + S, LN + Q0 + LN)]
+              + ([R("MN", 256), R("MB", 256), R("MX", 256)] if CFG["g3"] else [])):
+        act(r, R("ZM", 0, width(r)), ACT.Copy)
+    for r in [R("MN", 0, 256), R("MB", 0, 256)] + ([] if CFG["two"] else [R("SD", S, FD)]):
+        act(r, R("AC", 0, width(r)), ACT.Copy)
+    vset(R("RI"), 0)
+    vset(R("CUM"), 0.0)
+    vset(R("MCOL", 0, 1), 84.0)
+    vset(R("MCOL", 1, 2), math.log(0.25))
+    if plainp:
+        vset(R("RB"), -8192.0)
     giota(R("PI", 0, 1), [[0, 1]], 0, 1)
     giota(R("IOTA", 0, 256), [[1, 256]], 0, 0)
-    giota(R("KPAT"), [[0, 8], [1, 16]], 0, 0)
+    giota(R("KPAT", 0, 128), [[0, 8], [1, 16]], 0, 0)
+    if CFG["ohm"]:
+        giota(R("KPAT", 128, 256), [[0, 8], [1, 16]], 0, 0)
     giota(R("GPAT"), [[1, 8], [0, 16]], 0, 0)
-    giota(R("IOTA", 256, QT), [[1, QT - 256]], 256, 0)
-    giota(R("MD", 0, 256), [[96, 2], [1, 128]], CN, 0)
-    giota(R("MD", 256, 768), [[1, 512]], CN + LN, 0)
-    for j in range(6):
-        gsel(R("MD", 128 * j, 128 * j + 128), R("MD", 128 * j, 128 * j + 128), [[-1, 128]], ALU.is_equal, 0, 1)
+    giota(R("IOTA", 256, Q0 + LN), [[1, Q0]], 256, 0)
+    giota(R("IOTA", Q0 + LN, QT), [[1, 2 * LN]], Q0 + LN, 0)
+    md = {}
+    for l0, cnt in sorted(set(ch for t in range(RO - 1) for ch in chunks(t)), reverse=True):
+        if l0 not in md:
+            md[l0] = 128 * len(md)
+            gsel(R("MD", md[l0], md[l0] + cnt), R("IOTA", l0, l0 + cnt), [[-1, cnt]], ALU.is_equal, 0, 1)
+    for j in range(2):
+        giota(R("GI", j * (GW + 64), j * (GW + 64) + H), [[0, H]], S, 0)
     vts(R("PI", 1, 2), R("PI", 0, 1), 15, None, ALU.bitwise_and)
     vts(R("PI", 2, 3), R("PI", 0, 1), 4, None, ALU.arith_shift_right)
-    vcopy(R("CF", 0, 3), R("PI", 0, 3))
-    p_, pm, pg = R("CF", 0, 1), R("CF", 1, 2), R("CF", 2, 3)
-    vts(R("CF", 3, 4), pg, 8.0, 7.0, ALU.mult, ALU.add)
-    vts(R("CF", 4, 5), p_, 0.0, 2048.0, ALU.is_equal, ALU.mult)
-    vts(R("CF", 5, 6), p_, 1.0, -float(B1), ALU.is_equal, ALU.mult)
-    vts(R("CF", 6, 7), p_, 1.0, -float(B2), ALU.is_equal, ALU.mult)
-    vts(R("KC1"), R("KPAT"), R("CF", 4, 5), R("CF", 5, 6), ALU.mult, ALU.add)
-    vts(R("KC2"), R("KPAT"), R("CF", 4, 5), R("CF", 6, 7), ALU.mult, ALU.add)
-    vts(R("DM"), R("KPAT"), pm, None, ALU.is_equal)
+    vts(R("PI", 3, 4), R("PI", 0, 1), 63, None, ALU.bitwise_and)
+    vcopy(R("CF", 0, 4), R("PI", 0, 4))
+    p_, pm, pg, p64 = R("CF", 0, 1), R("CF", 1, 2), R("CF", 2, 3), R("CF", 3, 4)
+    g8 = R("CF", 4, 5)
+    vts(g8, pg, 8.0, 7.0, ALU.mult, ALU.add)
+    vts(R("CF", 5, 6), p_, 0.0, 2048.0, ALU.is_equal, ALU.mult)
+    vts(R("CF", 6, 7), p_, 1.0, -float(B1), ALU.is_equal, ALU.mult)
+    vts(R("CF", 7, 8), p_, 1.0, -float(B2), ALU.is_equal, ALU.mult)
+    kpat = R("KPAT", 0, 128)
+    vts(R("KC1"), kpat, R("CF", 5, 6), R("CF", 6, 7), ALU.mult, ALU.add)
+    vts(R("KC2"), kpat, R("CF", 5, 6), R("CF", 7, 8), ALU.mult, ALU.add)
+    vts(R("DM"), kpat, pm, None, ALU.is_equal)
     vts(R("OBD"), R("GPAT"), pg, None, ALU.is_equal)
-    act(R("NBD"), R("OBD"), ACT.Copy, scale=-1.0)
     vts(R("BSEL"), R("IOTA", 0, 8), pg, None, ALU.is_equal)
-    vts(R("IDF"), R("IOTA", 0, 128), p_, None, ALU.is_equal)
-    vts(R("SL"), R("IOTA", 0, 72), R("CF", 3, 4), 65536.0, ALU.is_equal, ALU.mult)
+    gsel(R("IB"), R("ONE2", 0, 128), [[-1, 128]], ALU.is_equal, 0, 1)
+    act(R("IDF"), R("IB"), ACT.Copy)
+    vts(R("SL"), R("IOTA", 0, 72), g8, 65536.0, ALU.is_equal, ALU.mult)
     gsel(R("TRI"), R("OBD"), [[1, 128]], ALU.is_gt, 0, -1)
-    act(R("TRB"), R("IDF"), ACT.Copy, scale=-1024.0)
-    act(R("IB"), R("IDF"), ACT.Copy)
-    act(R("NIB"), R("IDF"), ACT.Copy, scale=-1.0)
-    vts(R("RMIN"), R("KPAT"), 0.0, 2.0 ** 25, ALU.is_equal, ALU.mult)
-    act(R("RMAX"), R("RMIN"), ACT.Identity, bias=R("CF", 7, 8), scale=-1.0)
-    for j in range(2):
-        act(R("RSUM", 128 * j, 128 * j + 128), R("RMIN"), ACT.Identity, bias=R("MCOL", 7, 8), scale=-2.0 ** -25)
-    act(R("MN"), R("IOTA", 0, 256), ACT.Copy, scale=0.0)
-    vcopy(R("IU"), R("IOTA", 0, 64))
+    act(R("TRB"), R("IB"), ACT.Copy, scale=-1024.0)
+    act(R("NIB"), R("IB"), ACT.Copy, scale=-1.0)
+    act(R("I4"), R("IB"), ACT.Copy, scale=0.25)
+    for t in range(RO - 1):
+        act(R("MT", 128 * t, 128 * t + 128), R("IB"), ACT.Copy, scale=float(CN + LN * t))
+    if CFG["pe4"]:
+        act(R("I4F"), R("IB"), ACT.Copy, scale=-0.25)
+    if plainp:
+        act(R("NBD"), R("OBD"), ACT.Copy, scale=-1.0)
+    vts(R("RMIN"), kpat, 0.0, 2.0 ** 25, ALU.is_equal, ALU.mult)
+    vts(R("RMAX"), R("RMIN"), -1.0, 4096.0, ALU.mult, ALU.add)
+    vts(R("RMC"), R("RMIN"), 0.625, -2.0 ** 24, ALU.mult, ALU.add)
+    vcopy(R("IU"), R("IOTA", 0, 16))
     vts(R("BL"), R("IOTA", 0, 8), 16.0, 15.0, ALU.mult, ALU.add)
     vts(R("LANEL"), R("IOTA", 0, 16), 16.0, pm, ALU.mult, ALU.add)
-    vts(R("LANEX", 0, 12), R("LANEL", 0, 12), float(16 + H), None, ALU.add)
-    vts(R("LANEX", 12, 16), R("LANEL", 12, 16), float(16 - S), None, ALU.add)
+    vts(R("LX", 0, 12), R("LANEL", 0, 12), 2.0 ** 23 + H - C0, None, ALU.add)
+    vts(R("LX", 12, 16), R("LANEL", 12, 16), 2.0 ** 23 - S - C0, None, ALU.add)
     vts(R("LG"), R("LANEL"), float(LN - 1024), None, ALU.add)
-    vts(R("LANEO"), R("LANEL"), -float(LO), None, ALU.add)
-    vset(R("MCOL", 4, 5), 84.0)
-    vset(R("MCOL", 5, 6), 84.0 + math.log(2.5))
-    vset(R("MCOL", 6, 7), math.log(0.25))
-    act(R("WL"), R("LANEL"), ACT.Exp, bias=R("MCOL", 4, 5), scale=-LNR)
-    act(R("F0", 0, 256), R("IOTA", 0, 256), ACT.Exp, bias=R("MCOL", 5, 6), scale=-LNR)
-    for j in range(2):
-        vtt(R("THR", 128 * j, 128 * j + 128), R("F0", 128 * j, 128 * j + 128), R("DM"), ALU.mult)
-    act(R("LANE4"), R("LANEL"), ACT.Copy, scale=4.0)
-    return_fill = [(R("ONE2"), 1.0), (R("RB"), -8192.0), (R("ONES"), 1.0), (R("LVF"), 1.0), (R("D20", 0, PAD), 0.0), (R("D21", 0, PAD), 0.0),
-                   (R("NW"), 0.0), (R("CUM"), 0.0), (R("AC", 2 * XS_SLOT, C0), 0.0), (R("MCOL", 7, 8), 1.0),
-                   (R("NL", LO + Q0 + S, LO + Q0 + LN), 0.0), (R("SD", S, FD), 0.0), (R("GI", 0, 8 + H), 0.0),
-                   (R("NL", LN + Q0 + S, LN + Q0 + LN), 0.0), (R("KK", Q0 + S, Q0 + LN), 0.0),
-                   (R("CE", 2 * XS_SLOT, 2 * XS_SLOT + 16 + H), 0.0), (R("CE", C0 + CN + S, C0 + CN + LN), 0.0),
-                   (R("AC", C0 + CN + S, C0 + CN + LN), 0.0), (R("CE", 0, 16), 0.0), (R("CE", XS_SLOT, XS_SLOT + 16), 0.0)]
-    pre = len(ops)
-    vset(R("CF", 7, 8), 4096.0)
-    for r, c in return_fill:
-        vset(r, c)
-    vset(R("SEL"), 0)
-    vset(R("RI"), 0)
-    fills = ops[pre:]
-    del ops[pre:]
-    ops[0:0] = fills
-    for j in range(2):
-        copy_dma(R("AC", j * XS_SLOT, (j + 1) * XS_SLOT), R("AC", 2 * XS_SLOT, C0))
+    act(R("WL"), R("LANEL"), ACT.Exp, bias=R("MCOL", 0, 1), scale=-LNR)
+    gsel(R("ZS"), R("ONE2"), [[1, 144]], ALU.is_equal, -15, -1)
+    vts(R("CF", 8, 9), pm, 0.0, None, ALU.is_equal)
+    if CFG["gx"]:
+        vts(R("CF", 9, 12), R("IOTA", 8, 11), pm, None, ALU.is_equal)
+    act(R("ZS"), R("ZS"), ACT.Copy, scale=R("CF", 8, 9))
+    if CFG["wsel"]:
+        act(R("THL"), R("WL"), ACT.Copy, scale=2.5)
+        act(R("THX", 0, 12), R("WL", 0, 12), ACT.Copy, scale=2.5)
+    else:
+        vset(R("MCOL", 2, 3), 84.0 + math.log(2.5))
+        vset(R("LVF"), 1.0)
+        act(R("THR"), R("IOTA", 0, 256), ACT.Exp, bias=R("MCOL", 2, 3), scale=-LNR)
+        for j in range(2):
+            vtt(R("THR", 128 * j, 128 * j + 128), R("THR", 128 * j, 128 * j + 128), R("DM"), ALU.mult)
+            vts(R("RSUM", 128 * j, 128 * j + 128), kpat, 0.0, None, ALU.not_equal)
+    if not CFG["two"]:
+        act(R("LANE4"), R("LANEL"), ACT.Copy, scale=4.0)
+    if compact:
+        giota(R("ZP"), [[0, 3], [1, 64]], 0, 0)
+        giota(R("RS"), [[1, 8], [8, 8], [0, 16]], 0, 0)
+        vts(R("ZP", 0, 136), R("ZP", 0, 136), g8, None, ALU.is_equal)
+        act(R("ZN"), R("ZP", 0, 136), ACT.Copy, scale=-1.0)
+        vtt(R("ZPN", 1, 136), R("ZP", 1, 136), R("ZP", 0, 135), ALU.subtract)
+        for j in range(2):
+            vts(R("RS", 512 * j, 512 * j + 512), R("RS", 512 * j, 512 * j + 512), p64, None, ALU.is_equal)
+        giota(R("RZ"), [[0, 16], [1, 8]], 0, 0)
+        vts(R("RZ"), R("RZ"), 0.0, -8192.0, ALU.is_equal, ALU.mult)
+    if CFG["ga"]:
+        for t in range(RO - 1):
+            act(R("Y4", S * t, S * t + S), R("YS", S * t, S * t + S), ACT.Copy, scale=0.25)
     vcopy(R("ST16"), R("STI"))
     vcopy(R("NL", LN, LN + Q0), R("NBI"))
     vcopy(R("NL", LO, LO + Q0), R("DLI"))
     vcopy(R("QL0", 12, 16), R("STI", 12, 16))
     vcopy(R("CLF", 0, 4), R("STI", 12, 16))
-    act(R("I4"), R("IDF"), ACT.Copy, scale=0.25)
-    if CFG["relu"]:
-        act(R("SL2"), R("SL"), ACT.Copy, scale=2.0)
-        act(R("SLN"), R("SL"), ACT.Copy, scale=-1.0)
 
-    def xrep(t):
+    for t in range(RO):
         for k in range(16):
-            o, i = R("XREP", S * 16 * t + k, S * 16 * (t + 1), 16), R("XS", S * t, S * t + S)
-            if t > 0:
-                gsel(o, i, [[0, S]], ALU.is_ge, 0, 0)
-            elif k < 11:
+            o, i = R("XREP", S * 16 * t + k, (S * t + xlanes(t)) * 16, 16), R("XS", S * t, S * t + xlanes(t))
+            nv, ns = CFG["xr%d" % t] if t < 2 else (0, 0)
+            if k >= nv + ns:
+                gsel(o, i, [[0, xlanes(t)]], ALU.is_ge, 0, 0)
+            elif k < nv:
                 vcopy(o, i)
             else:
                 act(o, i, ACT.Copy)
-
-    for t in range(RO):
-        xrep(t)
-
-    nf = [0]
-
-    def oh(a, b, p1=128):
-        return R("CM", 256 + a, 256 + b) if CFG["f2"] else R("OH", a, b)
-
-    def xr(t, l0, cnt):
-        if l0 >= S:
-            return R("GREP", (l0 - S) * 16, (l0 - S + cnt) * 16)
-        return R("XREP", (S * t + l0) * 16, (S * t + l0 + cnt) * 16)
 
     def lists(t, ph, c, o16, of, win, lst, want_f):
         if (t, ph, c) in CFG["direct"]:
@@ -378,205 +460,326 @@ def build(g, core, T, topo, rank):
             sgather(of, win, lst)
             vcopy(o16, of)
 
-    def diffs(t, ph, s, dname, pad, win, oname, s0, cnt):
-        h = cnt // 2
-        off = [u for u in range(2) if ((t, ph, s, u) in CFG["off"] and (t, ph, s // 2) not in CFG["relu"])
-               or (s0 >= S and CFG["gpe"])]
-        if not off:
-            parts = [(s0, cnt, False)]
-        else:
-            parts = [(s0 + u * h, h, u in off) for u in range(2)]
-        for a, m, by_s in parts:
-            d = R(dname, pad + a * 16, pad + (a + m) * 16)
-            if by_s:
-                nf[0] += 1
-                fb = "OH" if CFG["f2"] and nf[0] % 2 else "F0"
-                f = R(fb, 0, m * 16)
-                sgather(d, win, R(oname, a, a + m))
-                if a >= S and CFG["gpe"]:
-                    x0 = (2 - t) * XS_SLOT + 16 + a - S
-                    mms([(f, R("IB"), d, True, False)]
-                        + [(R(fb, k, m * 16, 16), R("NIB"), R("CE", x0, x0 + m), False, k == 15) for k in range(16)])
+    def diffs(t, ph, c, l0, CH, dname, pad, win, oname):
+        u0, u1 = l0 // 32, (l0 + CH) // 32
+        u = u0
+        while u < u1:
+            a = 32 * u
+            if a >= S or (t, ph, u) in CFG["off"]:
+                fb = lease("F1" if (t, ph, u) in CFG["f1"] else "F0")
+                d = R(dname, pad + a * 16, pad + (a + 32) * 16)
+                if a < S or (t, ph) not in CFG["gm"]:
+                    (vgather if (t, ph, u) in CFG["gv"] else sgather)(d, win, R(oname, a, a + 32))
+                elif a == S:
+                    sgather(R(dname, pad + S * 16, pad + LN * 16), win, R(oname, S, LN))
+                if a >= xlanes(t):
+                    x = R("CE", a - S, a - S + 32) if a >= S else R("XS", S * t + a, S * t + a + 32)
+                    mms([(R(fb), R("IB"), d, True, False)]
+                        + [(R(fb, k, 512, 16), R("NIB"), x, False, k == 15) for k in range(16)])
                 else:
-                    mms([(f, R("IB"), d, True, False), (f, R("NIB"), xr(t, a, m), False, True)])
-                act(d, f, ACT.Abs)
+                    x = R("XREP", (S * t + a) * 16, (S * t + a + 32) * 16)
+                    mms([(R(fb), R("IB"), d, True, False), (R(fb), R("NIB"), x, False, True)])
+                ops[-1]["group"] = 1
+                act(d, R(fb), ACT.Abs)
+                ops[-1]["group"] = -1
+                u += 1
+                continue
+            m = 1
+            while (m < CFG["vm"] and u + m < u1 and 32 * (u + m) < S and (t, ph, u + m) not in CFG["off"]
+                   and signed(t, ph, u + m) == signed(t, ph, u)):
+                m += 1
+            d = R(dname, pad + a * 16, pad + (a + 32 * m) * 16)
+            vgtt(d, win, R(oname, a, a + 32 * m), R("XREP", (S * t + a) * 16, (S * t + a + 32 * m) * 16), ALU.subtract)
+            if signed(t, ph, u):
+                vts(R(dname + "R", pad + a * 16, pad + (a + 32 * m) * 16), d, -2.0, 0.0, ALU.mult, ALU.max)
             else:
-                vgtt(d, win, R(oname, a, a + m), xr(t, a, m), ALU.subtract)
-                if (t, ph, s // 2) in CFG["relu"]:
-                    vts(R("DR", a * 16, (a + m) * 16), d, 0.0, None, ALU.max)
-                else:
-                    act(d, d, ACT.Abs)
+                act(d, d, ACT.Abs)
+            u += m
 
-    def keys(bank, CH, l0, idf, kc, dname, pad, relu=False):
-        full = R(bank, 0, 128, 1, 0, CH)
-        row = (full, R("ONE2", 0, CH, 1, 0, 2), R(kc, 0, 128, 1, 0, 2), False, relu)
-        mms([(full, R(idf, l0, l0 + CH), R("IDF"), True, False)] + ([] if relu else [row]))
-        for nm, sl, end in ([(dname, "SLN", False), ("DR", "SL2", True)] if relu else [(dname, "SL", True)]):
+    def runs(t, ph, l0, cnt, parts=False):
+        out = []
+        for a in range(l0, l0 + cnt, 32):
+            if signed(t, ph, a // 32):
+                if out and sum(out[-1]) == a and not (parts and out[-1][0] == l0 + 32):
+                    out[-1] = (out[-1][0], out[-1][1] + 32)
+                else:
+                    out.append((a, 32))
+        return out
+
+    def keys(t, ph, c, CH, l0, idf, kc, dname, pad):
+        bank, a = ("K%d" % c, 0) if c < 2 else ("K1", 128)
+        full = R(bank, a, a + 128, 1, 0, CH)
+        srcs = [(dname, l0, CH)] + [(dname + "R", l, cnt) for l, cnt in runs(t, ph, l0, CH, True)]
+        late = len(srcs) > 1
+        rows = [(full, R("ONE2", 0, CH, 1, 0, 2), R(kc, 0, 128, 1, 0, 2), False, late)]
+        lst = [(full, R(idf, l0, l0 + CH), R("IDF"), True, False)] + ([] if late else rows)
+        if c < 2:
+            mms(lst)
             lst = []
-            for k in range(16):
-                a = pad + l0 * 16 + k
-                lst.append((R(bank, k % 2, 128, 2, 0, CH), R(nm, a, pad + (l0 + CH) * 16, 16),
-                            R(sl, 7 - k // 2, 71 - k // 2), False, end and k == 15 and not relu))
-            mms(lst + ([row] if relu and end else []))
+        for nm, l, cnt in srcs:
+            end = (nm, l, cnt) == srcs[-1]
+            mms(lst + [(R(bank, a + k % 2, a + 128, 2, l - l0, l - l0 + cnt),
+                        R(nm, pad + l * 16 + k, pad + (l + cnt) * 16, 16),
+                        R("SL", 7 - k // 2, 71 - k // 2), False, end and not late and k == 15) for k in range(16)]
+                + (rows if end and late else []))
+        return full
+
+    def pick_lists(out, src, w):
+        mms([(out, R("ZS", 15 - l, 143 - l), R(src[0], src[1] + l, src[1] + w, 16), l == 0, l == 15) for l in range(16)])
 
     for t in range(RO):
         last = t == RO - 1
         L = LN if t in (1, 2) else S
-        CH, NB = L // 2, L // 16
-        hb, SUB = NB // 2, L // 4
+        NB = L // 16
         ql, lo = Q0 + LN * t, CN + LN * t
         CL = ["ST16", "QL0", "QL1", "QL2"][t]
         QL = "QL%d" % t
-        slot = (2 - t) * XS_SLOT
-
         O2, D2 = "O2%d" % (t % 2), "D2%d" % (t % 2)
-        if L == LN:
-            lu = "LU%d" % (t - 1)
-            sgather(R("GREP"), R("XR%d" % (t - 1)), R(lu, 8, 8 + H))
-            gsel(R("CE", slot + 16, slot + 16 + H), R("GREP", 0, H * 16, 16), [[0, H]], ALU.is_ge, 0, 0)
-            gsel(R("KK", ql + S, ql + LN), R("GREP", 0, H * 16, 16), [[0, H]], ALU.is_ge, 0, 0)
-            vcopy(R("CLF", 4, 5), R(lu, 0, 1))
-            vts(R("LVF", 12, 16), R("LANEL", 0, 4), R("CLF", 4, 5), None, ALU.is_lt)
-        nnw, llw = R("NL", LN, LN + ql), R("NL", LO, LO + ql)
-        for c in range(2):
-            l0, b0 = c * CH, c * hb
-            bank = "K%d" % c
-            lists(t, 1, c, R("O1", l0, l0 + CH), R("CANDF", l0, l0 + CH), nnw, R(CL, b0, b0 + hb), True)
-            for s in range(2):
-                diffs(t, 1, 2 * c + s, "D1", 0, R("KK", 0, ql), "O1", l0 + s * SUB, SUB)
-            keys(bank, CH, l0, "CANDF", "KC1", "D1", 0, (t, 1, c) in CFG["relu"])
-            vscan(R("MN", 128 * c, 128 * c + 128, 1, 0, CH), R("RMIN", 0, 128, 1, 0, CH), R(bank, 0, 128, 1, 0, CH),
-                  ALU.add, ALU.min)
-            vgtt(R("XP", 128 * c, 128 * c + 128), R("MN", 128 * c, 128 * c + 128), R("BL"), R("DM"), ALU.mult)
-            mms([(R("TR", b0, b0 + hb), R("XP", 128 * c, 128 * c + 128, 1, 0, CH), R("BSEL", 0, hb, 1, 0, CH), True, True)])
-            vcopy(R("K1I", b0, b0 + hb), R("TR", b0, b0 + hb))
-            vts(R("QI", b0, b0 + hb), R("K1I", b0, b0 + hb), 2047, None, ALU.bitwise_and)
-            vcopy(R(QL, b0, b0 + hb), R("QI", b0, b0 + hb))
-        for c in range(2):
-            l0, b0 = c * CH, c * hb
-            bank = "K%d" % c
-            lists(t, 2, c, R(O2, l0, l0 + CH), R("LIF", l0, l0 + CH), llw, R(QL, b0, b0 + hb), not last)
-            for s in range(2):
-                diffs(t, 2, 2 * c + s, D2, PAD, R("CE", C0, C0 + lo), O2, l0 + s * SUB, SUB)
-            if last:
-                continue
-            keys(bank, CH, l0, "LIF", "KC2", D2, PAD)
-            kb = R(bank, 0, 128, 1, 0, CH)
-            vscan(R("MN", 128 * c, 128 * c + 128, 1, 0, CH), R("RMIN", 0, 128, 1, 0, CH), kb, ALU.add, ALU.min)
-            vscan(R("MX", 128 * c, 128 * c + 128, 1, 0, CH), R("RMAX", 0, 128, 1, 0, CH), kb, ALU.add, ALU.max)
-            if CFG["merge"] and c == 0:
-                continue
-            c0, c1 = (0 if CFG["merge"] else c), c + 1
-            e8 = lambda nm: R(nm, 8 * c0, 8 * c1, 1, 0, CH)
-            vts(e8("TI"), R("MX", 128 * c0 + 15, 128 * c1, 16, 0, CH), -1.0, float(30 * 2048 + 2047), ALU.mult, ALU.add)
-            vts(e8("T2"), e8("TI"), 32767, None, ALU.bitwise_and)
-            vtt(e8("SEL"), R("MN", 128 * c0 + 15, 128 * c1, 16, 0, CH), e8("T2"), ALU.min)
-            vts(e8("RI"), e8("SEL"), 11, 15, ALU.arith_shift_right, ALU.bitwise_and)
-            for u in range(c0, c1):
-                vgtt(R("XP", 128 * u, 128 * u + 128), R("SEL", 8 * u, 8 * u + 8), R("IU", 0, 8), R("DM"), ALU.mult)
-                mms([(R("TR", 16 + u * hb, 16 + u * hb + hb), R("XP", 128 * u, 128 * u + 128, 1, 0, CH),
-                      R("BSEL", 0, hb, 1, 0, CH), True, True)])
-                vgtt(R("OHT", 128 * u, 128 * u + 128), R("RI", 8 * u, 8 * u + 8), R("IU", 0, 8), R("KPAT"), ALU.is_equal)
-                m0 = 128 * (2 * t + u)
-                mms([(oh(u * CH, u * CH + CH), R("OHT", 128 * u, 128 * u + 128, 1, 0, CH),
-                      R("MD", m0, m0 + CH, 1, 0, CH), True, True)])
         nb_ = lambda nm: R(nm, 0, NB)
         if not last:
-            vcopy(nb_("QF"), nb_("QI"))
-            sgather(R("RQF", 0, L), R("IOTA", 0, ql), nb_(QL))
-            sgather(R("SD", FD, FD + L), nnw, nb_(QL))
-            vcopy(R("RQ16", 0, L), R("RQF", 0, L))
-            for b in range(NB):
-                e = R("E", LN * b + 16 * b, LN * b + L)
-                vts(e, R("RQ16", 16 * b, L), R("QF", b, b + 1), R("WL", b, b + 1), ALU.is_equal, ALU.mult)
-            for b0 in range(0, NB, 4):
-                mms([(R("CM", 16 * b, L), R("OBD"), R("E", LN * b + 16 * b, LN * b + L), b == 0, b == NB - 1)
-                     for b in range(b0, b0 + 4)])
-            vtt(R("WM", 0, L), R("CM", 0, L), R("THR", 0, L), ALU.is_lt)
-            vscan(R("WS", 0, L), R("RSUM", 0, L), R("WM", 0, L), ALU.mult, ALU.add)
-            vtt(nb_("WINF"), R("WS", 15, L, 16), nb_("LVF"), ALU.mult)
-            vts(nb_("FK"), nb_("K1I"), 0.0, -float(LO - LN), ALU.is_ge, ALU.mult)
-            vtt(nb_("WF"), nb_("FK"), nb_("WINF"), ALU.mult)
-            vtt(nb_("QD"), nb_("QF"), nb_("LANEO"), ALU.subtract)
-            vtt(nb_("QB"), nb_("QD"), nb_("WINF"), ALU.mult)
-            vtt(nb_("QA"), nb_("QB"), nb_("LANEL"), ALU.add)
-            if CFG["nldma"]:
-                copy_dma(R("NL", LN + ql, LN + ql + L), R("SD", FD, FD + L))
+            load("y", R("CE", H, LN), "xs", S * t, S * t + S)
+        if L == LN:
+            lu = R("LU%d" % (t - 1), 0, 4)
+            sgather(R("CE", 0, H), R("XR%d" % (t - 1)), lu)
+            copy_dma(R("KK", ql + S, ql + LN), R("CE", 0, H))
+            vts(R("LVF", 12, 16), lu, float(S), None, ALU.is_lt)
+            if CFG["wsel"]:
+                vtt(R("THX", 12, 16), R("THL", 12, 16), R("LVF", 12, 16), ALU.mult)
+        nnw, llw = R("NL", LN, LN + ql), R("NL", LO, LO + ql)
+        for c, (l0, CH) in enumerate(chunks(t)):
+            b0, b1 = l0 // 16, (l0 + CH) // 16
+            old = R("NL", LN, LN + max(Q0, ql - LN))
+            if t not in CFG["m1"]:
+                lists(t, 1, c, R("O1", l0, l0 + CH), R("CANDF", l0, l0 + CH), old, R(CL, b0, b1), True)
+            elif c == 0:
+                lists(t, 1, c, R("O1", 0, L), R("CANDF", 0, L), old, nb_(CL), True)
+            diffs(t, 1, c, l0, CH, "D1", 0, R("KK", 0, ql), "O1")
+            kb = keys(t, 1, c, CH, l0, "CANDF", "KC1", "D1", 0)
+            vscan(R("MN", 128 * c, 128 * c + 128, 1, 0, CH), R("RMIN", 0, 128, 1, 0, CH), kb, ALU.add, ALU.min)
+            vgtt(R("XP", 128 * c, 128 * c + 128), R("MN", 128 * c, 128 * c + 128), R("BL"), R("DM"), ALU.mult)
+            mms([(R("TR", b0, b1), R("XP", 128 * c, 128 * c + 128, 1, 0, CH), R("BSEL", 0, b1 - b0, 1, 0, CH), True, True)])
+            vcopy(R("K1I", b0, b1), R("TR", b0, b1))
+            vts(R("QI", b0, b1), R("K1I", b0, b1), 2047, None, ALU.bitwise_and)
+            vcopy(R(QL, b0, b1), R("QI", b0, b1))
+        if not last:
+            if t in CFG["gx"]:
+                act(R("IOM", 0, L), R("IOTA", ql, ql + L), ACT.Copy, scale=R("CF", 9 + t, 10 + t))
+                vgtt(R("SD", FD, FD + L), nnw, nb_(QL), R("IOM", 0, L), ALU.max)
             else:
-                act(R("NL", LN + ql, LN + ql + L), R("SD", FD, FD + L), ACT.Copy)
+                sgather(R("SD", FD, FD + L), nnw, nb_(QL))
+            for l0, l1 in ([(0, S), (S, LN)] if t in CFG["g3"] and L == LN else [(0, L)]):
+                b0, b1 = l0 // 16, l1 // 16
+                vts(R("QF", b0, b1), R("QI", b0, b1), float(QOFF), None, ALU.add)
+                sgather(R("RQF", l0, l1), R("IOTA", 0, ql), R(QL, b0, b1))
+                vts(R("RQ16", l0, l1), R("RQF", l0, l1), float(QOFF), None, ALU.add)
+                e = lambda b: R("E", LN * b + max(16 * b, l0), LN * b + l1)
+                for b in range(b1):
+                    vts(e(b), R("RQ16", max(16 * b, l0), l1), R("QF", b, b + 1), R("WL", b, b + 1), ALU.is_equal, ALU.mult)
+                for a in range(0, b1, CFG["eg"]):
+                    mms([(R("CM", max(16 * b, l0), l1), R("OBD"), e(b), b == 0, b == b1 - 1)
+                         for b in range(a, min(b1, a + CFG["eg"]))])
+                if CFG["wsel"]:
+                    act(R("CMB", l0, l1), R("CM", l0, l1), ACT.Copy)
+                    pick_lists(R("TR", 48 + b0, 48 + b1), R("CMB", l0), l1 - l0)
+                    vtt(R("WINF", b0, b1), R("TR", 48 + b0, 48 + b1), R("THX", b0, b1), ALU.is_lt)
+                else:
+                    vtt(R("WM", l0, l1), R("CM", l0, l1), R("THR", l0, l1), ALU.is_lt)
+                    vscan(R("WS", l0, l1), R("RSUM", l0, l1), R("WM", l0, l1), ALU.mult, ALU.add)
+                    vtt(R("WINF", b0, b1), R("WS", l0 + 15, l1, 16), R("LVF", b0, b1), ALU.mult)
+            vtt(nb_("HD"), nb_("QF"), nb_("WINF"), ALU.mult)
+            vtt(nb_("HF"), nb_("HD"), nb_("K1I"), ALU.min)
+            vtt(nb_("HM"), nb_("HD"), nb_("LANEL"), ALU.max)
+            if CFG["two"]:
+                vtt(nb_("HM2"), nb_("HM"), nb_("LANEL"), ALU.add)
+            if t < 2:
+                vts(R("WTH", 0, 12), R("WINF", 0, 12), -2.0 ** 23, 2.0 ** 23, ALU.mult, ALU.add)
+            if t in CFG["dg"] + CFG["gx"]:
+                sgather(R("NL", LN + ql, LN + ql + L), nnw, nb_(QL))
+            else:
+                copy_dma(R("NL", LN + ql, LN + ql + L), R("SD", FD, FD + L))
             copy_dma(R("NL", LN + ql, LN + ql + L, 1, t, 128, 16), R("RQF", 0, L, 1, t, 128, 16))
-            copy_dma(R("SD", FD, FD + L, 1, 8 + t, 128, 16), R("IOTA", ql, ql + L, 1, 8 + t, 128, 16))
+            if t not in CFG["gx"]:
+                copy_dma(R("SD", FD, FD + L, 1, 8 + t, 128, 16), R("IOTA", ql, ql + L, 1, 8 + t, 128, 16))
+        for c, (l0, CH) in enumerate(chunks(t)):
+            b0, b1 = l0 // 16, (l0 + CH) // 16
+            lists(t, 2, c, R(O2, l0, l0 + CH), R("LIF", l0, l0 + CH), llw, R(QL, b0, b1), not last)
+            diffs(t, 2, c, l0, CH, D2, PAD, R("CE", C0, C0 + lo), O2)
+            if last:
+                continue
+            kb = keys(t, 2, c, CH, l0, "LIF", "KC2", D2, PAD)
+            m0 = 128 * c
+            vscan(R("MB", m0, m0 + 128, 1, 0, CH), R("RMC", 0, 128, 1, 0, CH), kb, ALU.max, ALU.min)
+            vscan(R("MX", m0, m0 + 128, 1, 0, CH), R("RMAX", 0, 128, 1, 0, CH), kb, ALU.add, ALU.max)
+            vgtt(R("XQ", m0, m0 + 128), R("MB", m0, m0 + 128), R("BL"), R("DM"), ALU.mult)
+            mms([(R("TR", 16 + b0, 16 + b1), R("XQ", m0, m0 + 128, 1, 0, CH), R("BSEL", 0, b1 - b0, 1, 0, CH), True, True)])
+            if CFG["xq"] and c < len(chunks(t)) - 1:
+                continue
+            c0, c1 = (0 if CFG["xq"] else c), c + 1
+            np_ = chunks(t)[c0][1]
+            e8 = lambda nm: R(nm, 8 * c0, 8 * c1, 1, 0, np_)
+            vts(e8("TI"), R("MX", 128 * c0 + 15, 128 * c1, 16, 0, np_), -1.0, float(30 * 2048 + 2047), ALU.mult, ALU.add)
+            vts(e8("T2"), e8("TI"), 32767, None, ALU.bitwise_and)
+            vtt(e8("SEL"), R("MB", 128 * c0 + 15, 128 * c1, 16, 0, np_), e8("T2"), ALU.min)
+            vts(e8("RI"), e8("SEL"), 11, 15, ALU.arith_shift_right, ALU.bitwise_and)
+            ohm = CFG["ohm"] and c1 - c0 == 2
+            if ohm:
+                vgtt(R("OHT", 0, 256), R("RI", 0, 16), R("IU"), R("KPAT", 0, 256), ALU.is_equal)
+            for u in range(c0, c1):
+                a, cnt = chunks(t)[u]
+                if not ohm:
+                    vgtt(R("OHT", 128 * u, 128 * u + 128), R("RI", 8 * u, 8 * u + 8), R("IU", 0, 8), R("KPAT", 0, 128),
+                         ALU.is_equal)
+                oh, oht = R("TR", 256 + a, 256 + a + cnt), R("OHT", 128 * u, 128 * u + 128, 1, 0, cnt)
+                mms([(oh, oht, R("MD", md[a], md[a] + cnt, 1, 0, cnt), True, False),
+                     (oh, oht, R("MT", 128 * t, 128 * t + cnt, 1, 0, cnt), False, True)])
+        if not last:
             if t == 1:
-                vtt(R("PU1", 0, 4), R("QF", 12, 16), R("CLF", 0, 4), ALU.subtract)
+                vtt(R("PU1", 0, 4), R("QI", 12, 16), R("CLF", 0, 4), ALU.subtract)
                 vtt(R("PU2", 0, 4), R("PU1", 0, 4), R("LVF", 12, 16), ALU.mult)
                 vtt(R("PU3", 0, 4), R("PU2", 0, 4), R("CLF", 0, 4), ALU.add)
                 vcopy(R(QL, 12, 16), R("PU3", 0, 4))
             sel = R("TR", 16, 16 + NB)
-            vts(nb_("NV"), sel, 0.0, None, ALU.is_ge)
-            vcopy(nb_("SI"), sel)
-            vtt(nb_("MM"), nb_("NV"), nb_("WF"), ALU.mult)
-            vtt(nb_("TB1"), nb_("LANE4"), nb_("MM"), ALU.subtract)
-            vts(nb_("TB16"), nb_("TB1"), 0.25, None, ALU.mult)
-            vtt(R("SD", 0, L), oh(0, L), R("LIF", 0, L), ALU.max)
-            sgather(R("DAT", 0, L), R("SD", 0, FD + L), nb_("TB16"))
-            vtt(nb_("TA1"), nb_("QA"), nb_("MM"), ALU.add)
-            vcopy(nb_("TA16"), nb_("TA1"))
-            vscat(R("NL", 0, LO + ql), nb_("TA16"), R("DAT", 0, L))
+            vtt(nb_("YY"), sel, nb_("HF"), ALU.min)
+            if CFG["two"]:
+                vtt(nb_("TA1"), nb_("YY"), nb_("LANEL"), ALU.max)
+                vcopy(nb_("TA16"), nb_("TA1"))
+                vscat(R("NL", 0, LN + ql), nb_("TA16"), R("SD", FD, FD + L))
+                vtt(nb_("TB1"), nb_("HM2"), nb_("TA1"), ALU.subtract)
+                vcopy(nb_("TB16"), nb_("TB1"))
+                vtt(R("SD", 0, L), R("TR", 256, 256 + L), R("LIF", 0, L), ALU.max)
+                vscat(R("NL", LO - LN, LO + ql), nb_("TB16"), R("SD", 0, L))
+            else:
+                vts(nb_("FF"), nb_("YY"), 0.0, float(LO - LN), ALU.is_gt, ALU.mult)
+                vtt(nb_("TB1"), nb_("LANE4"), nb_("FF"), ALU.add)
+                vts(nb_("TB16"), nb_("TB1"), 0.25, None, ALU.mult)
+                vtt(R("SD", 0, L), R("TR", 256, 256 + L), R("LIF", 0, L), ALU.max)
+                sgather(R("DAT", 0, L), R("SD", 0, FD + L), nb_("TB16"))
+                vtt(nb_("TA1"), nb_("HM"), nb_("FF"), ALU.subtract)
+                vcopy(nb_("TA16"), nb_("TA1"))
+                vscat(R("NL", 0, LO + ql), nb_("TA16"), R("DAT", 0, L))
             copy_dma(R("NL", LO + ql, LO + ql + L), R("SD", 0, L))
             if t < 2:
-                sx, gp, gl = "SX%d" % t, R("GP0", 0, 12), R("GL%d" % t, 0, 4)
-                vtt(R("NW", 0, 12), R("NV", 0, 12), R("WINF", 0, 12), ALU.mult)
-                vscan(R("CUM", 1, 13), R("ONES", 0, 12), R("NW", 0, 12), ALU.mult, ALU.add)
-                mms([(R("TR", 32, 45), R("TRI"), R("NW", 0, 13), True, False),
-                     (R("TR", 32, 45), R("TRB"), R("NW", 0, 13), False, False),
-                     (R("TR", 32, 45), R("OBD"), R("CUM", 0, 13), False, True)])
+                sx, gp, g0 = R("SX%d" % t, 0, 4), R("GP0", 0, 12), t * (GW + 64)
+                vtt(R("NW", 0, 12), R("TR", 16, 28), R("WTH", 0, 12), ALU.is_gt)
+                vscan(R("CUM", 1, 12), R("ONE2", 0, 11), R("NW", 0, 11), ALU.mult, ALU.add)
+                mms([(R("TR", 32, 44), R("TRI"), R("NW", 0, 12), True, False),
+                     (R("TR", 32, 44), R("TRB"), R("NW", 0, 12), False, False),
+                     (R("TR", 32, 44), R("OBD"), R("CUM", 0, 12), False, True)])
                 vtt(R("GP", 0, 12), R("TR", 32, 44), R("LG", 0, 12), ALU.min)
-                vcopy(R("GI", 0, 1), R("TR", 44, 45))
                 vts(gp, R("GP", 0, 12), 1024.0, None, ALU.add)
-                vscat(R("GI", 8, 8 + LN + S), gp, R("IOTA", 0, S))
-                vcopy(R(sx), R("GI", 0, 8 + H))
-                send(t, "x", R(sx))
-                vtt(R("GD"), R("GI", 8, 8 + H), R("DM", 0, H), ALU.mult)
-                vscan(R("GS"), R("RSUM", 0, H), R("GD"), ALU.mult, ALU.add)
-                vcopy(gl, R("GS", 15, H, 16))
-            vts(nb_("CI"), nb_("SI"), 2047, None, ALU.bitwise_and)
-            vts(nb_("U2"), nb_("NV"), -8192.0, float((t + 1) * XS_SLOT), ALU.mult, ALU.add)
-            vtt(nb_("U3"), nb_("U2"), nb_("CI"), ALU.add)
-            vtt(nb_("U4"), nb_("U3"), nb_("LANEX"), ALU.max)
-            vcopy(nb_("CN16"), nb_("U4"))
-            sgather(R("CE", C0 + lo, C0 + lo + L), R("CE", slot, C0 + lo), nb_("CN16"))
-            sgather(R("GG"), R("AC", slot, C0 + lo), R("CN16", 0, 12))
+                vscat(R("GI", g0, g0 + GW), gp, R("IOTA", 0, S))
+                pick_lists(R("TR", 44, 48), R("GI", g0), H)
+                vcopy(sx, R("TR", 44, 48))
+                send(t, "x", sx)
+            vcopy(nb_("SI"), sel)
+            vts(nb_("CI"), nb_("SI"), 2 ** 23 + 2047, None, ALU.bitwise_and)
+            vtt(nb_("U4"), nb_("CI"), nb_("LX"), ALU.max)
+            vts(nb_("CN16"), nb_("U4"), float(C0 - 2 ** 23), None, ALU.add)
+            sgather(R("CE", C0 + lo, C0 + lo + L), R("CE", 0, C0 + lo), nb_("CN16"))
+            if CFG["pe4"] or not CFG["ga"]:
+                sgather(R("GG"), R("AC", 0, C0 + lo), R("CN16", 0, 12))
         rr = "RR%d" % (t % 2)
-        for j in range(6):
-            (vgather if (t, j) in CFG["agv"] else sgather)(R("AG", 512 * j, 512 * j + 512), R("AC", C0, C0 + lo),
-                                                           R(O2, 32 * j, 32 * j + 32))
+        quarter = not last and not CFG["pe4"]
+        j = 0
+        while j < 6:
+            m = 1
+            while m < CFG["agm"] and (j + m) % 3 and ((t, j) in CFG["agv"]) == ((t, j + m) in CFG["agv"]):
+                m += 1
+            (vgather if (t, j) in CFG["agv"] else sgather)(R("AG", 512 * j, 512 * (j + m)), R("AC", C0, C0 + lo),
+                                                           R(O2, 32 * j, 32 * (j + m)))
+            j += m
+        both = (t, 0) in CFG["cx"] and (t, 1) in CFG["cx"] and t not in CFG["split"]
+        lst, fb = [], lease("F1")
+        for h in range(2):
+            if (t, h) not in CFG["cx"]:
+                continue
+            srcs = [(D2, HL * h, HL)] + [(D2 + "R", l, cnt) for l, cnt in runs(t, 2, HL * h, HL)]
+            for u, rows in enumerate(DIFF_ROWS):
+                grp = [(R(fb, 2 * l + u, 2 * (l + cnt), 2), R(z, 7 - r, 135 - r),
+                        R(nm, PAD + l * 16 + k, PAD + (l + cnt) * 16, 16)) for nm, l, cnt in srcs for k, z, r in rows]
+                if u == 0:
+                    grp.append((grp[0][0], R("RZ", 0, 128, 1, 0, 1), R("ONE2", 0, HL, 1, 0, 1)))
+                lst += [m + (i == 0, i == len(grp) - 1) for i, m in enumerate(grp)]
+            if both and h == 0:
+                continue
+            a, b = (0 if both else S * h), S * h + S
+            for i in range(0, len(lst), CFG["dfm"]):
+                mms(lst[i:i + CFG["dfm"]])
+                ops[-1].update(group=int(i == 0), starts=i == 0, wr=[R(fb, a, b)])
+                if i == 0:
+                    ops[-1]["rd"] = ops[-1]["rd"] + [m[2] for m in lst]
+            act(R("RH", a, b), R(fb, a, b), ACT.Exp, scale=1.0 / 64)
+            act(R(fb, a, b, 1, 64), R(fb, a, b, 1, 64), ACT.Exp, scale=1.0 / 64)
+            vtt(R("RH", a, b, 1, 64), R(fb, a, b, 1, 64), R("RH", a, b, 1, 64), ALU.subtract)
+            ops[-1]["group"] = -1
+            lst, fb = [], lease("F1")
         for j in range(6):
             bank = "R%d" % (j % 2)
-            a = PAD + 512 * j
-            mms([(R(bank), R("OBD"), R(D2, a, a + 512), True, False),
-                 (R(bank, 0, 512, 16), R("ONE2", 0, 128, 1, 0, 2), R("RB", 0, 32, 1, 0, 2), False, False),
-                 (R(bank), R("NBD"), R(D2, a - 1, a + 511), False, True)])
-            act(R(rr, 512 * j, 512 * j + 512), R(bank), ACT.Exp, scale=1.0 / 64)
-            vscan(R("SC", 512 * j, 512 * j + 512), R(rr, 512 * j, 512 * j + 512), R("AG", 512 * j, 512 * j + 512),
-                  ALU.mult, ALU.add)
-        wb = R("TR", 64, 64 + S) if CFG["f2"] else R("CM", 256, 256 + S)
-        mms([(wb, R("OBD"), R(D2, PAD + 15, PAD + S * 16, 16), True, True)])
-        yo = R("YO", S * t, S * t + S)
-        if last:
-            act(wb, wb, ACT.Exp, scale=-1.0 / 64)
-            vtt(yo, R("SC", 15, 3072, 16), wb, ALU.mult)
-        else:
-            act(wb, wb, ACT.Exp, bias=R("MCOL", 6, 7), scale=-1.0 / 64)
-            vtt(R("P4"), R("SC", 15, 3072, 16), wb, ALU.mult)
-            xb = R("TR" if CFG["f2"] else "OH", 256, 256 + S)
-            mms([(xb, R("I4"), R("YS", S * t, S * t + S), True, False), (xb, R("IDF"), R("GG"), False, True)])
-            vtt(R("AC", C0 + lo, C0 + lo + S), xb, R("P4"), ALU.subtract)
-            act(yo, R("P4"), ACT.Copy, scale=4.0)
-            if t < 2:
-                sgather(R("SA%d" % t), R("AC", C0 + lo, C0 + lo + S), R("GL%d" % t, 0, 4))
-                send(t, "a", R("SA%d" % t))
-        dma("y", (lambda tt=t: T.yp[:, S * tt:S * tt + S]), (lambda i=yo: A(i)), [yo], [])
+            h, a = j // 3, PAD + 512 * j
+            cols = lambda nm: R(nm, 512 * j, 512 * j + 512)
+            if (t, h) in CFG["cx"]:
+                mms([(R(bank, r, 512, 8), R("RS", 128 * r, 128 * r + 128), R("RH", 64 * j, 64 * j + 64), True, True)
+                     for r in range(8)])
+                vscan(cols("SC"), R(bank), cols("AG"), ALU.mult, ALU.add)
+            else:
+                lst = []
+                for nm in [D2] + ([D2 + "R"] if signed(t, 2, j) else []):
+                    lst += [(R(bank), R("OBD"), R(nm, a, a + 512), nm == D2, False),
+                            (R(bank, 1), R("NBD"), R(nm, a, a + 511), False, False)]
+                mms(lst + [(R(bank, 0, 512, 16), R("ONE2", 0, 128, 1, 0, 2), R("RB", 0, 32, 1, 0, 2), False, True)])
+                act(cols(rr), R(bank), ACT.Exp, scale=1.0 / 64)
+                vscan(cols("SC"), cols(rr), cols("AG"), ALU.mult, ALU.add)
+        for a, b in ([(0, HL), (HL, S)] if t in CFG["split"] else [(0, S)]):
+            wb, last_row = R("TR", 64 + a, 64 + b), R("SC", 16 * a + 15, 16 * b, 16)
+            srcs = [(D2, a, b - a)] + [(D2 + "R", l, cnt) for l, cnt in runs(t, 2, a, b - a)]
+            mms([(R("TR", 64 + l, 64 + l + cnt), R("OBD"), R(nm, PAD + 15 + l * 16, PAD + (l + cnt) * 16, 16),
+                  i == 0, i == len(srcs) - 1) for i, (nm, l, cnt) in enumerate(srcs)])
+            act(wb, wb, ACT.Exp, bias=R("MCOL", 1, 2) if quarter else 0.0, scale=-1.0 / 64)
+            yo, xb = R("YO", S * t + a, S * t + b), R("CM", 256 + a, 256 + b)
+            ys, gg, an = R("YS", S * t + a, S * t + b), R("GG", a, b), R("AC", C0 + lo + a, C0 + lo + b)
+            if quarter and CFG["ga"]:
+                vtt(wb, last_row, wb, ALU.mult)
+                vtt(R("P4", a, b), R("Y4", S * t + a, S * t + b), wb, ALU.subtract)
+                act(yo, wb, ACT.Copy, scale=4.0)
+                vgtt(an, R("AC", 0, C0 + lo), R("CN16", a // 16, b // 16), R("P4", a, b), ALU.add)
+            elif quarter:
+                vtt(R("P4", a, b), last_row, wb, ALU.mult)
+                mms([(xb, R("I4"), ys, True, False), (xb, R("IDF"), gg, False, True)])
+                vtt(an, xb, R("P4", a, b), ALU.subtract)
+                act(yo, R("P4", a, b), ACT.Copy, scale=4.0)
+            else:
+                vtt(yo, last_row, wb, ALU.mult)
+                if not last:
+                    mms([(xb, R("I4"), ys, True, False), (xb, R("IDF"), gg, False, False), (xb, R("I4F"), yo, False, True)])
+                    act(an, xb, ACT.Copy)
+            dma("y", (lambda r=yo: T.yp[:, r[1]:r[2]]), (lambda i=yo: A(i)), [yo], [])
+        if t < 2:
+            sgather(R("SA%d" % t), R("AC", C0 + lo, C0 + lo + S + 8), R("SX%d" % t, 0, 4))
+            send(t, "a", R("SA%d" % t))
     return ops, neng
+
+
+def price(ops, c):
+    out = []
+    for o in ops:
+        w = o["work"]
+        if w[0] == "plain":
+            out.append((c["ov"] + max(64, w[1]) * CYC * c["f"], 0.0))
+        elif w[0] == "gather":
+            out.append(((50 if o["eng"] == "v" else 65) + w[1] * c["gc"] * CYC, 0.0))
+        elif w[0] == "scatter":
+            out.append((50 + w[1] * c["sc"] * CYC, 0.0))
+        elif w[0] == "tensor":
+            out.append((w[1] * c["pe"], 40.0))
+        elif w[0] == "pool":
+            out.append((w[1] * c["f"], 0.0))
+        elif w[0] == "dma":
+            out.append((w[1], c["dl"] + w[2]))
+        elif w[0] == "send":
+            out.append((w[1], 0.0))
+        else:
+            out.append((0.0, c["rl"] * w[1]))
+    return out
 
 
 def dependences(ops):
@@ -585,61 +788,304 @@ def dependences(ops):
         deps = {}
         acc = [(r, False) for r in o["rd"]] + [(r, True) for r in o["wr"]]
         for r, w in acc:
-            psum = r[0] in _PS
             for (j, r2, w2) in hist.get(r[0], []):
-                if j == i or not overlap(r, r2):
-                    continue
-                if psum:
-                    same = ops[j]["eng"] == o["eng"]
-                    if same and not (w or w2):
-                        continue
-                    deps[j] = deps.get(j, False) or not (same and (o["eng"] == "t" or (w and CFG["lean"])))
-                elif w or w2:
-                    inorder = (w and CFG["lean"] and ops[j]["eng"] == o["eng"] and o["kind"] == "c"
-                               and ops[j]["kind"] == "c")
+                if j != i and (w or w2) and overlap(r, r2):
+                    inorder = w and ops[j]["eng"] == o["eng"] == "t"
                     deps[j] = deps.get(j, False) or not inorder
         for r, w in acc:
             lst = hist.setdefault(r[0], [])
-            if w and r[3] == 1 and r[4] == 0 and r[5] == 128 and r[6] == 1 and r[0] not in _PS:
+            if w and r[3] == 1 and r[4] == 0 and r[5] == 128 and r[6] == 1 and not psum(r):
                 lst[:] = [e for e in lst if not (r[1] <= e[1][1] and e[1][2] <= r[2])]
-            if w and r[0] in _PS and any(ops[e[0]]["eng"] != o["eng"] for e in lst):
-                lst[:] = []
             lst.append((i, r, w))
-        o["deps"] = deps
-    for i, o in enumerate(ops):
         if o["kind"] == "arr":
-            snd = [j for j in range(i) if ops[j]["kind"] == "send"][-1]
-            o["after"] = snd
+            deps[o["x"][2]] = False
+        o["deps"] = deps
 
 
-def one_pass(ops, preds, succ, pri, back):
+def one_pass(ops, cost, preds, succ, pri, back):
     n = len(ops)
-    sem, look = CFG["sem"], CFG["look"]
+    sem, look = CFG["cost"]["sem"], CFG["look"]
     left = [len(p) for p in preds]
-    rdy = [ops[i]["lat"] if back else 0.0 for i in range(n)]
+    rdy = [cost[i][1] if back else 0.0 for i in range(n)]
     start, fin = [0.0] * n, [0.0] * n
-    free = {}
+    free, used, opened = {}, {b: {} for b in _PS}, set()
     ready = [i for i in range(n) if left[i] == 0]
     order = []
     while ready:
-        est = {i: max(rdy[i], free.get(ops[i]["eng"], 0.0)) if ops[i]["eng"] else rdy[i] for i in ready}
-        first = min(ready, key=lambda i: (est[i], -pri[i]))
+        est = {}
+        for i in ready:
+            o = ops[i]
+            if back or not (o["starts"] and o["banks"][0] in opened):
+                est[i] = max([rdy[i], free.get(o["eng"], 0.0)]
+                             + [x + sem for b in o["banks"] for e, x in used[b].items() if e != o["eng"]])
+        first = min(est, key=lambda i: (est[i] + look * cost[i][0], -pri[i]))
         e = ops[first]["eng"]
-        pick = max([i for i in ready if ops[i]["eng"] == e and est[i] <= est[first] + look], key=lambda i: (pri[i], -i))
+        pick = max([i for i in est if ops[i]["eng"] == e and est[i] <= est[first] + look * cost[first][0]],
+                   key=lambda i: (pri[i], -i))
         ready.remove(pick)
         order.append(pick)
-        end = est[pick] + ops[pick]["cost"]
+        end = est[pick] + cost[pick][0]
         if e:
             free[e] = end
         start[pick] = est[pick]
-        fin[pick] = end + (0.0 if back else ops[pick]["lat"])
+        fin[pick] = end + (0.0 if back else cost[pick][1])
+        for b in ops[pick]["banks"]:
+            used[b][e] = fin[pick]
+        if ops[pick]["group"] > 0:
+            opened.add(ops[pick]["banks"][0])
+        elif ops[pick]["group"] < 0:
+            opened.discard(ops[pick]["banks"][0])
         for k in succ[pick]:
             hard = ops[pick]["deps"].get(k, True) if back else ops[k]["deps"].get(pick, True)
-            rdy[k] = max(rdy[k], fin[pick] + (sem if hard else 0.0) + (ops[k]["lat"] if back else 0.0))
+            rdy[k] = max(rdy[k], fin[pick] + (sem if hard else 0.0) + (cost[k][1] if back else 0.0))
             left[k] -= 1
             if left[k] == 0:
                 ready.append(k)
     return order, start, fin
+
+
+def marks(order, eng, banks, n):
+    last, used, out = [n] * 6, [[n] * 3 for _ in _PS], []
+    for p, i in enumerate(order):
+        if p % 32 == 0:
+            out.append((last[:], [row[:] for row in used]))
+        last[eng[i]] = i
+        for b in banks[i]:
+            used[b][eng[i]] = i
+    return out
+
+
+def replay(order, eng, banks, fig, mark, p0=0, old=None, p1=0, limit=1e30):
+    cost, lat, deps, sem, sinks, tail = fig
+    n = len(order)
+    end, why = (old[3][:], old[2][:]) if old else ([0.0] * (n + 1), [n] * n)
+    last, used = mark[p0 // 32][0][:], [row[:] for row in mark[p0 // 32][1]]
+    left = p1 - p0 + p0 % 32 + 80 if old else n
+    for i in order[p0 - p0 % 32:]:
+        left -= 1
+        if left < 0:
+            break
+        e = eng[i]
+        w = last[e] if e < 5 else n
+        r = end[w]
+        for j, x in deps[i]:
+            x += end[j]
+            if x > r:
+                r, w = x, j
+        for b in banks[i]:
+            row = used[b]
+            for e2 in (0, 1, 2):
+                j = row[e2]
+                if e2 != e and j < n and end[j] + lat[j] + sem > r:
+                    r, w = end[j] + lat[j] + sem, j
+            row[e] = i
+        r += cost[i]
+        if r != end[i]:
+            if r + tail[i] > limit:
+                return None
+            end[i] = r
+            if left < 80:
+                left = 80
+        last[e] = i
+        why[i] = w
+    top = max(sinks, key=lambda i: end[i] + lat[i])
+    return end[top] + lat[top], top, why, end
+
+
+def nested(ops, order):
+    opened = set()
+    for i in order:
+        o = ops[i]
+        if o["starts"] and o["banks"][0] in opened:
+            return False
+        if o["group"] > 0:
+            opened.add(o["banks"][0])
+        elif o["group"] < 0:
+            opened.discard(o["banks"][0])
+    return True
+
+
+def shift(order, preds, a, b, forward):
+    pa, pb = order.index(a), order.index(b)
+    seg = order[pa:pb + 1]
+    if forward:
+        moved = {a}
+        for k in seg[1:]:
+            if preds[k] & moved:
+                moved.add(k)
+        if b in moved:
+            return None
+        return order[:pa] + [k for k in seg if k not in moved] + [k for k in seg if k in moved] + order[pb + 1:]
+    moved, need = {b}, set(preds[b])
+    for k in reversed(seg[:-1]):
+        if k in need:
+            moved.add(k)
+            need |= preds[k]
+    if a in moved:
+        return None
+    return order[:pa] + [k for k in seg if k in moved] + [k for k in seg if k not in moved] + order[pb + 1:]
+
+
+def tabu(ops, order, eng, banks, preds, fig, draw):
+    cost, lat, deps, sem = fig[:4]
+    n = len(ops)
+    best, kept, banned = None, order, {}
+    for it in range(CFG["tabu"]):
+        total, top, why, end = replay(order, eng, banks, fig, marks(order[:1], eng, banks, n))
+        if best is None or total < best:
+            best, kept = total, order
+        ready, tail, rest = [0.0] * n, [0.0] * (n + 1), lat[:]
+        before, after, last, used = [n] * n, [n] * n, [n] * 6, [[n] * 3 for _ in _PS]
+        links = []
+        for i in order:
+            e, ins = eng[i], deps[i]
+            for b in banks[i]:
+                ins = ins + [(j, lat[j] + sem) for e2, j in enumerate(used[b]) if e2 != e and j < n]
+                used[b][e] = i
+            links.append(ins)
+            ready[i] = max([end[j] + x for j, x in ins] + [0.0])
+            if e < 5:
+                before[i] = last[e]
+                if last[e] < n:
+                    after[last[e]] = i
+                last[e] = i
+        for i, ins in zip(reversed(order), reversed(links)):
+            tail[i] = cost[i] + max(rest[i], tail[after[i]])
+            for j, x in ins:
+                if x + tail[i] > rest[j]:
+                    rest[j] = x + tail[i]
+        runs, i = [[top]], top
+        while why[i] < n:
+            if why[i] == before[i]:
+                runs[-1].append(why[i])
+            else:
+                if why[i] not in preds[i]:
+                    runs.append([i, why[i]])
+                runs.append([why[i]])
+            i = why[i]
+        moves = []
+        for run in runs:
+            run.reverse()
+            m = len(run)
+            if m == 2 and eng[run[0]] != eng[run[1]]:
+                moves += [(total * (0.99 + 0.02 * draw(100) / 100), run[0], run[1], f) for f in (True, False)]
+                continue
+            for _ in range(min(m * (m - 1) // 2, CFG["tries"])):
+                x = draw(m - 1)
+                y = x + 1 + draw(min(m - 1 - x, CFG["reach"]))
+                for forward in (True, False):
+                    seq = run[x + 1:y + 1] + [run[x]] if forward else [run[y]] + run[x:y]
+                    r, heads = end[before[run[x]]], []
+                    for k in seq:
+                        r = max(r, ready[k])
+                        heads.append(r)
+                        r += cost[k]
+                    q, est = tail[after[run[y]]], 0.0
+                    for k, h in zip(reversed(seq), reversed(heads)):
+                        q = cost[k] + max(q, rest[k])
+                        est = max(est, h + q)
+                    moves.append((est + draw(50), run[x], run[y], forward))
+        moves.sort()
+        for est, a, b, forward in moves:
+            if banned.get((b, a), -1) >= it and est >= best:
+                continue
+            new = shift(order, preds, a, b, forward)
+            if new and nested(ops, new):
+                order = new
+                banned[a, b] = banned[b, a] = it + 8 + draw(12)
+                break
+        else:
+            break
+    return kept
+
+
+def improve(ops, order):
+    n = len(ops)
+    eng = ["vstgy".index(o["eng"]) if o["eng"] else 5 for o in ops]
+    banks = [[_PS.index(b) for b in o["banks"]] for o in ops]
+    preds, above = [], []
+    for o in ops:
+        far = 0
+        for j in o["deps"]:
+            far |= above[j]
+        preds.append(set(j for j in o["deps"] if not far >> j & 1))
+        above.append(far | sum(1 << j for j in preds[-1]))
+    special = set(i for i in range(n) if ops[i]["starts"] or ops[i]["group"])
+    figs = []
+    for c in CFG["figs"]:
+        cost = price(ops, c)
+        deps = [[(j, cost[j][1] + (c["sem"] if ops[i]["deps"][j] else 0.0)) for j in sorted(preds[i])] for i in range(n)]
+        tail = [x[1] for x in cost]
+        for i in range(n - 1, -1, -1):
+            for j, y in deps[i]:
+                tail[j] = max(tail[j], y + cost[i][0] + tail[i])
+        figs.append(([x[0] for x in cost], [x[1] for x in cost], deps, c["sem"],
+                     sorted(set(range(n)) - set().union(*preds)), tail))
+    x = [CFG["seed"]]
+
+    def draw(m):
+        x[0] = (x[0] * 1103515245 + 12345) % 2147483648
+        return (x[0] >> 8) % m
+
+    def waits(y):
+        i, why, out = y[1], y[2], []
+        while why[i] < n:
+            if why[i] not in preds[i]:
+                out.append((why[i], i))
+            i = why[i]
+        return out
+
+    mark = marks(order, eng, banks, n)
+    res = [replay(order, eng, banks, f, mark) for f in figs]
+    scale = [1.0 / y[0] for y in res]
+    cur = best = float(len(res))
+    kept, edges = order, sum(map(waits, res), [])
+    for it in range(CFG["moves"]):
+        if not edges:
+            break
+        a, b = edges[draw(len(edges))]
+        pa, pb = order.index(a), order.index(b)
+        kind = draw(3)
+        if kind:
+            if kind == 2:
+                b, pb, pa = a, pa, max(0, pa - 1 - draw(CFG["reach"]))
+            else:
+                pa = max(0, pa - (draw(12) if draw(3) == 0 else 0))
+            moved, need = {b}, set(preds[b])
+            for k in reversed(order[pa:pb]):
+                if k in need:
+                    moved.add(k)
+                    need |= preds[k]
+            if a in moved and kind == 1:
+                continue
+            seg = order[pa:pb + 1]
+            new = order[:pa] + [k for k in seg if k in moved] + [k for k in seg if k not in moved] + order[pb + 1:]
+        else:
+            pb = min(n - 1, pb + (draw(CFG["reach"]) if draw(2) else 0))
+            seg, moved = order[pa:pb + 1], {a}
+            for k in seg[1:]:
+                if preds[k] & moved:
+                    moved.add(k)
+            if b in moved:
+                continue
+            new = order[:pa] + [k for k in seg if k not in moved] + [k for k in seg if k in moved] + order[pb + 1:]
+        if moved & special and not nested(ops, [k for k in new if k in special]):
+            continue
+        allow = CFG["slack"] * draw(1000) / 1000.0 * (1.0 - it / CFG["moves"])
+        rs, s = [], cur
+        for f, y, z in zip(figs, res, scale):
+            rs.append(replay(new, eng, banks, f, mark, pa, y, pb, y[0] + (allow + 0.002) / z))
+            if rs[-1] is None:
+                break
+            s += (rs[-1][0] - y[0]) * z
+        if s < cur + allow and rs[-1]:
+            res = [replay(new, eng, banks, f, mark, pa, y, n) for f, y in zip(figs, rs)]
+            cur = s = sum(y[0] * z for y, z in zip(res, scale))
+            order, edges = new, sum(map(waits, res), [])
+            mark = marks(order, eng, banks, n)
+            if s < best:
+                best, kept = s, new
+    return kept, replay(kept, eng, banks, figs[0], mark)[3]
 
 
 PLAN = {}
@@ -648,27 +1094,37 @@ PLAN = {}
 def schedule(ops):
     n = len(ops)
     if n not in PLAN:
-        preds = [list(o["deps"]) + ([o["after"]] if o["kind"] == "arr" else []) for o in ops]
+        cost = price(ops, CFG["cost"])
+        preds = [list(o["deps"]) for o in ops]
         succ = [[] for _ in ops]
         for i in range(n):
             for j in preds[i]:
                 succ[j].append(i)
         pri = [0.0] * n
         for i in range(n - 1, -1, -1):
-            pri[i] = ops[i]["cost"] + ops[i]["lat"] + CFG["sem"] + max([pri[k] for k in succ[i]] + [0.0])
+            pri[i] = sum(cost[i]) + CFG["cost"]["sem"] + max([pri[k] for k in succ[i]] + [0.0])
         best = None
         for it in range(CFG["iters"]):
-            order, start, fin = one_pass(ops, preds, succ, pri, False)
+            order, start, fin = one_pass(ops, cost, preds, succ, pri, False)
             if best is None or max(fin) < best[0]:
                 best = (max(fin), order, start)
-            pri = one_pass(ops, succ, preds, fin, True)[2]
+            if max(fin) < best[0] * (1 + CFG["back"]):
+                base = fin
+            pri = one_pass(ops, cost, succ, preds, base, True)[2]
             x = CFG["seed"] * 7919 + it
             for i in range(n):
                 x = (x * 1103515245 + 12345) % 2147483648
                 pri[i] += CFG["noise"] * x / 2147483648
-        PLAN[n] = best
-    for i in range(n):
-        ops[i]["t0"] = PLAN[n][2][i]
+        PLAN[n] = (best[0],) + improve(ops, best[1])
+    seen = {b: {} for b in _PS}
+    for i in PLAN[n][1]:
+        o = ops[i]
+        o["t0"] = PLAN[n][2][i]
+        for b in o["banks"]:
+            for e, j in seen[b].items():
+                if e != o["eng"]:
+                    o["deps"][j] = True
+            seen[b][o["eng"]] = i
     return PLAN[n][1]
 
 

@@ -1,50 +1,69 @@
-import math
 from concourse.mybir import AluOpType as ALU, ActivationFunctionType as ACT
 
 CN, Q0, S, H, RO, EPS, RHO = 1280, 384, 192, 64, 4, 44, 60
 LN = S + H
+NEW = [0, S, S + LN, S + 2 * LN]
 C0 = LN
-CT = CN + 3 * LN
-QT = Q0 + 3 * LN
-PAD = 0
+CT, QT = CN + NEW[3], Q0 + NEW[3]
 LO = 2 * LN + QT
-FD = (LO - LN) // 4
-B1 = RHO * 65536 + 32768
+X0 = 128
+B1 = (RHO + 1) * 65536
 B2 = EPS * 65536 + 32768
+MAGIC = 1.5 * 2.0 ** 35
 LNR = 0.668
-GW = H + LN + S - 64
-HL = S // 2
-F, BF, I32, U16 = "float32", "bfloat16", "int32", "uint16"
+GW = LN + S
+F, BF, I32, U16, HF = "float32", "bfloat16", "int32", "uint16", "float16"
+
+CFG = {
+    "off": [(0, 1, 1), (0, 2, 1), (0, 2, 2), (1, 1, 0), (1, 1, 4), (1, 2, 0), (2, 1, 0), (2, 1, 4), (2, 2, 0),
+            (2, 2, 4), (3, 1, 0), (3, 1, 4)],
+    "f1": [(0, 2, 2), (1, 1, 4), (2, 1, 4), (2, 2, 4), (3, 1, 4), (1, 1, 7), (1, 2, 7), (2, 1, 7), (2, 2, 7)],
+    "gm": [(t, p, 6) for t in (1, 2) for p in (1, 2)],
+    "vm": [],
+    "agv": [(3, 0), (3, 1)],
+    "agm": [2, 2, 2, 1],
+    "pieces": [[(0, 128, "r"), (128, 64, "r")]] * 3 + [[(0, 96, "s"), (96, 96, "s")]],
+    "cut": [128, 128, 128, 96],
+    "g3": [],
+    "gw": [[0], [0, 1], [0, 1]], "gf": [[0, 1]] * 3, "ge": [[0]] * 3, "gc": [[0]] * 3,
+    "sa": ["AC", "KC1", "KC2", "RMAX", "RMC", "LX", "LG", "CF"],
+    "ga": [],
+    "rq": [],
+    "xr": [[(0, S, "vvvvvvvvvvvsssss+")], [(0, S, "vvvvvvgggggggggg+")], [(0, S, "g+gggg")], [(0, S, "g+gggg")]],
+    "eg": 8, "hm": 4, "pm": 2, "stage": True,
+    "iters": 12, "look": 0.5, "seed": 3, "noise": 200, "back": 0.02,
+    "rounds": [(1, 480000, 0.008), (1, 200000, 0.004)], "tries": 3, "reach": 40, "cap": 0.001,
+    "aim": 50, "far": 40, "window": 250, "stay": 4000,
+    "cost": dict(f=1.15, gc=1.55, sc=4.2, pe=.5, sem=170, ov=0, dl=2200, rl=3200, gp=1.05, fs=1.4),
+    "figs": [dict(f=1.1, gc=1.6, sc=4.0, pe=.47, sem=160, ov=5, dl=1750, rl=2500, gp=1.0, fs=1.0),
+             dict(f=1.2, gc=1.45, sc=4.5, pe=.54, sem=190, ov=0, dl=2600, rl=4200, gp=1.1, fs=1.8)],
+}
+CYC = 0.83
 
 _SB = {
-    "XS": (768, BF), "YS": (768, BF), "I4": (128, BF), "I4F": (128, F), "D1R": (3072, BF), "D20R": (3072, BF), "D21R": (3072, BF),
-    "NBI": (Q0, I32), "DLI": (Q0, I32), "STI": (16, I32), "KK": (QT, BF), "CE": (C0 + CT, BF), "AC": (C0 + CT, F),
-    "NL": (LO + QT, F), "IOTA": (QT, F), "XREP": (768 * 16, BF), "D1": (4096, BF), "D20": (PAD + 4096, BF),
-    "D21": (PAD + 4096, BF), "AG": (3072, F), "RR0": (3072, F), "RR1": (3072, F), "SC": (3072, F), "O1": (LN, U16),
-    "O20": (LN, U16), "O21": (LN, U16), "CANDF": (LN, F), "SD": (FD + LN, F), "DAT": (LN, F),
-    "LIF": (LN, F), "RQF": (LN, F), "RQ16": (LN, U16), "E": (16 * LN, BF), "CMB": (LN, BF),
-    "WM": (LN, BF), "WS": (LN, BF), "THR": (256, F), "RSUM": (256, BF),
-    "MN": (384, F), "MB": (384, F), "MX": (384, F), "XP": (384, F), "XQ": (384, F), "OHT": (384, BF),
-    "P4": (S, F), "GG": (S, F), "YO": (768, F), "IB": (128, BF), "NIB": (128, BF), "LANE4": (16, F),
-    "GI": (2 * (GW + 64), BF), "RH": (384, BF), "RS": (1024, BF), "RZ": (128, BF), "IOM": (LN, F), "Y4": (3 * S, BF), "ZP": (192, BF), "ZN": (136, BF),
-    "ZPN": (136, BF), "ZS": (144, BF), "ZM": (128, BF),
-    "OBD": (128, BF), "NBD": (128, BF), "TRI": (128, BF), "TRB": (128, BF), "IDF": (128, F), "SL": (72, BF),
-    "DM": (128, F), "BSEL": (8, F), "KC1": (128, BF), "KC2": (128, BF), "ONE2": (144, BF), "RB": (32, BF),
-    "KPAT": (256, F), "GPAT": (128, F), "RMIN": (128, F), "RMAX": (128, F), "RMC": (128, F), "MD": (512, BF), "MT": (384, BF),
-    "TI": (24, I32), "T2": (24, I32), "SEL": (24, I32), "RI": (24, I32),
-    "WL": (16, F), "THL": (16, F), "THX": (16, F), "PI": (8, I32), "CF": (16, F), "IU": (16, U16), "BL": (8, U16),
-    "LANEL": (16, F), "LX": (16, F), "LG": (16, F), "MCOL": (8, F),
-    "ST16": (16, U16), "QL0": (16, U16), "QL1": (16, U16), "QL2": (16, U16), "QL3": (16, U16), "CLF": (8, F),
-    "K1I": (16, I32), "QI": (16, I32), "QF": (16, F),
-    "LVF": (16, F), "WINF": (16, F), "HD": (16, F), "HF": (16, F), "HM": (16, F), "HM2": (16, F), "YY": (16, F),
-    "FF": (16, F), "TB1": (16, F), "TB16": (16, U16), "TA1": (16, F), "WTH": (16, F),
-    "TA16": (16, U16), "SI": (16, I32), "CI": (16, I32), "U4": (16, F),
-    "CN16": (16, U16), "NW": (16, BF), "CUM": (16, BF), "GP": (16, F), "GP0": (16, U16),
-    "PU1": (8, F), "PU2": (8, F), "PU3": (8, F),
-    "SX0": (17, U16), "SX1": (17, U16), "LU0": (17, U16), "LU1": (17, U16), "XR0": (S + 16, BF), "XR1": (S + 16, BF),
-    "SA0": (H, F), "SA1": (H, F),
+    "XS": (X0 + 768, BF), "YS": (768, BF), "NBI": (Q0, I32), "DLI": (Q0, I32), "STI": (16, I32), "KK": (QT, BF),
+    "CE": (C0 + CT, BF), "AC": (C0 + CT + GW - H, F), "NL": (LO + QT, F), "IOTA": (QT, F), "XREP": (768 * 16, BF),
+    "X3": (768 * 16, BF), "D1": (4096, BF), "D20": (4096, BF), "D21": (4096, BF), "AG": (3072, F), "RR0": (3072, F),
+    "RR1": (3072, F), "SC": (3072, F), "O1": (LN, U16), "O20": (LN, U16), "O21": (LN, U16), "CAND": (LN, HF),
+    "LI": (LN, HF), "RQF": (LN, F), "RQ16": (LN, U16), "E": (16 * LN, BF), "CMB": (LN, BF), "W40": (768, F),
+    "W41": (768, F), "M": (3 * 384, F), "XP": (384, F), "XQ": (384, F), "OHT": (384, BF), "GG": (S, F), "YO": (768, F),
+    "IB": (128, BF), "NIB": (128, BF), "IH": (128, HF), "GI": (2 * GW, BF), "IOM": (3 * LN, F), "Z4": (144, BF),
+    "NZ4": (144, BF), "ZS": (144, BF), "OBD": (128, BF), "NBD": (128, BF), "TRI": (128, BF), "TRB": (128, BF),
+    "IDF": (128, F), "SL": (72, BF), "DM": (128, F), "BSEL": (8, F), "KC1": (128, BF), "KC2": (128, BF),
+    "ONE2": (144, BF), "RB": (32, BF), "KPAT": (384, F), "GPAT": (128, F), "RMIN": (128, F), "RMAX": (128, F),
+    "RMC": (128, F), "MD": (384, BF), "MT": (384, BF), "TI": (24, I32), "T2": (24, I32), "SEL": (24, I32),
+    "RI": (24, I32), "IU": (24, U16), "WL": (16, F), "THL": (16, F), "THX": (16, F), "PI": (8, I32), "CF": (16, F),
+    "BL": (8, U16), "LANEL": (16, F), "LX": (16, F), "LG": (16, F), "MCOL": (8, F), "ST16": (16, U16),
+    "QL0": (16, U16), "QL1": (16, U16), "QL2": (16, U16), "QL3": (16, U16), "CLF": (8, F), "K1R": (16, F),
+    "QF0": (16, F), "QF1": (16, F), "LVF": (16, F), "WINF": (16, F), "HD": (16, F), "HF": (16, F), "HM": (16, F),
+    "HM2": (16, F), "YY": (16, F), "TB1": (16, F), "TB16": (16, U16), "TA1": (16, F), "WTH": (16, F),
+    "TA16": (16, U16), "SI": (16, I32), "CI": (16, I32), "U4": (16, F), "CN16": (16, U16), "NW": (16, BF),
+    "CUM": (16, BF), "GP": (16, F), "GP0": (16, U16), "PU1": (8, F), "PU2": (8, F), "PU3": (8, F),
+    "SX0": (17, U16), "SX1": (17, U16), "LU0": (17, U16), "LU1": (17, U16), "XR0": (S, BF), "XR1": (S, BF),
+    "SA0": (S, F), "SA1": (S, F), "LV2": (8, F),
 }
 _PS = ["K0", "K1", "R0", "R1", "CM", "TR", "F0", "F1"]
+LINES = _PS + ["DM"]
 SCRATCH = {}
 POOL = {}
 for _n in _SB:
@@ -54,49 +73,12 @@ for _n in _SB:
         SCRATCH["SM" + _d] = ("sbuf", [128, POOL[_n][1] + 16], _d)
     else:
         SCRATCH[_n] = ("sbuf", [128, _w], _d)
+SCRATCH["X3"] = ("sbuf", [128, 768, 16], BF)
 for _n in _PS:
     SCRATCH[_n] = ("psum", [128, 512], F)
-NDMA = 60
-SEMAPHORES = (["sv", "ss", "st_", "sg", "sent", "hsent"] + ["dm%d" % i for i in range(NDMA)]
-              + [a + b + c for a in "gh" for b in "exa" for c in "01"])
-
-CFG = {
-    "direct": [(0, 1, 0), (1, 1, 0), (2, 1, 0), (3, 1, 0)],
-    "off": [(0, 1, 2), (0, 1, 5), (0, 2, 2), (0, 2, 5), (3, 1, 5)],
-    "f1": [(0, 1, 5)],
-    "em": [],
-    "agv": [],
-    "cx": [(t, h) for t in range(3) for h in range(2)],
-    "g3": [1],
-    "gv": [],
-    "gx": [], "dfm": 5, "dg": [], "ga": False, "m1": [], "gm": [], "ohm": False, "agm": 1, "eg": 4, "vm": 2, "two": False, "wsel": True, "pe4": False, "xq": True, "xr0": (10, 5), "xr1": (6, 0), "split": [3],
-    "iters": 8, "look": 30, "seed": 1, "noise": 250,
-    "cost": {"f": 1.1, "gc": 1.56, "sc": 3.8, "pe": 0.5, "sem": 120.0, "ov": 20.0, "dl": 1500.0, "rl": 2000.0},
-}
-CFG.update({'direct': [(0, 1, 0), (0, 2, 0), (1, 1, 0), (1, 2, 0), (2, 1, 0), (2, 2, 0), (3, 1, 0), (3, 2, 0)], 'off': [(0, 1, 2), (0, 1, 5), (0, 2, 2), (0, 2, 5), (1, 1, 3), (1, 2, 0), (2, 2, 0), (3, 1, 5)], 'f1': [(0, 1, 5), (1, 1, 3), (1, 1, 7), (1, 2, 1), (1, 2, 7), (2, 1, 2), (2, 1, 3), (2, 1, 7), (2, 2, 0)], 'relu': {}, 'agv': [(3, 1), (3, 3)], 'cx': [(0, 0), (0, 1), (1, 0), (1, 1), (2, 0), (2, 1)], 'g3': [], 'gv': [], 'eg': 8, 'vm': 1, 'two': False, 'wsel': True, 'pe4': False, 'xq': False, 'xr0': (10, 5), 'xr1': (6, 0), 'split': [2, 3], 'iters': 4, 'look': 0.1, 'seed': 378, 'noise': 250, 'cost': {'f': 1.1, 'gc': 1.56, 'sc': 3.8, 'pe': 0.5, 'sem': 80.0, 'ov': 0.0, 'dl': 1500.0, 'rl': 2000.0}})
-CFG.update({'off': [(0, 1, 2), (0, 1, 5), (0, 2, 2), (0, 2, 5), (1, 2, 0), (2, 2, 0), (3, 1, 5)], 'f1': [(0, 1, 5), (1, 1, 7), (1, 2, 7), (2, 1, 7), (2, 2, 0)], 'cx': [(0, 0), (0, 1), (1, 0), (1, 1), (2, 1)], 'gv': [(1, 1, 6)], 'xr1': (12, 0), 'split': [0, 2], 'seed': 2868, 'noise': 100})
-CFG.update({"tabu": 0, "tries": 12, "moves": 0, "back": 1.0, "reach": 40, "slack": 0.0005, "figs": [
-    {"f": 1.0, "gc": 1.56, "sc": 3.8, "pe": 0.45, "sem": 200.0, "ov": 0.0, "dl": 1500.0, "rl": 2000.0},
-    {"f": 1.4, "gc": 2.2, "sc": 5.0, "pe": 0.62, "sem": 120.0, "ov": 20.0, "dl": 2200.0, "rl": 3500.0}]})
-MID = {"f": 1.15, "gc": 1.75, "sc": 4.2, "pe": 0.52, "sem": 160.0, "ov": 0.0, "dl": 1700.0, "rl": 2500.0}
-CFG.update(m1=[1, 2, 3], ohm=True, agm=1, em=[], cx=[(t, h) for t in range(3) for h in range(2)], split=[3], gv=[],
-           two=True, xq=True, xr1=(4, 0), cost=MID, tabu=0, moves=70000, slack=.004, figs=[MID], iters=20, back=.02,
-           noise=400, look=.2, agv=[(3, 0), (3, 1)],
-           direct=[(t, 1, 0) for t in range(4)] + [(t, 2, k) for t in range(4) for k in range(2)],
-           off=[(0, 1, 2), (0, 2, 2), (0, 1, 5), (0, 2, 5), (0, 1, 1), (0, 2, 4), (1, 2, 0), (1, 1, 0), (2, 2, 0), (2, 1, 0),
-                (3, 1, 5), (3, 1, 2)],
-           f1=[(0, 1, 5), (0, 2, 5), (1, 1, 7), (1, 2, 7), (2, 1, 7), (2, 2, 7), (3, 1, 2)])
-CFG.update(moves=70000, slack=.005, ga=False, wsel=False, agv=[(3, 0)], look=.1, iters=60, noise=200, seed=3,
-           off=[(0, 1, 2), (0, 2, 2), (0, 1, 5), (0, 2, 5), (1, 2, 0), (2, 2, 0), (1, 1, 0), (3, 1, 5), (2, 1, 0), (0, 1, 1)],
-           cost=dict(f=1.15, gc=1.65, sc=4.6, pe=.65, sem=150, ov=0, dl=1900, rl=3000),
-           figs=[dict(f=1.15, gc=1.75, sc=4.2, pe=.52, sem=170, ov=0, dl=1700, rl=2500),
-                 dict(f=1.1, gc=1.5, sc=5, pe=.78, sem=130, ov=0, dl=2000, rl=3500)])
-CFG.update(moves=60000, gx=[0, 1, 2], wsel=True, agv=[(3, 0), (3, 1)],
-           off=[(0, 1, 2), (0, 2, 2), (0, 1, 5), (0, 2, 5), (0, 1, 1), (0, 2, 4), (1, 2, 0), (1, 1, 0), (2, 2, 0), (2, 1, 0),
-                (3, 1, 5), (3, 1, 2)],
-           figs=[dict(f=1.1, gc=1.65, sc=4.0, pe=.5, sem=190, ov=0, dl=1600, rl=2200),
-                 dict(f=1.15, gc=1.5, sc=4.5, pe=.64, sem=150, ov=0, dl=3500, rl=5000)])
-CYC = 0.83
+NDMA = 50
+SEMAPHORES = (["sv", "ss", "st_", "sg", "hsent"] + ["dm%d" % i for i in range(NDMA)]
+              + [a + b + c for a in "ghs" for b in "exa" for c in "01"])
 
 
 def R(name, lo=0, hi=None, step=1, p0=0, p1=128, ps=1):
@@ -110,7 +92,7 @@ def width(r):
 
 
 def two_byte(r):
-    return r[0] in _SB and _SB[r[0]][1] in (BF, U16)
+    return r[0] in _SB and _SB[r[0]][1] in (BF, U16, HF)
 
 
 def psum(r):
@@ -145,30 +127,18 @@ def far_core(T, topo, src):
 
 
 def landing(kind, t):
-    if kind == "e":
-        return R("XR%d" % t, 0, S)
-    if kind == "x":
-        return R("LU%d" % t, 0, 4)
-    a = C0 + CN + LN * (t + 1) + S
-    return R("AC", a, a + H)
+    return R("LU%d" % t, 0, 13) if kind == "x" else R({"e": "XR%d", "a": "SA%d"}[kind] % t)
 
 
 def chunks(t):
-    if t in (0, RO - 1):
-        return [(0, HL), (HL, HL)]
-    return [(0, HL), (HL, HL), (S, H)] if t in CFG["g3"] else [(0, 128), (128, 128)]
-
-
-def signed(t, ph, u):
-    return (t, ph, u) in CFG["em"] and (t, ph, u) not in CFG["off"] and 32 * u < S
+    a = CFG["cut"][t]
+    if t in CFG["g3"]:
+        return [(0, a), (a, S - a), (S, H)]
+    return [(0, a), (a, (LN if t in (1, 2) else S) - a)]
 
 
 def xlanes(t):
-    return 32 + 32 * max(u for ph in (1, 2) for u in range(S // 32) if (t, ph, u) not in CFG["off"])
-
-
-DIFF_ROWS = ([(0, "ZN", 1)] + [(k, "ZPN", k) for k in range(1, 7)] + [(7, "ZP", 7)],
-             [(7, "ZN", 0)] + [(k, "ZPN", k - 8) for k in range(8, 15)] + [(15, "ZP", 7)])
+    return 32 + 32 * max([u for ph in (1, 2) for u in range(S // 32) if (t, ph, u) not in CFG["off"]] + [-1])
 
 
 def relay_program(g, core, T, topo):
@@ -204,6 +174,8 @@ def build(g, core, T, topo, rank):
 
     def A(r):
         name, b = POOL.get(r[0], (r[0].split("#")[0], 0))
+        if name == "X3":
+            return T.X3[:, r[1] // 16:r[2] // 16, r[1] % 16 if r[3] > 1 else slice(0, 16)]
         return T[name][slice(r[4], r[5], r[6]) if r[6] > 1 else slice(r[4], r[5]),
                        slice(b + r[1], b + r[2], r[3]) if r[3] > 1 else slice(b + r[1], b + r[2])]
 
@@ -246,18 +218,30 @@ def build(g, core, T, topo, rank):
     def vgather(o, w, l):
         op("v", lambda: V.tensor_copy(A(o), IND(w, l)), [w, l], [o], ("gather", width(o)))
 
+    def vgadd(o, w, l, c):
+        op("v", lambda: V.tensor_scalar(A(o), IND(w, l), c, None, ALU.add), [w, l], [o], ("gather", width(o)))
+
     def vgtt(o, w, l, b, alu):
         op("v", lambda: V.tensor_tensor(A(o), IND(w, l), A(b), alu), [w, l, b], [o], ("gather", width(o)))
 
     def vscat(w, l, i):
         op("v", lambda: V.tensor_copy(IND(w, l), A(i)), [l, i], [w], ("scatter", width(i)))
 
-    def act(o, i, func, bias=0.0, scale=1.0):
-        op("s", lambda: SE.activation(A(o), A(i), func, bias=sc(bias), scale=sc(scale)), [i] + refs(bias, scale), [o],
-           ("plain", width(o)))
+    def vscat2(w, l, a, b, alu):
+        op("v", lambda: V.tensor_tensor(IND(w, l), A(a), A(b), alu), [l, a, b], [w], ("scatter", width(a)))
 
-    def sgather(o, w, l):
-        op("s", lambda: SE.activation(A(o), IND(w, l), ACT.Copy), [w, l], [o], ("gather", width(o)))
+    def act(o, i, func, bias=0.0, scale=1.0, first=0):
+        op("s", lambda: SE.activation(A(o), A(i), func, bias=sc(bias), scale=sc(scale)), [i] + refs(bias, scale), [o],
+           ("plain", width(o) + first))
+
+    def affine(o, i, scale, bias):
+        if o[0] in CFG["sa"]:
+            act(o, i, ACT.Identity, bias, scale)
+        else:
+            vts(o, i, scale, bias, ALU.mult, ALU.add)
+
+    def sgather(o, w, l, scale=1.0):
+        op("s", lambda: SE.activation(A(o), IND(w, l), ACT.Copy, scale=scale), [w, l], [o], ("gather", width(o)))
 
     def mms(lst):
         def fn():
@@ -273,6 +257,18 @@ def build(g, core, T, topo, rank):
         ops[-1]["starts"] = any(m[3] for m in lst)
         ops[-1]["group"] = (1 if lst[0][3] and not lst[-1][4] else 0) - (1 if lst[-1][4] and not ops[-1]["starts"] else 0)
 
+    def held(lst, m):
+        lst = [x + (i == 0, i == len(lst) - 1) for i, x in enumerate(lst)]
+        whole = R(lst[0][0][0], min(x[0][1] for x in lst), max(x[0][2] for x in lst))
+        for i in range(0, len(lst), m):
+            mms(lst[i:i + m])
+            ops[-1].update(group=int(i == 0), starts=i == 0, wr=[whole])
+            if i == 0:
+                ops[-1]["rd"] = ops[-1]["rd"] + [x[j] for x in lst for j in (1, 2)]
+
+    def close():
+        ops[-1]["group"] = -1
+
     def giota(o, pat, base, cm):
         if _SB[o[0]][1] == I32:
             fn = lambda: g.iota(A(o), pat, base, cm)
@@ -284,19 +280,34 @@ def build(g, core, T, topo, rank):
         op("g", lambda: g.affine_select(A(o), A(i), pat, cmp_, 0.0, base, cm), [i], [o],
            ("pool", 170 + 2 * width(o) * CYC))
 
+    def diagonal(o, c):
+        if o[0] in CFG["ga"]:
+            giota(o, [[0, 128]], c, 0)
+            gsel(o, o, [[-1, 128]], ALU.is_equal, 0, 1)
+        else:
+            act(o, R("IB"), ACT.Copy, scale=float(c))
+
     ndma = [0]
 
-    def dma(q, out, in_, rd, wr, more=0.0):
+    def dmas(q, pairs, rd, wr, after=()):
         k = ndma[0]
         ndma[0] += 1
         eng = {"y": SY, "s": SE, "g": g}[q]
-        op(q, lambda: eng.dma_start(out(), in_()), rd, wr, ("dma", 1000 if q == "g" else 60, more), "dma", "dm%d" % k)
 
-    def load(q, o, src, lo, hi, more=0.0):
-        dma(q, lambda: A(o), lambda: T[src][:, lo:hi], [], [o], more)
+        def fn():
+            for out, in_ in pairs:
+                eng.dma_start(out(), in_()).then_inc(T.sem["dm%d" % k], 16)
+        sides = wr or rd
+        size = sum(width(r) * len(range(r[4], r[5], r[6])) * (2 if two_byte(r) else 4) for r in sides)
+        rows = sum(8 if r[6] < 16 else 1 for r in sides)
+        op(q, fn, rd + list(after), wr, ("dma", len(pairs), rows, size), "dma", ("dm%d" % k, 16 * len(pairs)))
 
-    def copy_dma(o, i):
-        dma("y", lambda: A(o), lambda: A(i), [i], [o])
+    def load(q, o, src, lo, hi, after=()):
+        dmas(q, [(lambda: A(o), lambda: T[src][:, lo:hi])], [], [o], after)
+
+    def copies(pairs, after=()):
+        dmas("y", [((lambda r=o: A(r)), (lambda r=i: A(r))) for o, i in pairs], [i for o, i in pairs],
+             [o for o, i in pairs], after)
 
     mask, neng = few_engines(topo, core, far_core(T, topo, core))
     n = len(T.cores)
@@ -305,10 +316,10 @@ def build(g, core, T, topo, rank):
         dst, via = route(T, topo, rank, t)
         to = dst if via is None else via
         rid, pid = topo.addr(to, core)
-        sem = T.sem[("g%s%d" if via is None else "h%s%d") % (kind, t)]
+        sem, sent = T.sem[("g%s%d" if via is None else "h%s%d") % (kind, t)], "s%s%d" % (kind, t)
         land = landing(kind, t)
-        op("g", lambda: g.remote_dma(A(land), A(src), sem, T.sem.sent, pid, rid, mask), [src], [],
-           ("send", 1500 if kind == "e" else 500), "send")
+        op("g", lambda: g.remote_dma(A(land), A(src), sem, T.sem[sent], pid, rid, mask), [src], [],
+           ("send", 1500 if kind == "e" else 500), "dma", (sent, neng))
         me = len(ops) - 1
         frm = (rank - 1 - t % (n - 1)) % n
         _, v2 = route(T, topo, frm, t)
@@ -316,164 +327,156 @@ def build(g, core, T, topo, rank):
             cnt = few_engines(topo, T.cores[frm], far_core(T, topo, T.cores[frm]))[1]
         else:
             cnt = few_engines(topo, v2, core)[1]
-        op(None, None, [], [land], ("arrive", 1 if via is None else 2), "arr", ("g%s%d" % (kind, t), cnt, me))
+        op(None, None, [], [land], ("arrive", 2 - t), "arr", ("g%s%d" % (kind, t), cnt, me))
 
-    compact = len(CFG["cx"]) > 0
-    plainp = len(CFG["cx"]) < 2 * RO
-    QOFF = LN if CFG["two"] else LO
+    def xs(t, a, b):
+        return R("XS", X0 + S * t + a, X0 + S * t + b)
+
+    def scans(nm, c):
+        return 128 * c + 384 * ["MN", "MB", "MX"].index(nm)
 
     load("y", R("STI"), "st", 0, 16)
     load("s", R("NBI"), "nb", 0, Q0)
-    load("y", R("XS"), "xs", 0, 768)
+    load("y", xs(0, 0, S), "xs", 0, S)
     load("s", R("KK", 0, Q0), "kq", 0, Q0)
-    load("y", R("DLI"), "dl", 0, Q0)
-    load("y", R("CE", C0, C0 + CN), "cc", 0, CN, 500)
-    load("g", R("AC", C0, C0 + CN), "aa", 0, CN, 2000)
-    load("y", R("YS"), "ys", 0, 768)
-    for t in range(2):
-        send(t, "e", R("XS", S * t, S * t + S))
+    later = [R("STI")] if CFG["stage"] else []
+    load("y", xs(1, 0, 3 * S), "xs", S, 768)
+    load("y", R("DLI"), "dl", 0, Q0, later)
+    load("y", R("CE", C0, C0 + CN), "cc", 0, CN, later)
+    load("g", R("AC", C0, C0 + CN), "aa", 0, CN, later)
+    load("y", R("YS"), "ys", 0, 768, later)
     for t in range(3):
-        load("y", R("KK", Q0 + LN * t, Q0 + LN * t + S), "xs", S * t, S * t + S)
+        load("y", R("KK", Q0 + NEW[t], Q0 + NEW[t] + S), "xs", S * t, S * t + S, later)
 
-    vset(R("ZM"), 0.0)
+    zm = R("XS", 0, X0)
+    vset(zm, 0.0)
+    for t in range(2):
+        send(t, "e", xs(t, 0, S))
     vset(R("ONE2"), 1.0)
-    for r in ([R("AC", 0, 128), R("AC", 128, C0), R("CE", 0, H), R("CE", C0 + CN + S, C0 + CN + LN),
-               R("KK", Q0 + S, Q0 + LN), R("XR0", S, S + 16), R("XR1", S, S + 16), R("AC", C0 + CN + S, C0 + CN + LN),
-               R("NL", LO + Q0 + S, LO + Q0 + LN), R("NL", LN + Q0 + S, LN + Q0 + LN)]
-              + ([R("MN", 256), R("MB", 256), R("MX", 256)] if CFG["g3"] else [])):
-        act(r, R("ZM", 0, width(r)), ACT.Copy)
-    for r in [R("MN", 0, 256), R("MB", 0, 256)] + ([] if CFG["two"] else [R("SD", S, FD)]):
-        act(r, R("AC", 0, width(r)), ACT.Copy)
-    vset(R("RI"), 0)
+    if "AC" in CFG["sa"]:
+        for a in range(0, C0, 128):
+            act(R("AC", a, a + 128), zm, ACT.Copy)
+    else:
+        vset(R("AC", 0, C0), 0.0)
+    for t in range(3):
+        copies([(R("IOM", LN * t, LN * t + LN), R("AC", 0, LN))]
+               + ([(R("GI", GW * t, GW * t + H), R("XS", 0, H))] if t < 2 else [])
+               + ([(R("AC", C0 + CN + NEW[t] + S, C0 + CN + NEW[t + 1]), R("AC", 0, H))] if t else []), later)
     vset(R("CUM"), 0.0)
+    vset(R("NW"), 1.0)
+    vset(R("RI"), 0)
     vset(R("MCOL", 0, 1), 84.0)
-    vset(R("MCOL", 1, 2), math.log(0.25))
-    if plainp:
-        vset(R("RB"), -8192.0)
+    vset(R("RB"), -8192.0)
     giota(R("PI", 0, 1), [[0, 1]], 0, 1)
-    giota(R("IOTA", 0, 256), [[1, 256]], 0, 0)
+    giota(R("IOTA", 0, 72), [[1, 72]], 0, 0)
+    giota(R("IOTA", 72, Q0), [[1, Q0 - 72]], 72, 0)
     giota(R("KPAT", 0, 128), [[0, 8], [1, 16]], 0, 0)
-    if CFG["ohm"]:
-        giota(R("KPAT", 128, 256), [[0, 8], [1, 16]], 0, 0)
     giota(R("GPAT"), [[1, 8], [0, 16]], 0, 0)
-    giota(R("IOTA", 256, Q0 + LN), [[1, Q0]], 256, 0)
-    giota(R("IOTA", Q0 + LN, QT), [[1, 2 * LN]], Q0 + LN, 0)
+    copies([(R("KPAT", a, a + 128), R("KPAT", 0, 128)) for a in ([128, 256] if CFG["g3"] else [128])]
+           + [(R("M", CFG["cut"][0] // 128 * 128, 384), R("IOTA", CFG["cut"][0] // 128 * 128, 384))])
+    copies([(R("M", 384), R("AC", C0, C0 + 768))])
+    for t in range(RO - 1):
+        a, w = Q0 + NEW[t], NEW[t + 1] - NEW[t]
+        giota(R("IOTA", a, a + w), [[1, w]], a, 0)
+        copies([(R("IOM", LN * t, LN * t + w, 1, 8 + t, 128, 16), R("IOTA", a, a + w, 1, 8 + t, 128, 16))])
     md = {}
     for l0, cnt in sorted(set(ch for t in range(RO - 1) for ch in chunks(t)), reverse=True):
         if l0 not in md:
             md[l0] = 128 * len(md)
             gsel(R("MD", md[l0], md[l0] + cnt), R("IOTA", l0, l0 + cnt), [[-1, cnt]], ALU.is_equal, 0, 1)
-    for j in range(2):
-        giota(R("GI", j * (GW + 64), j * (GW + 64) + H), [[0, H]], S, 0)
     vts(R("PI", 1, 2), R("PI", 0, 1), 15, None, ALU.bitwise_and)
     vts(R("PI", 2, 3), R("PI", 0, 1), 4, None, ALU.arith_shift_right)
-    vts(R("PI", 3, 4), R("PI", 0, 1), 63, None, ALU.bitwise_and)
-    vcopy(R("CF", 0, 4), R("PI", 0, 4))
-    p_, pm, pg, p64 = R("CF", 0, 1), R("CF", 1, 2), R("CF", 2, 3), R("CF", 3, 4)
-    g8 = R("CF", 4, 5)
-    vts(g8, pg, 8.0, 7.0, ALU.mult, ALU.add)
-    vts(R("CF", 5, 6), p_, 0.0, 2048.0, ALU.is_equal, ALU.mult)
-    vts(R("CF", 6, 7), p_, 1.0, -float(B1), ALU.is_equal, ALU.mult)
-    vts(R("CF", 7, 8), p_, 1.0, -float(B2), ALU.is_equal, ALU.mult)
+    vcopy(R("CF", 0, 3), R("PI", 0, 3))
+    p_, pm, pg, g8 = R("CF", 0, 1), R("CF", 1, 2), R("CF", 2, 3), R("CF", 4, 5)
+    affine(g8, pg, 8.0, 7.0)
     kpat = R("KPAT", 0, 128)
-    vts(R("KC1"), kpat, R("CF", 5, 6), R("CF", 6, 7), ALU.mult, ALU.add)
-    vts(R("KC2"), kpat, R("CF", 5, 6), R("CF", 7, 8), ALU.mult, ALU.add)
+    for nm, c, step, add, off in (("KC1", 5, 4096.0, 4096.0, B1), ("KC2", 9, 2048.0, 0.0, B2)):
+        affine(R("CF", c, c + 1), p_, -step, step)
+        affine(R("CF", c + 1, c + 2), p_, -off - add, add)
+        affine(R(nm), kpat, R("CF", c, c + 1), R("CF", c + 1, c + 2))
     vts(R("DM"), kpat, pm, None, ALU.is_equal)
     vts(R("OBD"), R("GPAT"), pg, None, ALU.is_equal)
     vts(R("BSEL"), R("IOTA", 0, 8), pg, None, ALU.is_equal)
     gsel(R("IB"), R("ONE2", 0, 128), [[-1, 128]], ALU.is_equal, 0, 1)
-    act(R("IDF"), R("IB"), ACT.Copy)
+    vcopy(R("IH"), R("IB"))
+    diagonal(R("IDF"), 1)
+    diagonal(R("TRB"), -1024)
+    diagonal(R("NIB"), -1)
+    for t in range(RO - 1):
+        diagonal(R("MT", 128 * t, 128 * t + 128), CN + NEW[t])
     vts(R("SL"), R("IOTA", 0, 72), g8, 65536.0, ALU.is_equal, ALU.mult)
     gsel(R("TRI"), R("OBD"), [[1, 128]], ALU.is_gt, 0, -1)
-    act(R("TRB"), R("IB"), ACT.Copy, scale=-1024.0)
-    act(R("NIB"), R("IB"), ACT.Copy, scale=-1.0)
-    act(R("I4"), R("IB"), ACT.Copy, scale=0.25)
-    for t in range(RO - 1):
-        act(R("MT", 128 * t, 128 * t + 128), R("IB"), ACT.Copy, scale=float(CN + LN * t))
-    if CFG["pe4"]:
-        act(R("I4F"), R("IB"), ACT.Copy, scale=-0.25)
-    if plainp:
-        act(R("NBD"), R("OBD"), ACT.Copy, scale=-1.0)
+    act(R("NBD"), R("OBD"), ACT.Copy, scale=-1.0)
+    vset(R("Z4", 0, 16), 0.0)
+    gsel(R("Z4", 16), R("OBD"), [[0, 32], [1, 4]], ALU.is_equal, 0, 0)
+    act(R("NZ4"), R("Z4"), ACT.Copy, scale=-1.0)
     vts(R("RMIN"), kpat, 0.0, 2.0 ** 25, ALU.is_equal, ALU.mult)
-    vts(R("RMAX"), R("RMIN"), -1.0, 4096.0, ALU.mult, ALU.add)
-    vts(R("RMC"), R("RMIN"), 0.625, -2.0 ** 24, ALU.mult, ALU.add)
-    vcopy(R("IU"), R("IOTA", 0, 16))
+    affine(R("RMAX"), R("RMIN"), -1.0, 4096.0)
+    affine(R("RMC"), R("RMIN"), 0.625, -2.0 ** 24)
+    vcopy(R("IU"), R("IOTA", 0, 24))
     vts(R("BL"), R("IOTA", 0, 8), 16.0, 15.0, ALU.mult, ALU.add)
-    vts(R("LANEL"), R("IOTA", 0, 16), 16.0, pm, ALU.mult, ALU.add)
-    vts(R("LX", 0, 12), R("LANEL", 0, 12), 2.0 ** 23 + H - C0, None, ALU.add)
-    vts(R("LX", 12, 16), R("LANEL", 12, 16), 2.0 ** 23 - S - C0, None, ALU.add)
-    vts(R("LG"), R("LANEL"), float(LN - 1024), None, ALU.add)
-    act(R("WL"), R("LANEL"), ACT.Exp, bias=R("MCOL", 0, 1), scale=-LNR)
+    affine(R("LANEL"), R("IOTA", 0, 16), 16.0, pm)
+    affine(R("LX", 0, 12), R("LANEL", 0, 12), 1.0, 2.0 ** 23 + H - C0)
+    affine(R("LX", 12, 16), R("LANEL", 12, 16), 1.0, 2.0 ** 23 - S - C0)
+    affine(R("LG"), R("LANEL"), 1.0, float(LN - 1024))
+    affine(R("LV2", 0, 4), R("LANEL", 0, 4), 1.0, pm)
+    act(R("WL"), R("LANEL"), ACT.Exp, bias=R("MCOL", 0, 1), scale=-LNR, first=1400)
     gsel(R("ZS"), R("ONE2"), [[1, 144]], ALU.is_equal, -15, -1)
     vts(R("CF", 8, 9), pm, 0.0, None, ALU.is_equal)
-    if CFG["gx"]:
-        vts(R("CF", 9, 12), R("IOTA", 8, 11), pm, None, ALU.is_equal)
     act(R("ZS"), R("ZS"), ACT.Copy, scale=R("CF", 8, 9))
-    if CFG["wsel"]:
-        act(R("THL"), R("WL"), ACT.Copy, scale=2.5)
-        act(R("THX", 0, 12), R("WL", 0, 12), ACT.Copy, scale=2.5)
-    else:
-        vset(R("MCOL", 2, 3), 84.0 + math.log(2.5))
-        vset(R("LVF"), 1.0)
-        act(R("THR"), R("IOTA", 0, 256), ACT.Exp, bias=R("MCOL", 2, 3), scale=-LNR)
-        for j in range(2):
-            vtt(R("THR", 128 * j, 128 * j + 128), R("THR", 128 * j, 128 * j + 128), R("DM"), ALU.mult)
-            vts(R("RSUM", 128 * j, 128 * j + 128), kpat, 0.0, None, ALU.not_equal)
-    if not CFG["two"]:
-        act(R("LANE4"), R("LANEL"), ACT.Copy, scale=4.0)
-    if compact:
-        giota(R("ZP"), [[0, 3], [1, 64]], 0, 0)
-        giota(R("RS"), [[1, 8], [8, 8], [0, 16]], 0, 0)
-        vts(R("ZP", 0, 136), R("ZP", 0, 136), g8, None, ALU.is_equal)
-        act(R("ZN"), R("ZP", 0, 136), ACT.Copy, scale=-1.0)
-        vtt(R("ZPN", 1, 136), R("ZP", 1, 136), R("ZP", 0, 135), ALU.subtract)
-        for j in range(2):
-            vts(R("RS", 512 * j, 512 * j + 512), R("RS", 512 * j, 512 * j + 512), p64, None, ALU.is_equal)
-        giota(R("RZ"), [[0, 16], [1, 8]], 0, 0)
-        vts(R("RZ"), R("RZ"), 0.0, -8192.0, ALU.is_equal, ALU.mult)
-    if CFG["ga"]:
-        for t in range(RO - 1):
-            act(R("Y4", S * t, S * t + S), R("YS", S * t, S * t + S), ACT.Copy, scale=0.25)
+    act(R("THL"), R("WL"), ACT.Copy, scale=2.5)
+    act(R("THX", 0, 12), R("WL", 0, 12), ACT.Copy, scale=2.5)
     vcopy(R("ST16"), R("STI"))
     vcopy(R("NL", LN, LN + Q0), R("NBI"))
     vcopy(R("NL", LO, LO + Q0), R("DLI"))
     vcopy(R("QL0", 12, 16), R("STI", 12, 16))
-    vcopy(R("CLF", 0, 4), R("STI", 12, 16))
+    vts(R("CLF", 0, 4), R("STI", 12, 16), float(LN), None, ALU.add)
+
+    def repeat(eng, a, b, m):
+        o, i, w = (lambda: T.X3[:, a:b, m:2 * m]), (lambda: T.X3[:, a:b, 0:m]), (b - a) * m
+        fn = {"g": lambda: g.affine_select(o(), i(), [[0, b - a], [0, m]], ALU.is_ge, 0.0, 0, 0),
+              "v": lambda: V.tensor_copy(o(), i()), "s": lambda: SE.activation(o(), i(), ACT.Copy)}[eng]
+        op(eng, fn, [R("X3", 16 * a + k, 16 * b, 16) for k in range(m)],
+           [R("X3", 16 * a + k, 16 * b, 16) for k in range(m, 2 * m)],
+           {"g": ("pool", 170 + 2 * w * CYC), "v": ("plain", w / 2), "s": ("plain", w)}[eng])
+        if m == 8:
+            copies([(R("XREP", 16 * a, 16 * b), R("X3", 16 * a, 16 * b))])
 
     for t in range(RO):
-        for k in range(16):
-            o, i = R("XREP", S * 16 * t + k, (S * t + xlanes(t)) * 16, 16), R("XS", S * t, S * t + xlanes(t))
-            nv, ns = CFG["xr%d" % t] if t < 2 else (0, 0)
-            if k >= nv + ns:
-                gsel(o, i, [[0, xlanes(t)]], ALU.is_ge, 0, 0)
-            elif k < nv:
-                vcopy(o, i)
-            else:
-                act(o, i, ACT.Copy)
+        for a, b, who in CFG["xr"][t]:
+            a, b = S * t + a, S * t + min(b, xlanes(t))
+            single, double = who.split("+")
+            for k, eng in enumerate(single if a < b else ""):
+                o, i = R("X3" if double else "XREP", 16 * a + k, 16 * b, 16), xs(0, a, b)
+                if eng == "g":
+                    gsel(o, i, [[0, b - a]], ALU.is_ge, 0, 0)
+                elif eng == "v":
+                    vcopy(o, i)
+                else:
+                    act(o, i, ACT.Copy)
+            for j, eng in enumerate(double if a < b else ""):
+                repeat(eng, a, b, len(single) << j)
 
-    def lists(t, ph, c, o16, of, win, lst, want_f):
-        if (t, ph, c) in CFG["direct"]:
-            vgather(o16, R("NBI") if (t, ph) == (0, 1) else win, lst)
-            if want_f:
-                sgather(of, win, lst)
-        else:
-            sgather(of, win, lst)
-            vcopy(o16, of)
+    def lists(t, ph, o16, of, win, lst, want_f):
+        vgather(o16, R(["NBI", "DLI"][ph - 1]) if t == 0 else win, lst)
+        if want_f:
+            vts(of, o16, float(LN if ph == 1 else 0), None, ALU.add)
 
-    def diffs(t, ph, c, l0, CH, dname, pad, win, oname):
-        u0, u1 = l0 // 32, (l0 + CH) // 32
-        u = u0
+    def diffs(t, ph, l0, CH, dname, win, oname):
+        u, u1 = l0 // 32, (l0 + CH) // 32
+        have = u
+        off = lambda v: v < u1 and (32 * v >= S or (t, ph, v) in CFG["off"])
         while u < u1:
             a = 32 * u
-            if a >= S or (t, ph, u) in CFG["off"]:
+            if off(u):
                 fb = lease("F1" if (t, ph, u) in CFG["f1"] else "F0")
-                d = R(dname, pad + a * 16, pad + (a + 32) * 16)
-                if a < S or (t, ph) not in CFG["gm"]:
-                    (vgather if (t, ph, u) in CFG["gv"] else sgather)(d, win, R(oname, a, a + 32))
-                elif a == S:
-                    sgather(R(dname, pad + S * 16, pad + LN * 16), win, R(oname, S, LN))
+                d = R(dname, a * 16, (a + 32) * 16)
+                if have <= u:
+                    have = u + (2 if off(u + 1) and (t, ph, u) in CFG["gm"] else 1)
+                    sgather(R(dname, a * 16, 512 * have), win, R(oname, a, 32 * have))
                 if a >= xlanes(t):
-                    x = R("CE", a - S, a - S + 32) if a >= S else R("XS", S * t + a, S * t + a + 32)
+                    g0 = (t - 1) * GW + a - S
+                    x = R("GI", g0, g0 + 32) if a >= S else xs(t, a, a + 32)
                     mms([(R(fb), R("IB"), d, True, False)]
                         + [(R(fb, k, 512, 16), R("NIB"), x, False, k == 15) for k in range(16)])
                 else:
@@ -481,282 +484,258 @@ def build(g, core, T, topo, rank):
                     mms([(R(fb), R("IB"), d, True, False), (R(fb), R("NIB"), x, False, True)])
                 ops[-1]["group"] = 1
                 act(d, R(fb), ACT.Abs)
-                ops[-1]["group"] = -1
+                close()
                 u += 1
                 continue
-            m = 1
-            while (m < CFG["vm"] and u + m < u1 and 32 * (u + m) < S and (t, ph, u + m) not in CFG["off"]
-                   and signed(t, ph, u + m) == signed(t, ph, u)):
-                m += 1
-            d = R(dname, pad + a * 16, pad + (a + 32 * m) * 16)
-            vgtt(d, win, R(oname, a, a + 32 * m), R("XREP", (S * t + a) * 16, (S * t + a + 32 * m) * 16), ALU.subtract)
-            if signed(t, ph, u):
-                vts(R(dname + "R", pad + a * 16, pad + (a + 32 * m) * 16), d, -2.0, 0.0, ALU.mult, ALU.max)
-            else:
-                act(d, d, ACT.Abs)
+            m = 2 if (t, ph, u) in CFG["vm"] and u + 1 < u1 and not off(u + 1) else 1
+            vgtt(R(dname, a * 16, (a + 32 * m) * 16), win, R(oname, a, a + 32 * m),
+                 R("XREP", (S * t + a) * 16, (S * t + a + 32 * m) * 16), ALU.subtract)
+            for v in range(u, u + m):
+                act(R(dname, 512 * v, 512 * v + 512), R(dname, 512 * v, 512 * v + 512), ACT.Abs)
             u += m
 
-    def runs(t, ph, l0, cnt, parts=False):
-        out = []
-        for a in range(l0, l0 + cnt, 32):
-            if signed(t, ph, a // 32):
-                if out and sum(out[-1]) == a and not (parts and out[-1][0] == l0 + 32):
-                    out[-1] = (out[-1][0], out[-1][1] + 32)
-                else:
-                    out.append((a, 32))
-        return out
-
-    def keys(t, ph, c, CH, l0, idf, kc, dname, pad):
-        bank, a = ("K%d" % c, 0) if c < 2 else ("K1", 128)
-        full = R(bank, a, a + 128, 1, 0, CH)
-        srcs = [(dname, l0, CH)] + [(dname + "R", l, cnt) for l, cnt in runs(t, ph, l0, CH, True)]
-        late = len(srcs) > 1
-        rows = [(full, R("ONE2", 0, CH, 1, 0, 2), R(kc, 0, 128, 1, 0, 2), False, late)]
-        lst = [(full, R(idf, l0, l0 + CH), R("IDF"), True, False)] + ([] if late else rows)
-        if c < 2:
-            mms(lst)
-            lst = []
-        for nm, l, cnt in srcs:
-            end = (nm, l, cnt) == srcs[-1]
-            mms(lst + [(R(bank, a + k % 2, a + 128, 2, l - l0, l - l0 + cnt),
-                        R(nm, pad + l * 16 + k, pad + (l + cnt) * 16, 16),
-                        R("SL", 7 - k // 2, 71 - k // 2), False, end and not late and k == 15) for k in range(16)]
-                + (rows if end and late else []))
+    def keys(c, CH, l0, num, kc, dname):
+        bank = "K%d" % c if c < 2 else lease("R1")
+        full = R(bank, 0, 128, 1, 0, CH)
+        mms([(full, R(num, l0, l0 + CH), R("IH"), True, False),
+             (full, R("ONE2", 0, CH, 1, 0, 2), R(kc, 0, 128, 1, 0, 2), False, False)])
+        mms([(R(bank, k % 2, 128, 2, 0, CH), R(dname, l0 * 16 + k, (l0 + CH) * 16, 16),
+              R("SL", 7 - k // 2, 71 - k // 2), False, k == 15) for k in range(16)])
+        if c == 2:
+            ops[-1]["group"] = 0
+            ops[-2]["rd"] = ops[-2]["rd"] + ops[-1]["rd"]
         return full
+
+    def to_list(out, tile, m0, c, CH):
+        x = R(tile, 128 * c, 128 * c + 128)
+        vgtt(x, R("M", m0, m0 + 128), R("BL"), R("DM"), ALU.mult)
+        mms([(out, x[:4] + (0, CH, 1), R("BSEL", 0, CH // 16, 1, 0, CH), True, True)])
 
     def pick_lists(out, src, w):
         mms([(out, R("ZS", 15 - l, 143 - l), R(src[0], src[1] + l, src[1] + w, 16), l == 0, l == 15) for l in range(16)])
 
-    for t in range(RO):
+    def predict(t, a, cnt, form):
         last = t == RO - 1
-        L = LN if t in (1, 2) else S
-        NB = L // 16
-        ql, lo = Q0 + LN * t, CN + LN * t
-        CL = ["ST16", "QL0", "QL1", "QL2"][t]
-        QL = "QL%d" % t
+        lo = CN + NEW[t]
+        O2, D2, rr, w4 = "O2%d" % (t % 2), "D2%d" % (t % 2), "RR%d" % (t % 2), "W4%d" % (t % 2)
+        b = a + cnt
+        yo = R("YO", S * t + a, S * t + b)
+        reset = lambda bank, w: (R(bank, 0, w, 16), R("ONE2", 0, 128, 1, 0, 2), R("RB", 0, w // 16, 1, 0, 2))
+        if form == "r":
+            w = 4 * cnt if cnt <= 128 else 2 * cnt
+            for c in range(0, 4 * cnt, w):
+                wb, lst = lease("R%d" % (c // w)), []
+                for j in range(4):
+                    x = 16 * a + 4 * cnt * j + c
+                    lst += [(R(wb, 0, w), R("Z4", 16 - j, 144 - j), R(D2, x, x + w)),
+                            (R(wb, 1, w), R("NZ4", 16 - j, 144 - j), R(D2, x, x + w - 1))]
+                held(lst + [reset(wb, w)], CFG["hm"])
+                act(R(w4, 4 * a + c, 4 * a + c + w), R(wb, 0, w), ACT.Exp, scale=1.0 / 64)
+                close()
+            copies([(R(rr, 16 * a, 16 * b, 1, r, 128, 4), R(w4, 4 * a, 4 * b)) for r in range(4)])
+        have = 0
+        if form == "e":
+            for j in range(a // 32, b // 32):
+                bank, cols = lease("R%d" % (j % 2)), lambda nm: R(nm, 512 * j, 512 * j + 512)
+                held([(R(bank), R("OBD"), cols(D2))], 1)
+                act(cols(rr), R(bank), ACT.Exp, scale=-1.0 / 64)
+                close()
+                vgtt(cols("AG"), R("AC", C0, C0 + lo), R(O2, 32 * j, 32 * j + 32), cols(rr), ALU.mult)
+            acc = lease("F1")
+            held([(R(acc, 0, cnt), R("IDF"), R("AG", 16 * a + k, 16 * b, 16)) for k in range(16)], CFG["pm"])
+            act(yo, R(acc, 0, cnt), ACT.Copy)
+            close()
+            dmas("y", [(lambda: T.yp[:, yo[1]:yo[2]], lambda: A(yo))], [yo], [])
+            return
+        for j in range(a // 32, b // 32):
+            x, cols = 512 * j, lambda nm: R(nm, 512 * j, 512 * j + 512)
+            if form == "s":
+                bank = lease("R%d" % (j % 2))
+                held([(R(bank), R("OBD"), cols(D2)), (R(bank, 1), R("NBD"), R(D2, x, x + 511)), reset(bank, 512)], 3)
+                act(cols(rr), R(bank), ACT.Exp, scale=1.0 / 64)
+                close()
+            if have <= j:
+                have = j + 1
+                while have < min(b // 32, j + CFG["agm"][t]) and ((t, have) in CFG["agv"]) == ((t, j) in CFG["agv"]):
+                    have += 1
+                (vgather if (t, j) in CFG["agv"] else sgather)(R("AG", x, 512 * have), R("AC", C0, C0 + lo),
+                                                               R(O2, 32 * j, 32 * have))
+            vscan(cols("SC"), cols(rr), cols("AG"), ALU.mult, ALU.add)
+        wb = R("TR", 64 + a, 64 + b)
+        mms([(wb, R("OBD"), R(D2, 15 + a * 16, b * 16, 16), True, True)])
+        act(wb, wb, ACT.Exp, scale=-1.0 / 64)
+        vtt(yo, R("SC", 16 * a + 15, 16 * b, 16), wb, ALU.mult)
+        if not last:
+            xb = R("CM", 256 + a, 256 + b)
+            mms([(xb, R("NIB"), R("YS", S * t + a, S * t + b), True, False), (xb, R("IDF"), R("GG", a, b), False, False),
+                 (xb, R("IDF"), yo, False, True)])
+            act(R("AC", C0 + lo + a, C0 + lo + b), xb, ACT.Copy, scale=-0.25)
+        if last or b == S:
+            yo = yo if last else R("YO", S * t, S * t + S)
+            dmas("y", [(lambda: T.yp[:, yo[1]:yo[2]], lambda: A(yo))], [yo], [])
+
+    def nearest(t, c):
+        l0, CH = chunks(t)[c]
+        b0, b1, m0, qf = l0 // 16, (l0 + CH) // 16, scans("MN", c), "QF%d" % (t % 2)
+        old = R("NL", LN, LN + Q0 + NEW[max(t - 1, 0)])
+        lists(t, 1, R("O1", l0, l0 + CH), R("CAND", l0, l0 + CH), old, R(["ST16", "QL0", "QL1", "QL2"][t], b0, b1), True)
+        diffs(t, 1, l0, CH, "D1", R("KK", 0, Q0 + NEW[t]), "O1")
+        kb = keys(c, CH, l0, "CAND", "KC1", "D1")
+        vscan(R("M", m0, m0 + 128, 1, 0, CH), R("RMIN", 0, 128, 1, 0, CH), kb, ALU.add, ALU.min)
+        if c == 2:
+            close()
+        to_list(R("TR", b0, b1), "XP", m0, c, CH)
+        vts(R("K1R", b0, b1), R("TR", b0, b1), MAGIC, -MAGIC, ALU.add, ALU.add)
+        vtt(R(qf, b0, b1), R("TR", b0, b1), R("K1R", b0, b1), ALU.subtract)
+        vts(R("QL%d" % t, b0, b1), R(qf, b0, b1), -float(LN), None, ALU.add)
+
+    def winners(t, c0, c1):
+        l0, l1 = chunks(t)[c0][0], sum(chunks(t)[c1 - 1])
+        b0, b1, qf = l0 // 16, l1 // 16, "QF%d" % (t % 2)
+        ql, lst, nb_ = Q0 + NEW[t], R("QL%d" % t, b0, b1), lambda nm: R(nm, b0, b1)
+        sgather(R("NL", LN + ql + l0, LN + ql + l1), R("NL", LN, LN + ql), lst)
+        if t in CFG["rq"]:
+            vgadd(R("RQ16", l0, l1), R("IOTA", 0, ql), lst, float(LN))
+        if t < 2 or t not in CFG["rq"]:
+            sgather(R("RQF", l0, l1), R("IOTA", 0, ql), lst)
+        if t not in CFG["rq"]:
+            vts(R("RQ16", l0, l1), R("RQF", l0, l1), float(LN), None, ALU.add)
+        e = lambda b: R("E", LN * b + max(16 * b, l0), LN * b + l1)
+        for b in range(b1):
+            vts(e(b), R("RQ16", max(16 * b, l0), l1), R(qf, b, b + 1), R("WL", b, b + 1), ALU.is_equal, ALU.mult)
+        for a in range(0, b1, CFG["eg"]):
+            mms([(R("CM", max(16 * b, l0), l1), R("OBD"), e(b), b == 0, b == b1 - 1)
+                 for b in range(a, min(b1, a + CFG["eg"]))])
+        act(R("CMB", l0, l1), R("CM", l0, l1), ACT.Copy)
+        pick_lists(R("TR", 48 + b0, 48 + b1), R("CMB", l0), l1 - l0)
+        vtt(nb_("WINF"), R("TR", 48 + b0, 48 + b1), nb_("THX"), ALU.is_lt)
+        vtt(nb_("HD"), nb_(qf), nb_("WINF"), ALU.mult)
+        vtt(nb_("HF"), nb_("HD"), nb_("K1R"), ALU.min)
+
+    def dictionary(t, c):
+        l0, CH = chunks(t)[c]
+        b0, b1, mb, mx = l0 // 16, (l0 + CH) // 16, scans("MB", c), scans("MX", c)
         O2, D2 = "O2%d" % (t % 2), "D2%d" % (t % 2)
-        nb_ = lambda nm: R(nm, 0, NB)
+        lists(t, 2, R(O2, l0, l0 + CH), R("LI", l0, l0 + CH), R("NL", LO, LO + Q0 + NEW[t]), R("QL%d" % t, b0, b1),
+              t < RO - 1)
+        diffs(t, 2, l0, CH, D2, R("CE", C0, C0 + CN + NEW[t]), O2)
+        if t == RO - 1:
+            return
+        kb = keys(c, CH, l0, "LI", "KC2", D2)
+        vscan(R("M", mb, mb + 128, 1, 0, CH), R("RMC", 0, 128, 1, 0, CH), kb, ALU.max, ALU.min)
+        vscan(R("M", mx, mx + 128, 1, 0, CH), R("RMAX", 0, 128, 1, 0, CH), kb, ALU.add, ALU.max)
+        if c == 2:
+            ops[-1]["rd"].append(R("M", mb, mb + 128))
+            close()
+        to_list(R("TR", 16 + b0, 16 + b1), "XQ", mb, c, CH)
+
+    def forks(t, c0, c1):
+        l0, l1 = chunks(t)[c0][0], sum(chunks(t)[c1 - 1])
+        ql, nb_ = Q0 + NEW[t], lambda nm: R(nm, l0 // 16, l1 // 16)
+        nnew = R("NL", LN + ql + l0, LN + ql + l1)
+        vtt(nb_("YY"), R("TR", 16 + l0 // 16, 16 + l1 // 16), nb_("HF"), ALU.min)
+        vtt(nb_("TA1"), nb_("YY"), nb_("LANEL"), ALU.max)
+        vcopy(nb_("TA16"), nb_("TA1"))
+        vscat2(R("NL", 0, LN + ql), nb_("TA16"), nnew, R("IOM", LN * t + l0, LN * t + l1), ALU.max)
+        if t < 2:
+            copies([(nnew[:4] + (t, 128, 16), R("RQF", l0, l1, 1, t, 128, 16))])
+
+    def entries(t, c0, c1):
+        l0, l1 = chunks(t)[c0][0], sum(chunks(t)[c1 - 1])
+        np_, ql, nb_ = chunks(t)[c0][1], Q0 + NEW[t], lambda nm: R(nm, l0 // 16, l1 // 16)
+        e8 = lambda nm: R(nm, 8 * c0, 8 * c1, 1, 0, np_)
+        ends = lambda nm: R("M", scans(nm, c0) + 15, scans(nm, c0) + 128 * (c1 - c0), 16, 0, np_)
+        vts(e8("TI"), ends("MX"), -1.0, float(30 * 2048 + 2047), ALU.mult, ALU.add)
+        vts(e8("T2"), e8("TI"), 32767, None, ALU.bitwise_and)
+        vtt(e8("SEL"), ends("MB"), e8("T2"), ALU.min)
+        vts(e8("RI"), e8("SEL"), 11, 15, ALU.arith_shift_right, ALU.bitwise_and)
+        vgtt(R("OHT", 128 * c0, 128 * c1), R("RI", 8 * c0, 8 * c1), R("IU", 0, 8 * (c1 - c0)),
+             R("KPAT", 0, 128 * (c1 - c0)), ALU.is_equal)
+        for c in range(c0, c1):
+            a, cnt = chunks(t)[c]
+            oh, oht = R("TR", 256 + a, 256 + a + cnt), R("OHT", 128 * c, 128 * c + 128, 1, 0, cnt)
+            mms([(oh, oht, R("MD", md[a], md[a] + cnt, 1, 0, cnt), True, False),
+                 (oh, oht, R("MT", 128 * t, 128 * t + cnt, 1, 0, cnt), False, True)])
+        dnew = R("NL", LO + ql + l0, LO + ql + l1)
+        vtt(nb_("HM"), nb_("HD"), nb_("LANEL"), ALU.max)
+        vtt(nb_("HM2"), nb_("HM"), nb_("LANEL"), ALU.add)
+        vtt(nb_("TB1"), nb_("HM2"), nb_("TA1"), ALU.subtract)
+        vcopy(nb_("TB16"), nb_("TB1"))
+        vtt(dnew, R("TR", 256 + l0, 256 + l1), R("LI", l0, l1), ALU.max)
+        vscat(R("NL", LO - LN, LO + ql), nb_("TB16"), dnew)
+
+    def centres(t, c0, c1):
+        l0, l1 = chunks(t)[c0][0], sum(chunks(t)[c1 - 1])
+        b0, lo, nb_ = l0 // 16, CN + NEW[t], lambda nm: R(nm, l0 // 16, l1 // 16)
+        w0 = H if l1 <= S else 0
+        vcopy(nb_("SI"), R("TR", 16 + b0, 16 + l1 // 16))
+        vts(nb_("CI"), nb_("SI"), 2 ** 23 + 2047, None, ALU.bitwise_and)
+        vtt(nb_("U4"), nb_("CI"), nb_("LX"), ALU.max)
+        vts(nb_("CN16"), nb_("U4"), float(C0 - w0 - 2 ** 23), None, ALU.add)
+        sgather(R("CE", C0 + lo + l0, C0 + lo + l1), R("CE", w0, C0 + lo), nb_("CN16"))
+        if l0 < S:
+            sgather(R("GG", l0, min(l1, S)), R("AC", w0, C0 + lo), R("CN16", b0, min(l1, S) // 16), -4.0)
+
+    def guests_in(t):
+        ql, lu, g0 = Q0 + NEW[t], "LU%d" % (t - 1), (t - 1) * GW
+        vscat(R("GI", g0, g0 + GW), R(lu, 0, 12), landing("e", t - 1))
+        copies([(R("KK", ql + S, ql + LN), R("GI", g0, g0 + H)), (R("CE", 0, H), R("GI", g0, g0 + H))])
+        vcopy(R("CF", 10 + t, 11 + t), R(lu, 12, 13))
+        vts(R("LVF", 12, 16), R("LV2", 0, 4), R("CF", 10 + t, 11 + t), None, ALU.is_lt)
+        vtt(R("THX", 12, 16), R("THL", 12, 16), R("LVF", 12, 16), ALU.mult)
+
+    def guests_out(t):
+        sx = R("SX%d" % t, 0, 13)
+        affine(R("WTH", 0, 12), R("WINF", 0, 12), -2.0 ** 23, 2.0 ** 23)
+        vtt(R("NW", 0, 12), R("TR", 16, 28), R("WTH", 0, 12), ALU.is_gt)
+        vscan(R("CUM", 1, 13), R("ONE2", 0, 12), R("NW", 0, 12), ALU.mult, ALU.add)
+        mms([(R("TR", 32, 45), R("TRI"), R("NW", 0, 13), True, False),
+             (R("TR", 32, 45), R("TRB"), R("NW", 0, 13), False, False),
+             (R("TR", 32, 45), R("OBD"), R("CUM", 0, 13), False, True)])
+        vtt(R("GP", 0, 13), R("TR", 32, 45), R("LG", 0, 13), ALU.min)
+        vts(sx, R("GP", 0, 13), 1024.0, None, ALU.add)
+        send(t, "x", sx)
+
+    early = set()
+    for t in range(RO):
+        last, nc = t == RO - 1, len(chunks(t))
+        groups = lambda key: list(zip(CFG[key][t], CFG[key][t][1:] + [nc]))
         if not last:
             load("y", R("CE", H, LN), "xs", S * t, S * t + S)
-        if L == LN:
-            lu = R("LU%d" % (t - 1), 0, 4)
-            sgather(R("CE", 0, H), R("XR%d" % (t - 1)), lu)
-            copy_dma(R("KK", ql + S, ql + LN), R("CE", 0, H))
-            vts(R("LVF", 12, 16), lu, float(S), None, ALU.is_lt)
-            if CFG["wsel"]:
-                vtt(R("THX", 12, 16), R("THL", 12, 16), R("LVF", 12, 16), ALU.mult)
-        nnw, llw = R("NL", LN, LN + ql), R("NL", LO, LO + ql)
-        for c, (l0, CH) in enumerate(chunks(t)):
-            b0, b1 = l0 // 16, (l0 + CH) // 16
-            old = R("NL", LN, LN + max(Q0, ql - LN))
-            if t not in CFG["m1"]:
-                lists(t, 1, c, R("O1", l0, l0 + CH), R("CANDF", l0, l0 + CH), old, R(CL, b0, b1), True)
-            elif c == 0:
-                lists(t, 1, c, R("O1", 0, L), R("CANDF", 0, L), old, nb_(CL), True)
-            diffs(t, 1, c, l0, CH, "D1", 0, R("KK", 0, ql), "O1")
-            kb = keys(t, 1, c, CH, l0, "CANDF", "KC1", "D1", 0)
-            vscan(R("MN", 128 * c, 128 * c + 128, 1, 0, CH), R("RMIN", 0, 128, 1, 0, CH), kb, ALU.add, ALU.min)
-            vgtt(R("XP", 128 * c, 128 * c + 128), R("MN", 128 * c, 128 * c + 128), R("BL"), R("DM"), ALU.mult)
-            mms([(R("TR", b0, b1), R("XP", 128 * c, 128 * c + 128, 1, 0, CH), R("BSEL", 0, b1 - b0, 1, 0, CH), True, True)])
-            vcopy(R("K1I", b0, b1), R("TR", b0, b1))
-            vts(R("QI", b0, b1), R("K1I", b0, b1), 2047, None, ALU.bitwise_and)
-            vcopy(R(QL, b0, b1), R("QI", b0, b1))
-        if not last:
-            if t in CFG["gx"]:
-                act(R("IOM", 0, L), R("IOTA", ql, ql + L), ACT.Copy, scale=R("CF", 9 + t, 10 + t))
-                vgtt(R("SD", FD, FD + L), nnw, nb_(QL), R("IOM", 0, L), ALU.max)
-            else:
-                sgather(R("SD", FD, FD + L), nnw, nb_(QL))
-            for l0, l1 in ([(0, S), (S, LN)] if t in CFG["g3"] and L == LN else [(0, L)]):
-                b0, b1 = l0 // 16, l1 // 16
-                vts(R("QF", b0, b1), R("QI", b0, b1), float(QOFF), None, ALU.add)
-                sgather(R("RQF", l0, l1), R("IOTA", 0, ql), R(QL, b0, b1))
-                vts(R("RQ16", l0, l1), R("RQF", l0, l1), float(QOFF), None, ALU.add)
-                e = lambda b: R("E", LN * b + max(16 * b, l0), LN * b + l1)
-                for b in range(b1):
-                    vts(e(b), R("RQ16", max(16 * b, l0), l1), R("QF", b, b + 1), R("WL", b, b + 1), ALU.is_equal, ALU.mult)
-                for a in range(0, b1, CFG["eg"]):
-                    mms([(R("CM", max(16 * b, l0), l1), R("OBD"), e(b), b == 0, b == b1 - 1)
-                         for b in range(a, min(b1, a + CFG["eg"]))])
-                if CFG["wsel"]:
-                    act(R("CMB", l0, l1), R("CM", l0, l1), ACT.Copy)
-                    pick_lists(R("TR", 48 + b0, 48 + b1), R("CMB", l0), l1 - l0)
-                    vtt(R("WINF", b0, b1), R("TR", 48 + b0, 48 + b1), R("THX", b0, b1), ALU.is_lt)
-                else:
-                    vtt(R("WM", l0, l1), R("CM", l0, l1), R("THR", l0, l1), ALU.is_lt)
-                    vscan(R("WS", l0, l1), R("RSUM", l0, l1), R("WM", l0, l1), ALU.mult, ALU.add)
-                    vtt(R("WINF", b0, b1), R("WS", l0 + 15, l1, 16), R("LVF", b0, b1), ALU.mult)
-            vtt(nb_("HD"), nb_("QF"), nb_("WINF"), ALU.mult)
-            vtt(nb_("HF"), nb_("HD"), nb_("K1I"), ALU.min)
-            vtt(nb_("HM"), nb_("HD"), nb_("LANEL"), ALU.max)
-            if CFG["two"]:
-                vtt(nb_("HM2"), nb_("HM"), nb_("LANEL"), ALU.add)
-            if t < 2:
-                vts(R("WTH", 0, 12), R("WINF", 0, 12), -2.0 ** 23, 2.0 ** 23, ALU.mult, ALU.add)
-            if t in CFG["dg"] + CFG["gx"]:
-                sgather(R("NL", LN + ql, LN + ql + L), nnw, nb_(QL))
-            else:
-                copy_dma(R("NL", LN + ql, LN + ql + L), R("SD", FD, FD + L))
-            copy_dma(R("NL", LN + ql, LN + ql + L, 1, t, 128, 16), R("RQF", 0, L, 1, t, 128, 16))
-            if t not in CFG["gx"]:
-                copy_dma(R("SD", FD, FD + L, 1, 8 + t, 128, 16), R("IOTA", ql, ql + L, 1, 8 + t, 128, 16))
-        for c, (l0, CH) in enumerate(chunks(t)):
-            b0, b1 = l0 // 16, (l0 + CH) // 16
-            lists(t, 2, c, R(O2, l0, l0 + CH), R("LIF", l0, l0 + CH), llw, R(QL, b0, b1), not last)
-            diffs(t, 2, c, l0, CH, D2, PAD, R("CE", C0, C0 + lo), O2)
-            if last:
-                continue
-            kb = keys(t, 2, c, CH, l0, "LIF", "KC2", D2, PAD)
-            m0 = 128 * c
-            vscan(R("MB", m0, m0 + 128, 1, 0, CH), R("RMC", 0, 128, 1, 0, CH), kb, ALU.max, ALU.min)
-            vscan(R("MX", m0, m0 + 128, 1, 0, CH), R("RMAX", 0, 128, 1, 0, CH), kb, ALU.add, ALU.max)
-            vgtt(R("XQ", m0, m0 + 128), R("MB", m0, m0 + 128), R("BL"), R("DM"), ALU.mult)
-            mms([(R("TR", 16 + b0, 16 + b1), R("XQ", m0, m0 + 128, 1, 0, CH), R("BSEL", 0, b1 - b0, 1, 0, CH), True, True)])
-            if CFG["xq"] and c < len(chunks(t)) - 1:
-                continue
-            c0, c1 = (0 if CFG["xq"] else c), c + 1
-            np_ = chunks(t)[c0][1]
-            e8 = lambda nm: R(nm, 8 * c0, 8 * c1, 1, 0, np_)
-            vts(e8("TI"), R("MX", 128 * c0 + 15, 128 * c1, 16, 0, np_), -1.0, float(30 * 2048 + 2047), ALU.mult, ALU.add)
-            vts(e8("T2"), e8("TI"), 32767, None, ALU.bitwise_and)
-            vtt(e8("SEL"), R("MB", 128 * c0 + 15, 128 * c1, 16, 0, np_), e8("T2"), ALU.min)
-            vts(e8("RI"), e8("SEL"), 11, 15, ALU.arith_shift_right, ALU.bitwise_and)
-            ohm = CFG["ohm"] and c1 - c0 == 2
-            if ohm:
-                vgtt(R("OHT", 0, 256), R("RI", 0, 16), R("IU"), R("KPAT", 0, 256), ALU.is_equal)
-            for u in range(c0, c1):
-                a, cnt = chunks(t)[u]
-                if not ohm:
-                    vgtt(R("OHT", 128 * u, 128 * u + 128), R("RI", 8 * u, 8 * u + 8), R("IU", 0, 8), R("KPAT", 0, 128),
-                         ALU.is_equal)
-                oh, oht = R("TR", 256 + a, 256 + a + cnt), R("OHT", 128 * u, 128 * u + 128, 1, 0, cnt)
-                mms([(oh, oht, R("MD", md[a], md[a] + cnt, 1, 0, cnt), True, False),
-                     (oh, oht, R("MT", 128 * t, 128 * t + cnt, 1, 0, cnt), False, True)])
-        if not last:
-            if t == 1:
-                vtt(R("PU1", 0, 4), R("QI", 12, 16), R("CLF", 0, 4), ALU.subtract)
-                vtt(R("PU2", 0, 4), R("PU1", 0, 4), R("LVF", 12, 16), ALU.mult)
-                vtt(R("PU3", 0, 4), R("PU2", 0, 4), R("CLF", 0, 4), ALU.add)
-                vcopy(R(QL, 12, 16), R("PU3", 0, 4))
-            sel = R("TR", 16, 16 + NB)
-            vtt(nb_("YY"), sel, nb_("HF"), ALU.min)
-            if CFG["two"]:
-                vtt(nb_("TA1"), nb_("YY"), nb_("LANEL"), ALU.max)
-                vcopy(nb_("TA16"), nb_("TA1"))
-                vscat(R("NL", 0, LN + ql), nb_("TA16"), R("SD", FD, FD + L))
-                vtt(nb_("TB1"), nb_("HM2"), nb_("TA1"), ALU.subtract)
-                vcopy(nb_("TB16"), nb_("TB1"))
-                vtt(R("SD", 0, L), R("TR", 256, 256 + L), R("LIF", 0, L), ALU.max)
-                vscat(R("NL", LO - LN, LO + ql), nb_("TB16"), R("SD", 0, L))
-            else:
-                vts(nb_("FF"), nb_("YY"), 0.0, float(LO - LN), ALU.is_gt, ALU.mult)
-                vtt(nb_("TB1"), nb_("LANE4"), nb_("FF"), ALU.add)
-                vts(nb_("TB16"), nb_("TB1"), 0.25, None, ALU.mult)
-                vtt(R("SD", 0, L), R("TR", 256, 256 + L), R("LIF", 0, L), ALU.max)
-                sgather(R("DAT", 0, L), R("SD", 0, FD + L), nb_("TB16"))
-                vtt(nb_("TA1"), nb_("HM"), nb_("FF"), ALU.subtract)
-                vcopy(nb_("TA16"), nb_("TA1"))
-                vscat(R("NL", 0, LO + ql), nb_("TA16"), R("DAT", 0, L))
-            copy_dma(R("NL", LO + ql, LO + ql + L), R("SD", 0, L))
-            if t < 2:
-                sx, gp, g0 = R("SX%d" % t, 0, 4), R("GP0", 0, 12), t * (GW + 64)
-                vtt(R("NW", 0, 12), R("TR", 16, 28), R("WTH", 0, 12), ALU.is_gt)
-                vscan(R("CUM", 1, 12), R("ONE2", 0, 11), R("NW", 0, 11), ALU.mult, ALU.add)
-                mms([(R("TR", 32, 44), R("TRI"), R("NW", 0, 12), True, False),
-                     (R("TR", 32, 44), R("TRB"), R("NW", 0, 12), False, False),
-                     (R("TR", 32, 44), R("OBD"), R("CUM", 0, 12), False, True)])
-                vtt(R("GP", 0, 12), R("TR", 32, 44), R("LG", 0, 12), ALU.min)
-                vts(gp, R("GP", 0, 12), 1024.0, None, ALU.add)
-                vscat(R("GI", g0, g0 + GW), gp, R("IOTA", 0, S))
-                pick_lists(R("TR", 44, 48), R("GI", g0), H)
-                vcopy(sx, R("TR", 44, 48))
-                send(t, "x", sx)
-            vcopy(nb_("SI"), sel)
-            vts(nb_("CI"), nb_("SI"), 2 ** 23 + 2047, None, ALU.bitwise_and)
-            vtt(nb_("U4"), nb_("CI"), nb_("LX"), ALU.max)
-            vts(nb_("CN16"), nb_("U4"), float(C0 - 2 ** 23), None, ALU.add)
-            sgather(R("CE", C0 + lo, C0 + lo + L), R("CE", 0, C0 + lo), nb_("CN16"))
-            if CFG["pe4"] or not CFG["ga"]:
-                sgather(R("GG"), R("AC", 0, C0 + lo), R("CN16", 0, 12))
-        rr = "RR%d" % (t % 2)
-        quarter = not last and not CFG["pe4"]
-        j = 0
-        while j < 6:
-            m = 1
-            while m < CFG["agm"] and (j + m) % 3 and ((t, j) in CFG["agv"]) == ((t, j + m) in CFG["agv"]):
-                m += 1
-            (vgather if (t, j) in CFG["agv"] else sgather)(R("AG", 512 * j, 512 * (j + m)), R("AC", C0, C0 + lo),
-                                                           R(O2, 32 * j, 32 * (j + m)))
-            j += m
-        both = (t, 0) in CFG["cx"] and (t, 1) in CFG["cx"] and t not in CFG["split"]
-        lst, fb = [], lease("F1")
-        for h in range(2):
-            if (t, h) not in CFG["cx"]:
-                continue
-            srcs = [(D2, HL * h, HL)] + [(D2 + "R", l, cnt) for l, cnt in runs(t, 2, HL * h, HL)]
-            for u, rows in enumerate(DIFF_ROWS):
-                grp = [(R(fb, 2 * l + u, 2 * (l + cnt), 2), R(z, 7 - r, 135 - r),
-                        R(nm, PAD + l * 16 + k, PAD + (l + cnt) * 16, 16)) for nm, l, cnt in srcs for k, z, r in rows]
-                if u == 0:
-                    grp.append((grp[0][0], R("RZ", 0, 128, 1, 0, 1), R("ONE2", 0, HL, 1, 0, 1)))
-                lst += [m + (i == 0, i == len(grp) - 1) for i, m in enumerate(grp)]
-            if both and h == 0:
-                continue
-            a, b = (0 if both else S * h), S * h + S
-            for i in range(0, len(lst), CFG["dfm"]):
-                mms(lst[i:i + CFG["dfm"]])
-                ops[-1].update(group=int(i == 0), starts=i == 0, wr=[R(fb, a, b)])
-                if i == 0:
-                    ops[-1]["rd"] = ops[-1]["rd"] + [m[2] for m in lst]
-            act(R("RH", a, b), R(fb, a, b), ACT.Exp, scale=1.0 / 64)
-            act(R(fb, a, b, 1, 64), R(fb, a, b, 1, 64), ACT.Exp, scale=1.0 / 64)
-            vtt(R("RH", a, b, 1, 64), R(fb, a, b, 1, 64), R("RH", a, b, 1, 64), ALU.subtract)
-            ops[-1]["group"] = -1
-            lst, fb = [], lease("F1")
-        for j in range(6):
-            bank = "R%d" % (j % 2)
-            h, a = j // 3, PAD + 512 * j
-            cols = lambda nm: R(nm, 512 * j, 512 * j + 512)
-            if (t, h) in CFG["cx"]:
-                mms([(R(bank, r, 512, 8), R("RS", 128 * r, 128 * r + 128), R("RH", 64 * j, 64 * j + 64), True, True)
-                     for r in range(8)])
-                vscan(cols("SC"), R(bank), cols("AG"), ALU.mult, ALU.add)
-            else:
-                lst = []
-                for nm in [D2] + ([D2 + "R"] if signed(t, 2, j) else []):
-                    lst += [(R(bank), R("OBD"), R(nm, a, a + 512), nm == D2, False),
-                            (R(bank, 1), R("NBD"), R(nm, a, a + 511), False, False)]
-                mms(lst + [(R(bank, 0, 512, 16), R("ONE2", 0, 128, 1, 0, 2), R("RB", 0, 32, 1, 0, 2), False, True)])
-                act(cols(rr), R(bank), ACT.Exp, scale=1.0 / 64)
-                vscan(cols("SC"), cols(rr), cols("AG"), ALU.mult, ALU.add)
-        for a, b in ([(0, HL), (HL, S)] if t in CFG["split"] else [(0, S)]):
-            wb, last_row = R("TR", 64 + a, 64 + b), R("SC", 16 * a + 15, 16 * b, 16)
-            srcs = [(D2, a, b - a)] + [(D2 + "R", l, cnt) for l, cnt in runs(t, 2, a, b - a)]
-            mms([(R("TR", 64 + l, 64 + l + cnt), R("OBD"), R(nm, PAD + 15 + l * 16, PAD + (l + cnt) * 16, 16),
-                  i == 0, i == len(srcs) - 1) for i, (nm, l, cnt) in enumerate(srcs)])
-            act(wb, wb, ACT.Exp, bias=R("MCOL", 1, 2) if quarter else 0.0, scale=-1.0 / 64)
-            yo, xb = R("YO", S * t + a, S * t + b), R("CM", 256 + a, 256 + b)
-            ys, gg, an = R("YS", S * t + a, S * t + b), R("GG", a, b), R("AC", C0 + lo + a, C0 + lo + b)
-            if quarter and CFG["ga"]:
-                vtt(wb, last_row, wb, ALU.mult)
-                vtt(R("P4", a, b), R("Y4", S * t + a, S * t + b), wb, ALU.subtract)
-                act(yo, wb, ACT.Copy, scale=4.0)
-                vgtt(an, R("AC", 0, C0 + lo), R("CN16", a // 16, b // 16), R("P4", a, b), ALU.add)
-            elif quarter:
-                vtt(R("P4", a, b), last_row, wb, ALU.mult)
-                mms([(xb, R("I4"), ys, True, False), (xb, R("IDF"), gg, False, True)])
-                vtt(an, xb, R("P4", a, b), ALU.subtract)
-                act(yo, R("P4", a, b), ACT.Copy, scale=4.0)
-            else:
-                vtt(yo, last_row, wb, ALU.mult)
-                if not last:
-                    mms([(xb, R("I4"), ys, True, False), (xb, R("IDF"), gg, False, False), (xb, R("I4F"), yo, False, True)])
-                    act(an, xb, ACT.Copy)
-            dma("y", (lambda r=yo: T.yp[:, r[1]:r[2]]), (lambda i=yo: A(i)), [yo], [])
+        if t in (1, 2):
+            guests_in(t)
+        for c in range(nc):
+            if (t, c) not in early:
+                nearest(t, c)
+        for c0, c1 in ([] if last else groups("gw")):
+            winners(t, c0, c1)
+        for c in range(nc):
+            dictionary(t, c)
+        if t == 1:
+            vtt(R("PU1", 0, 4), R("QF1", 12, 16), R("CLF", 0, 4), ALU.subtract)
+            vtt(R("PU2", 0, 4), R("PU1", 0, 4), R("LVF", 12, 16), ALU.mult)
+            vtt(R("PU3", 0, 4), R("PU2", 0, 4), R("CLF", 0, 4), ALU.add)
+            vts(R("QL1", 12, 16), R("PU3", 0, 4), -float(LN), None, ALU.add)
         if t < 2:
-            sgather(R("SA%d" % t), R("AC", C0 + lo, C0 + lo + S + 8), R("SX%d" % t, 0, 4))
-            send(t, "a", R("SA%d" % t))
-    return ops, neng
+            guests_out(t)
+        if not last:
+            for c0, c1 in groups("gf"):
+                forks(t, c0, c1)
+                for c in range(c0, c1):
+                    if c == 0 or (c == 1 and c1 < nc and sum(chunks(t + 1)[1]) == S):
+                        nearest(t + 1, c)
+                        early.add((t + 1, c))
+            for c0, c1 in groups("ge"):
+                entries(t, c0, c1)
+            for c0, c1 in groups("gc"):
+                centres(t, c0, c1)
+        for a, cnt, form in CFG["pieces"][t]:
+            predict(t, a, cnt, form)
+        if t < 2:
+            a, b = C0 + CN + NEW[t], C0 + CN + NEW[t + 1] + S
+            send(t, "a", R("AC", a, a + S))
+            vscat(R("AC", b, b + GW), R("LU%d" % t, 0, 12), landing("a", t))
+    return ops
 
 
 def price(ops, c):
@@ -772,13 +751,17 @@ def price(ops, c):
         elif w[0] == "tensor":
             out.append((w[1] * c["pe"], 40.0))
         elif w[0] == "pool":
-            out.append((w[1] * c["f"], 0.0))
+            out.append((w[1] * c["f"] * c.get("gp", 1.0), 0.0))
         elif w[0] == "dma":
-            out.append((w[1], c["dl"] + w[2]))
+            move = w[2] * c["dl"] / 40 + w[3] / 600
+            if o["eng"] == "y":
+                out.append((max(60 * w[1], move), c["dl"] - 100))
+            else:
+                out.append((1000 * c.get("fs", 1.0) if o["eng"] == "g" else 60, c["dl"] + move))
         elif w[0] == "send":
-            out.append((w[1], 0.0))
+            out.append((w[1] * c.get("fs", 1.0), 0.4 * c["rl"]))
         else:
-            out.append((0.0, c["rl"] * w[1]))
+            out.append((0.0, c["rl"] * (w[1] - 0.4)))
     return out
 
 
@@ -807,8 +790,8 @@ def one_pass(ops, cost, preds, succ, pri, back):
     sem, look = CFG["cost"]["sem"], CFG["look"]
     left = [len(p) for p in preds]
     rdy = [cost[i][1] if back else 0.0 for i in range(n)]
-    start, fin = [0.0] * n, [0.0] * n
-    free, used, opened = {}, {b: {} for b in _PS}, set()
+    fin = [0.0] * n
+    free, used, opened = {}, {b: {} for b in LINES}, set()
     ready = [i for i in range(n) if left[i] == 0]
     order = []
     while ready:
@@ -827,7 +810,6 @@ def one_pass(ops, cost, preds, succ, pri, back):
         end = est[pick] + cost[pick][0]
         if e:
             free[e] = end
-        start[pick] = est[pick]
         fin[pick] = end + (0.0 if back else cost[pick][1])
         for b in ops[pick]["banks"]:
             used[b][e] = fin[pick]
@@ -841,168 +823,15 @@ def one_pass(ops, cost, preds, succ, pri, back):
             left[k] -= 1
             if left[k] == 0:
                 ready.append(k)
-    return order, start, fin
+    return order, fin
 
 
-def marks(order, eng, banks, n):
-    last, used, out = [n] * 6, [[n] * 3 for _ in _PS], []
-    for p, i in enumerate(order):
-        if p % 32 == 0:
-            out.append((last[:], [row[:] for row in used]))
-        last[eng[i]] = i
-        for b in banks[i]:
-            used[b][eng[i]] = i
-    return out
-
-
-def replay(order, eng, banks, fig, mark, p0=0, old=None, p1=0, limit=1e30):
-    cost, lat, deps, sem, sinks, tail = fig
-    n = len(order)
-    end, why = (old[3][:], old[2][:]) if old else ([0.0] * (n + 1), [n] * n)
-    last, used = mark[p0 // 32][0][:], [row[:] for row in mark[p0 // 32][1]]
-    left = p1 - p0 + p0 % 32 + 80 if old else n
-    for i in order[p0 - p0 % 32:]:
-        left -= 1
-        if left < 0:
-            break
-        e = eng[i]
-        w = last[e] if e < 5 else n
-        r = end[w]
-        for j, x in deps[i]:
-            x += end[j]
-            if x > r:
-                r, w = x, j
-        for b in banks[i]:
-            row = used[b]
-            for e2 in (0, 1, 2):
-                j = row[e2]
-                if e2 != e and j < n and end[j] + lat[j] + sem > r:
-                    r, w = end[j] + lat[j] + sem, j
-            row[e] = i
-        r += cost[i]
-        if r != end[i]:
-            if r + tail[i] > limit:
-                return None
-            end[i] = r
-            if left < 80:
-                left = 80
-        last[e] = i
-        why[i] = w
-    top = max(sinks, key=lambda i: end[i] + lat[i])
-    return end[top] + lat[top], top, why, end
-
-
-def nested(ops, order):
-    opened = set()
-    for i in order:
-        o = ops[i]
-        if o["starts"] and o["banks"][0] in opened:
-            return False
-        if o["group"] > 0:
-            opened.add(o["banks"][0])
-        elif o["group"] < 0:
-            opened.discard(o["banks"][0])
-    return True
-
-
-def shift(order, preds, a, b, forward):
-    pa, pb = order.index(a), order.index(b)
-    seg = order[pa:pb + 1]
-    if forward:
-        moved = {a}
-        for k in seg[1:]:
-            if preds[k] & moved:
-                moved.add(k)
-        if b in moved:
-            return None
-        return order[:pa] + [k for k in seg if k not in moved] + [k for k in seg if k in moved] + order[pb + 1:]
-    moved, need = {b}, set(preds[b])
-    for k in reversed(seg[:-1]):
-        if k in need:
-            moved.add(k)
-            need |= preds[k]
-    if a in moved:
-        return None
-    return order[:pa] + [k for k in seg if k in moved] + [k for k in seg if k not in moved] + order[pb + 1:]
-
-
-def tabu(ops, order, eng, banks, preds, fig, draw):
-    cost, lat, deps, sem = fig[:4]
+def improve(ops, order, moves, slack):
     n = len(ops)
-    best, kept, banned = None, order, {}
-    for it in range(CFG["tabu"]):
-        total, top, why, end = replay(order, eng, banks, fig, marks(order[:1], eng, banks, n))
-        if best is None or total < best:
-            best, kept = total, order
-        ready, tail, rest = [0.0] * n, [0.0] * (n + 1), lat[:]
-        before, after, last, used = [n] * n, [n] * n, [n] * 6, [[n] * 3 for _ in _PS]
-        links = []
-        for i in order:
-            e, ins = eng[i], deps[i]
-            for b in banks[i]:
-                ins = ins + [(j, lat[j] + sem) for e2, j in enumerate(used[b]) if e2 != e and j < n]
-                used[b][e] = i
-            links.append(ins)
-            ready[i] = max([end[j] + x for j, x in ins] + [0.0])
-            if e < 5:
-                before[i] = last[e]
-                if last[e] < n:
-                    after[last[e]] = i
-                last[e] = i
-        for i, ins in zip(reversed(order), reversed(links)):
-            tail[i] = cost[i] + max(rest[i], tail[after[i]])
-            for j, x in ins:
-                if x + tail[i] > rest[j]:
-                    rest[j] = x + tail[i]
-        runs, i = [[top]], top
-        while why[i] < n:
-            if why[i] == before[i]:
-                runs[-1].append(why[i])
-            else:
-                if why[i] not in preds[i]:
-                    runs.append([i, why[i]])
-                runs.append([why[i]])
-            i = why[i]
-        moves = []
-        for run in runs:
-            run.reverse()
-            m = len(run)
-            if m == 2 and eng[run[0]] != eng[run[1]]:
-                moves += [(total * (0.99 + 0.02 * draw(100) / 100), run[0], run[1], f) for f in (True, False)]
-                continue
-            for _ in range(min(m * (m - 1) // 2, CFG["tries"])):
-                x = draw(m - 1)
-                y = x + 1 + draw(min(m - 1 - x, CFG["reach"]))
-                for forward in (True, False):
-                    seq = run[x + 1:y + 1] + [run[x]] if forward else [run[y]] + run[x:y]
-                    r, heads = end[before[run[x]]], []
-                    for k in seq:
-                        r = max(r, ready[k])
-                        heads.append(r)
-                        r += cost[k]
-                    q, est = tail[after[run[y]]], 0.0
-                    for k, h in zip(reversed(seq), reversed(heads)):
-                        q = cost[k] + max(q, rest[k])
-                        est = max(est, h + q)
-                    moves.append((est + draw(50), run[x], run[y], forward))
-        moves.sort()
-        for est, a, b, forward in moves:
-            if banned.get((b, a), -1) >= it and est >= best:
-                continue
-            new = shift(order, preds, a, b, forward)
-            if new and nested(ops, new):
-                order = new
-                banned[a, b] = banned[b, a] = it + 8 + draw(12)
-                break
-        else:
-            break
-    return kept
-
-
-def improve(ops, order):
-    n = len(ops)
-    eng = ["vstgy".index(o["eng"]) if o["eng"] else 5 for o in ops]
-    banks = [[_PS.index(b) for b in o["banks"]] for o in ops]
+    order = list(order)
+    eng = ["vstgy".index(o["eng"]) if o["eng"] else 5 + i for i, o in enumerate(ops)] + [-99]
+    lines = [[eng[i]] + [-1 - LINES.index(b) for b in o["banks"]] for i, o in enumerate(ops)]
+    banked = [l[1:] for l in lines]
     preds, above = [], []
     for o in ops:
         far = 0
@@ -1010,90 +839,286 @@ def improve(ops, order):
             far |= above[j]
         preds.append(set(j for j in o["deps"] if not far >> j & 1))
         above.append(far | sum(1 << j for j in preds[-1]))
-    special = set(i for i in range(n) if ops[i]["starts"] or ops[i]["group"])
-    figs = []
+    starts, group = [o["starts"] for o in ops], [o["group"] for o in ops]
+    special = set(i for i in range(n) if starts[i] or group[i])
+    pos = [0] * n + [-1]
+    before, after = [{} for _ in range(n + 1)], [{} for _ in range(n + 1)]
+
+    def link(seg, p0, first, final):
+        last = dict(first)
+        for p, i in enumerate(seg):
+            pos[i] = p0 + p
+            for l in lines[i]:
+                j = last.get(l, n)
+                before[i][l], after[j][l], last[l] = j, i, i
+        for l, j in last.items():
+            k = final.get(l, n)
+            after[j][l], before[k][l] = k, j
+
+    win, figs = [0, n], []
     for c in CFG["figs"]:
-        cost = price(ops, c)
-        deps = [[(j, cost[j][1] + (c["sem"] if ops[i]["deps"][j] else 0.0)) for j in sorted(preds[i])] for i in range(n)]
-        tail = [x[1] for x in cost]
-        for i in range(n - 1, -1, -1):
-            for j, y in deps[i]:
-                tail[j] = max(tail[j], y + cost[i][0] + tail[i])
-        figs.append(([x[0] for x in cost], [x[1] for x in cost], deps, c["sem"],
-                     sorted(set(range(n)) - set().union(*preds)), tail))
+        pr = price(ops, c)
+        cost, lat = [x[0] for x in pr] + [0.0], [x[1] for x in pr] + [0.0]
+        ins = [[(j, lat[j] + (c["sem"] if ops[i]["deps"][j] else 0.0)) for j in sorted(preds[i])] for i in range(n)]
+        outs = [[] for _ in range(n)]
+        for i in range(n):
+            for j, y in ins[i]:
+                outs[j].append((i, y))
+        figs.append((cost, lat, ins, outs, [y + c["sem"] for y in lat[:n]] + [0.0], [0.0] * (n + 1), [0.0] * (n + 1)))
+
+    def heads(f, p, stop):
+        cost, lat, ins, outs, hand, end, rest = f
+        top = win[1]
+        while p < top and p <= stop:
+            i = order[p]
+            p += 1
+            e, b = eng[i], before[i]
+            r = end[b[e]]
+            for j, y in ins[i]:
+                y += end[j]
+                if y > r:
+                    r = y
+            for l in banked[i]:
+                j = b[l]
+                if eng[j] != e and end[j] + hand[j] > r:
+                    r = end[j] + hand[j]
+            r += cost[i]
+            if r != end[i]:
+                end[i] = r
+                for k, y in outs[i]:
+                    if pos[k] > stop:
+                        stop = pos[k]
+                for k in after[i].values():
+                    if pos[k] > stop:
+                        stop = pos[k]
+
+    def tails(f, p, stop):
+        cost, lat, ins, outs, hand, end, rest = f
+        low = win[0]
+        while p >= low and p >= stop:
+            i = order[p]
+            p -= 1
+            e, a = eng[i], after[i]
+            r = rest[a[e]]
+            if lat[i] > r:
+                r = lat[i]
+            for k, y in outs[i]:
+                y += rest[k]
+                if y > r:
+                    r = y
+            for l in banked[i]:
+                k = a[l]
+                if k < n and eng[k] != e and rest[k] + hand[i] > r:
+                    r = rest[k] + hand[i]
+            r += cost[i]
+            if r != rest[i]:
+                rest[i] = r
+                for j, y in ins[i]:
+                    if pos[j] < stop:
+                        stop = pos[j]
+                for j in before[i].values():
+                    if j < n and pos[j] < stop:
+                        stop = pos[j]
+
+    tmp = [0.0] * (n + 1)
+
+    def through(f, seg, pa, pb, first, final, limit):
+        cost, lat, ins, outs, hand, end, rest = f
+        last, top = {}, 0.0
+        for i in seg:
+            e = eng[i]
+            r = tmp[last[e]] if e in last else end[first[e]]
+            last[e] = i
+            for j, y in ins[i]:
+                y += tmp[j] if pos[j] >= pa else end[j]
+                if y > r:
+                    r = y
+            for l in banked[i]:
+                if l in last:
+                    j = last[l]
+                    y = tmp[j]
+                else:
+                    j = first[l]
+                    y = end[j]
+                last[l] = i
+                if eng[j] != e and y + hand[j] > r:
+                    r = y + hand[j]
+            r += cost[i]
+            tmp[i] = r
+            z = lat[i]
+            for k, y in outs[i]:
+                if pos[k] > pb and y + rest[k] > z:
+                    z = y + rest[k]
+            if r + z > top:
+                top = r + z
+                if top > limit:
+                    return None
+        for l, j in last.items():
+            k = final[l]
+            y = tmp[j] + rest[k] + (hand[j] if l < 0 and k < n and eng[k] != eng[j] else 0.0)
+            if y > top:
+                top = y
+        return None if top > limit else top
+
+    def waits(m, part):
+        cost, lat, ins, outs, hand, end, rest = figs[m]
+        out, total = [], span[m] - 0.01
+        for i in [i for i in part if end[i] - cost[i] + rest[i] > total]:
+            r = end[i] - cost[i] - 0.01
+            for l, j in before[i].items():
+                if (pos[j] >= win[0] and j not in preds[i]
+                        and end[j] + (hand[j] if l < 0 and eng[j] != eng[i] else 0.0) > r):
+                    out.append((j, i, m))
+        return out
+
+    def pause(f, total, i, back):
+        cost, lat, ins, outs, hand, end, rest = f
+        e, out, k, need = eng[i], [], i, cost[i] * draw(100) / 100.0
+        if back:
+            late = total - max([y + rest[j] for j, y in outs[i]] + [lat[i]]) - cost[i]
+            for _ in range(CFG["far"]):
+                k = after[k][e]
+                if k == n or end[k] > late + cost[i]:
+                    break
+                j = after[k][e]
+                if j < n and end[j] - cost[j] - end[k] >= need:
+                    out.append(k)
+        else:
+            soon = max([y + end[j] for j, y in ins[i]] + [0.0])
+            for _ in range(CFG["far"]):
+                k = before[k][e]
+                if k == n or end[k] < soon:
+                    break
+                if end[k] - cost[k] - max(end[before[k][e]], soon) >= need:
+                    out.append(k)
+        return out[draw(len(out))] if out else None
+
+    def nests(seg, first):
+        opened = {}
+        for i in seg:
+            if i in special:
+                l = lines[i][1]
+                if l not in opened:
+                    j = first[l]
+                    while j < n and not (group[j] and lines[j][1] == l):
+                        j = before[j][l]
+                    opened[l] = j < n and group[j] > 0
+                if starts[i] and opened[l]:
+                    return False
+                if group[i]:
+                    opened[l] = group[i] > 0
+        return True
+
     x = [CFG["seed"]]
 
     def draw(m):
         x[0] = (x[0] * 1103515245 + 12345) % 2147483648
         return (x[0] >> 8) % m
 
-    def waits(y):
-        i, why, out = y[1], y[2], []
-        while why[i] < n:
-            if why[i] not in preds[i]:
-                out.append((why[i], i))
-            i = why[i]
-        return out
+    def longest():
+        part = order[win[0]:win[1]]
+        span[:] = [max([end[i] - cost[i] + rest[i] for i in part]) for cost, lat, ins, outs, hand, end, rest in figs]
+        return sum(y * z for y, z in zip(span, scale)), sum([waits(m, part) for m in range(len(figs))], [])
 
-    mark = marks(order, eng, banks, n)
-    res = [replay(order, eng, banks, f, mark) for f in figs]
-    scale = [1.0 / y[0] for y in res]
-    cur = best = float(len(res))
-    kept, edges = order, sum(map(waits, res), [])
-    for it in range(CFG["moves"]):
-        if not edges:
-            break
-        a, b = edges[draw(len(edges))]
-        pa, pb = order.index(a), order.index(b)
-        kind = draw(3)
-        if kind:
-            if kind == 2:
-                b, pb, pa = a, pa, max(0, pa - 1 - draw(CFG["reach"]))
-            else:
-                pa = max(0, pa - (draw(12) if draw(3) == 0 else 0))
-            moved, need = {b}, set(preds[b])
-            for k in reversed(order[pa:pb]):
-                if k in need:
-                    moved.add(k)
-                    need |= preds[k]
-            if a in moved and kind == 1:
-                continue
-            seg = order[pa:pb + 1]
-            new = order[:pa] + [k for k in seg if k in moved] + [k for k in seg if k not in moved] + order[pb + 1:]
-        else:
-            pb = min(n - 1, pb + (draw(CFG["reach"]) if draw(2) else 0))
-            seg, moved = order[pa:pb + 1], {a}
-            for k in seg[1:]:
-                if preds[k] & moved:
-                    moved.add(k)
-            if b in moved:
-                continue
-            new = order[:pa] + [k for k in seg if k not in moved] + [k for k in seg if k in moved] + order[pb + 1:]
-        if moved & special and not nested(ops, [k for k in new if k in special]):
+    def afresh():
+        link(order, 0, {}, {})
+        win[:] = [0, n]
+        for f in figs:
+            heads(f, 0, n)
+            tails(f, n - 1, 0)
+
+    scale = [0.9 / sum(f[0][i] for i in range(n) if eng[i] == 0) for f in figs]
+    reach, cap, it, edges, kept, span = CFG["reach"], CFG["cap"], 0, [], None, []
+    while it < moves:
+        if it % CFG["stay"] < CFG["tries"] or not edges:
+            if kept:
+                order[win[0]:win[1]] = kept
+            afresh()
+            win[0] = max(0, min(n - CFG["window"], draw(n) - CFG["window"] // 2))
+            win[1] = min(n, win[0] + CFG["window"])
+            best, edges = longest()
+            kept = order[win[0]:win[1]]
+            it += CFG["tries"]
             continue
-        allow = CFG["slack"] * draw(1000) / 1000.0 * (1.0 - it / CFG["moves"])
-        rs, s = [], cur
-        for f, y, z in zip(figs, res, scale):
-            rs.append(replay(new, eng, banks, f, mark, pa, y, pb, y[0] + (allow + 0.002) / z))
-            if rs[-1] is None:
-                break
-            s += (rs[-1][0] - y[0]) * z
-        if s < cur + allow and rs[-1]:
-            res = [replay(new, eng, banks, f, mark, pa, y, n) for f, y in zip(figs, rs)]
-            cur = s = sum(y[0] * z for y, z in zip(res, scale))
-            order, edges = new, sum(map(waits, res), [])
-            mark = marks(order, eng, banks, n)
+        allow = slack * draw(1000) / 1000.0 * (1.0 - it % CFG["stay"] / CFG["stay"]) * (1.2 - it / moves)
+        pick = None
+        for _ in range(CFG["tries"]):
+            it += 1
+            a, b, m = edges[draw(len(edges))]
+            pa, pb = pos[a], pos[b]
+            kind = draw(3)
+            if draw(100) < CFG["aim"]:
+                k = pause(figs[m], span[m], a, draw(2))
+                if k is None or not win[0] <= pos[k] < win[1]:
+                    continue
+                if pos[k] < pa:
+                    kind, b, pb, pa = 3, a, pa, pos[k]
+                else:
+                    kind, b, pb = -1, n, pos[k]
+            if kind > 0:
+                if kind == 3:
+                    pass
+                elif kind == 2:
+                    b, pb, pa = a, pa, max(win[0], pa - 1 - draw(reach))
+                else:
+                    pa = max(win[0], pa - (draw(12) if draw(3) == 0 else 0))
+                moved, need, old = {b}, set(preds[b]), order[pa:pb + 1]
+                for k in reversed(old):
+                    if k in need:
+                        moved.add(k)
+                        need |= preds[k]
+                if a in moved and kind == 1:
+                    continue
+                seg = [k for k in old if k in moved] + [k for k in old if k not in moved]
+            else:
+                pb = min(win[1] - 1, pb + (draw(reach) if draw(2) and kind == 0 else 0))
+                old, moved = order[pa:pb + 1], {a}
+                for k in old:
+                    if preds[k] & moved:
+                        moved.add(k)
+                if b in moved:
+                    continue
+                seg = [k for k in old if k not in moved] + [k for k in old if k in moved]
+            first, final = {}, {}
+            for k in old:
+                for l in lines[k]:
+                    if l not in first:
+                        first[l] = before[k][l]
+                    final[l] = after[k][l]
+            if moved & special and not nests(seg, first):
+                continue
+            s = 0.0
+            for f, y, z in zip(figs, span, scale):
+                top = through(f, seg, pa, pb, first, final, y + (allow + cap) / z)
+                if top is None:
+                    break
+                s += max((top - y) * z, -cap)
+            else:
+                if s < allow:
+                    allow, pick = s, (seg, pa, pb, first, final)
+        if pick:
+            seg, pa, pb, first, final = pick
+            order[pa:pb + 1] = seg
+            link(seg, pa, first, final)
+            far = max(pos[k] for k in final.values())
+            near = min(pos[k] if k < n else pa for k in first.values())
+            for f in figs:
+                heads(f, pa, max(pb, far))
+                tails(f, pb, min(pa, near))
+            s, edges = longest()
             if s < best:
-                best, kept = s, new
-    return kept, replay(kept, eng, banks, figs[0], mark)[3]
+                best, kept = s, order[win[0]:win[1]]
+    order[win[0]:win[1]] = kept
+    afresh()
+    return longest()[0], order, figs[0][5]
 
 
-PLAN = {}
+PLAN = []
 
 
 def schedule(ops):
     n = len(ops)
-    if n not in PLAN:
+    if not PLAN:
         cost = price(ops, CFG["cost"])
         preds = [list(o["deps"]) for o in ops]
         succ = [[] for _ in ops]
@@ -1103,32 +1128,33 @@ def schedule(ops):
         pri = [0.0] * n
         for i in range(n - 1, -1, -1):
             pri[i] = sum(cost[i]) + CFG["cost"]["sem"] + max([pri[k] for k in succ[i]] + [0.0])
-        best = None
+        plans = []
         for it in range(CFG["iters"]):
-            order, start, fin = one_pass(ops, cost, preds, succ, pri, False)
-            if best is None or max(fin) < best[0]:
-                best = (max(fin), order, start)
-            if max(fin) < best[0] * (1 + CFG["back"]):
+            order, fin = one_pass(ops, cost, preds, succ, pri, False)
+            plans = sorted(plans + [(max(fin), order)])
+            if max(fin) < plans[0][0] * (1 + CFG["back"]):
                 base = fin
-            pri = one_pass(ops, cost, succ, preds, base, True)[2]
+            pri = one_pass(ops, cost, succ, preds, base, True)[1]
             x = CFG["seed"] * 7919 + it
             for i in range(n):
                 x = (x * 1103515245 + 12345) % 2147483648
                 pri[i] += CFG["noise"] * x / 2147483648
-        PLAN[n] = (best[0],) + improve(ops, best[1])
-    seen = {b: {} for b in _PS}
-    for i in PLAN[n][1]:
+        for keep, moves, slack in CFG["rounds"]:
+            plans = sorted([improve(ops, p[1], moves, slack) for p in plans[:keep]] + [p for p in plans if len(p) > 2])
+        PLAN.extend(plans[0][1:])
+    seen = {b: {} for b in LINES}
+    for i in PLAN[0]:
         o = ops[i]
-        o["t0"] = PLAN[n][2][i]
+        o["t0"] = PLAN[1][i]
         for b in o["banks"]:
             for e, j in seen[b].items():
                 if e != o["eng"]:
                     o["deps"][j] = True
             seen[b][o["eng"]] = i
-    return PLAN[n][1]
+    return PLAN[0]
 
 
-def emit(g, T, ops, order, neng):
+def emit(g, T, ops, order):
     queue = {"v": g.vector, "s": g.scalar, "t": g.tensor, "g": g, "y": g.sync}
     csem = {"v": "sv", "s": "ss", "t": "st_", "g": "sg"}
     needed = set()
@@ -1160,11 +1186,7 @@ def emit(g, T, ops, order, neng):
                         kn[s2] = max(kn.get(s2, 0), v2)
         ins = o["fn"]()
         if o["kind"] == "dma":
-            ins.then_inc(T.sem[o["x"]], 16)
-            o["tok"] = (o["x"], 16)
-        elif o["kind"] == "send":
-            totals["sent"] = totals.get("sent", 0) + neng
-            continue
+            o["tok"] = o["x"]
         elif i in needed:
             count[e] = count.get(e, 0) + 1
             ins.then_inc(T.sem[csem[e]], 1)
@@ -1184,6 +1206,6 @@ def rank_program(g, core, T, topo):
     if rank is None:
         relay_program(g, core, T, topo)
         return
-    ops, neng = build(g, core, T, topo, rank)
+    ops = build(g, core, T, topo, rank)
     dependences(ops)
-    emit(g, T, ops, schedule(ops), neng)
+    emit(g, T, ops, schedule(ops))

from concourse.mybir import AluOpType as ALU, ActivationFunctionType as ACT

CN, Q0, S, H, RO, EPS, RHO = 1280, 384, 192, 64, 4, 44, 60
LN = S + H
NEW = [0, S, S + LN, S + 2 * LN]
C0 = LN
CT, QT = CN + NEW[3], Q0 + NEW[3]
LO = 2 * LN + QT
X0 = 128
B1 = (RHO + 1) * 65536
B2 = EPS * 65536 + 32768
MAGIC = 1.5 * 2.0 ** 35
LNR = 0.668
GW = LN + S
F, BF, I32, U16, HF = "float32", "bfloat16", "int32", "uint16", "float16"

CFG = {
    "off": [(0, 1, 1), (0, 2, 1), (0, 2, 2), (1, 1, 0), (1, 1, 4), (1, 2, 0), (2, 1, 0), (2, 1, 4), (2, 2, 0),
            (2, 2, 4), (3, 1, 0), (3, 1, 4)],
    "f1": [(0, 2, 2), (1, 1, 4), (2, 1, 4), (2, 2, 4), (3, 1, 4), (1, 1, 7), (1, 2, 7), (2, 1, 7), (2, 2, 7)],
    "gm": [(t, p, 6) for t in (1, 2) for p in (1, 2)],
    "vm": [],
    "agv": [(3, 0), (3, 1)],
    "agm": [2, 2, 2, 1],
    "pieces": [[(0, 128, "r"), (128, 64, "r")]] * 3 + [[(0, 96, "s"), (96, 96, "s")]],
    "cut": [128, 128, 128, 96],
    "g3": [],
    "gw": [[0], [0, 1], [0, 1]], "gf": [[0, 1]] * 3, "ge": [[0]] * 3, "gc": [[0]] * 3,
    "sa": ["AC", "KC1", "KC2", "RMAX", "RMC", "LX", "LG", "CF"],
    "ga": [],
    "rq": [],
    "xr": [[(0, S, "vvvvvvvvvvvsssss+")], [(0, S, "vvvvvvgggggggggg+")], [(0, S, "g+gggg")], [(0, S, "g+gggg")]],
    "eg": 8, "hm": 4, "pm": 2, "stage": True,
    "iters": 12, "look": 0.5, "seed": 3, "noise": 200, "back": 0.02,
    "rounds": [(1, 480000, 0.008), (1, 200000, 0.004)], "tries": 3, "reach": 40, "cap": 0.001,
    "aim": 50, "far": 40, "window": 250, "stay": 4000,
    "cost": dict(f=1.15, gc=1.55, sc=4.2, pe=.5, sem=170, ov=0, dl=2200, rl=3200, gp=1.05, fs=1.4),
    "figs": [dict(f=1.1, gc=1.6, sc=4.0, pe=.47, sem=160, ov=5, dl=1750, rl=2500, gp=1.0, fs=1.0),
             dict(f=1.2, gc=1.45, sc=4.5, pe=.54, sem=190, ov=0, dl=2600, rl=4200, gp=1.1, fs=1.8)],
}
CYC = 0.83

_SB = {
    "XS": (X0 + 768, BF), "YS": (768, BF), "NBI": (Q0, I32), "DLI": (Q0, I32), "STI": (16, I32), "KK": (QT, BF),
    "CE": (C0 + CT, BF), "AC": (C0 + CT + GW - H, F), "NL": (LO + QT, F), "IOTA": (QT, F), "XREP": (768 * 16, BF),
    "X3": (768 * 16, BF), "D1": (4096, BF), "D20": (4096, BF), "D21": (4096, BF), "AG": (3072, F), "RR0": (3072, F),
    "RR1": (3072, F), "SC": (3072, F), "O1": (LN, U16), "O20": (LN, U16), "O21": (LN, U16), "CAND": (LN, HF),
    "LI": (LN, HF), "RQF": (LN, F), "RQ16": (LN, U16), "E": (16 * LN, BF), "CMB": (LN, BF), "W40": (768, F),
    "W41": (768, F), "M": (3 * 384, F), "XP": (384, F), "XQ": (384, F), "OHT": (384, BF), "GG": (S, F), "YO": (768, F),
    "IB": (128, BF), "NIB": (128, BF), "IH": (128, HF), "GI": (2 * GW, BF), "IOM": (3 * LN, F), "Z4": (144, BF),
    "NZ4": (144, BF), "ZS": (144, BF), "OBD": (128, BF), "NBD": (128, BF), "TRI": (128, BF), "TRB": (128, BF),
    "IDF": (128, F), "SL": (72, BF), "DM": (128, F), "BSEL": (8, F), "KC1": (128, BF), "KC2": (128, BF),
    "ONE2": (144, BF), "RB": (32, BF), "KPAT": (384, F), "GPAT": (128, F), "RMIN": (128, F), "RMAX": (128, F),
    "RMC": (128, F), "MD": (384, BF), "MT": (384, BF), "TI": (24, I32), "T2": (24, I32), "SEL": (24, I32),
    "RI": (24, I32), "IU": (24, U16), "WL": (16, F), "THL": (16, F), "THX": (16, F), "PI": (8, I32), "CF": (16, F),
    "BL": (8, U16), "LANEL": (16, F), "LX": (16, F), "LG": (16, F), "MCOL": (8, F), "ST16": (16, U16),
    "QL0": (16, U16), "QL1": (16, U16), "QL2": (16, U16), "QL3": (16, U16), "CLF": (8, F), "K1R": (16, F),
    "QF0": (16, F), "QF1": (16, F), "LVF": (16, F), "WINF": (16, F), "HD": (16, F), "HF": (16, F), "HM": (16, F),
    "HM2": (16, F), "YY": (16, F), "TB1": (16, F), "TB16": (16, U16), "TA1": (16, F), "WTH": (16, F),
    "TA16": (16, U16), "SI": (16, I32), "CI": (16, I32), "U4": (16, F), "CN16": (16, U16), "NW": (16, BF),
    "CUM": (16, BF), "GP": (16, F), "GP0": (16, U16), "PU1": (8, F), "PU2": (8, F), "PU3": (8, F),
    "SX0": (17, U16), "SX1": (17, U16), "LU0": (17, U16), "LU1": (17, U16), "XR0": (S, BF), "XR1": (S, BF),
    "SA0": (S, F), "SA1": (S, F), "LV2": (8, F),
}
_PS = ["K0", "K1", "R0", "R1", "CM", "TR", "F0", "F1"]
LINES = _PS + ["DM"]
SCRATCH = {}
POOL = {}
for _n in _SB:
    _w, _d = _SB[_n]
    if _w <= 16 and _n != "STI":
        POOL[_n] = ("SM" + _d, 16 * len([1 for _v in POOL.values() if _v[0] == "SM" + _d]))
        SCRATCH["SM" + _d] = ("sbuf", [128, POOL[_n][1] + 16], _d)
    else:
        SCRATCH[_n] = ("sbuf", [128, _w], _d)
SCRATCH["X3"] = ("sbuf", [128, 768, 16], BF)
for _n in _PS:
    SCRATCH[_n] = ("psum", [128, 512], F)
NDMA = 50
SEMAPHORES = (["sv", "ss", "st_", "sg", "hsent"] + ["dm%d" % i for i in range(NDMA)]
              + [a + b + c for a in "ghs" for b in "exa" for c in "01"])


def R(name, lo=0, hi=None, step=1, p0=0, p1=128, ps=1):
    if hi is None:
        hi = _SB[name][0] if name in _SB else 512
    return (name, lo, hi, step, p0, p1, ps)


def width(r):
    return len(range(r[1], r[2], r[3]))


def two_byte(r):
    return r[0] in _SB and _SB[r[0]][1] in (BF, U16, HF)


def psum(r):
    return r[0] not in _SB


def overlap(a, b):
    if a[2] <= b[1] or b[2] <= a[1]:
        return False
    if a[3] == b[3] and a[3] > 1 and (a[1] - b[1]) % a[3] != 0:
        return False
    return True


def route(T, topo, rank, t):
    n = len(T.cores)
    src, dst = T.cores[rank], T.cores[(rank + 1 + t % (n - 1)) % n]
    if topo.may_write(src, dst):
        return dst, None
    cand = [h for h in topo.cores_of(src) if T.rank_of(h) is None and topo.may_write(h, dst) and topo.may_write(src, h)]
    cand.sort(key=lambda h: (topo.die(h) != topo.die(src), h))
    return dst, cand[0]


def few_engines(topo, src, far):
    es = topo.engines(src, far)
    return sum(1 << e for e in es), len(es)


def far_core(T, topo, src):
    return [d for d in T.cores if topo.chip(d) != topo.chip(src) and topo.may_write(src, d)][0]


def landing(kind, t):
    return R("LU%d" % t, 0, 13) if kind == "x" else R({"e": "XR%d", "a": "SA%d"}[kind] % t)


def chunks(t):
    a = CFG["cut"][t]
    if t in CFG["g3"]:
        return [(0, a), (a, S - a), (S, H)]
    return [(0, a), (a, (LN if t in (1, 2) else S) - a)]


def xlanes(t):
    return 32 + 32 * max([u for ph in (1, 2) for u in range(S // 32) if (t, ph, u) not in CFG["off"]] + [-1])


def relay_program(g, core, T, topo):
    total = 0
    for t in range(2):
        for r in range(len(T.cores)):
            dst, via = route(T, topo, r, t)
            if via != core:
                continue
            src = T.cores[r]
            _, n_in = few_engines(topo, src, far_core(T, topo, src))
            mask, n = few_engines(topo, core, dst)
            rid, pid = topo.addr(dst, core)
            for kind in "exa":
                r_ = landing(kind, t)
                ap = T[r_[0]][:, r_[1]:r_[2]]
                g.wait_ge(T.sem["h%s%d" % (kind, t)], n_in)
                g.remote_dma(ap, ap, T.sem["g%s%d" % (kind, t)], T.sem.hsent, pid, rid, mask)
                total += n
    if total:
        g.wait_ge(T.sem.hsent, total)


def build(g, core, T, topo, rank):
    ops = []
    V, SE, PE, SY = g.vector, g.scalar, g.tensor, g.sync

    leases = [0]

    def lease(bank):
        leases[0] += 1
        return "%s#%d" % (bank, leases[0])

    def A(r):
        name, b = POOL.get(r[0], (r[0].split("#")[0], 0))
        if name == "X3":
            return T.X3[:, r[1] // 16:r[2] // 16, r[1] % 16 if r[3] > 1 else slice(0, 16)]
        return T[name][slice(r[4], r[5], r[6]) if r[6] > 1 else slice(r[4], r[5]),
                       slice(b + r[1], b + r[2], r[3]) if r[3] > 1 else slice(b + r[1], b + r[2])]

    def IND(w, o):
        return A(w).indirect(A(o))

    def op(eng, fn, rd, wr, work, kind="c", extra=None):
        ops.append({"eng": eng, "fn": fn, "rd": rd, "wr": wr, "work": work, "kind": kind, "x": extra,
                    "banks": sorted(set(r[0][:2] for r in rd + wr if psum(r))), "starts": False, "group": 0})

    def sc(x):
        return A(x) if isinstance(x, tuple) else x

    def refs(*xs):
        return [x for x in xs if isinstance(x, tuple)]

    def plain(o, *ins):
        return ("plain", width(o) * (0.5 if all(two_byte(r) for r in (o,) + ins) else 1))

    def vcopy(o, i):
        op("v", lambda: V.tensor_copy(A(o), A(i)), [i], [o], plain(o, i))

    def vts(o, i, s1, s2, o0, o1=None):
        if o1 is None:
            fn = lambda: V.tensor_scalar(A(o), A(i), sc(s1), None, o0)
        else:
            fn = lambda: V.tensor_scalar(A(o), A(i), sc(s1), sc(s2), o0, o1)
        op("v", fn, [i] + refs(s1, s2), [o], plain(o, i))

    def vtt(o, a, b, alu):
        op("v", lambda: V.tensor_tensor(A(o), A(a), A(b), alu), [a, b], [o],
           ("plain", width(o) * (1 if psum(a) or psum(b) else 2)))

    def vset(o, c):
        op("v", lambda: V.memset(A(o), c), [], [o], plain(o))

    def vscan(o, d0, d1, o0, o1):
        op("v", lambda: V.tensor_tensor_scan(A(o), A(d0), A(d1), 0.0, o0, o1), [d0, d1], [o], plain(o, d0, d1))

    def vgather(o, w, l):
        op("v", lambda: V.tensor_copy(A(o), IND(w, l)), [w, l], [o], ("gather", width(o)))

    def vgadd(o, w, l, c):
        op("v", lambda: V.tensor_scalar(A(o), IND(w, l), c, None, ALU.add), [w, l], [o], ("gather", width(o)))

    def vgtt(o, w, l, b, alu):
        op("v", lambda: V.tensor_tensor(A(o), IND(w, l), A(b), alu), [w, l, b], [o], ("gather", width(o)))

    def vscat(w, l, i):
        op("v", lambda: V.tensor_copy(IND(w, l), A(i)), [l, i], [w], ("scatter", width(i)))

    def vscat2(w, l, a, b, alu):
        op("v", lambda: V.tensor_tensor(IND(w, l), A(a), A(b), alu), [l, a, b], [w], ("scatter", width(a)))

    def act(o, i, func, bias=0.0, scale=1.0, first=0):
        op("s", lambda: SE.activation(A(o), A(i), func, bias=sc(bias), scale=sc(scale)), [i] + refs(bias, scale), [o],
           ("plain", width(o) + first))

    def affine(o, i, scale, bias):
        if o[0] in CFG["sa"]:
            act(o, i, ACT.Identity, bias, scale)
        else:
            vts(o, i, scale, bias, ALU.mult, ALU.add)

    def sgather(o, w, l, scale=1.0):
        op("s", lambda: SE.activation(A(o), IND(w, l), ACT.Copy, scale=scale), [w, l], [o], ("gather", width(o)))

    def mms(lst):
        def fn():
            ins = None
            for o, l, r, st, sp in lst:
                ins = PE.matmul(A(o), A(l), A(r), st, sp)
            return ins
        c = sum(max(min(64, width(l)), width(r)) * (1 if two_byte(l) else 4) for o, l, r, st, sp in lst)
        rd = []
        for o, l, r, st, sp in lst:
            rd += [x for x in (l, r) if x not in rd]
        op("t", fn, rd, [R(lst[0][0][0], min(m[0][1] for m in lst), max(m[0][2] for m in lst))], ("tensor", c))
        ops[-1]["starts"] = any(m[3] for m in lst)
        ops[-1]["group"] = (1 if lst[0][3] and not lst[-1][4] else 0) - (1 if lst[-1][4] and not ops[-1]["starts"] else 0)

    def held(lst, m):
        lst = [x + (i == 0, i == len(lst) - 1) for i, x in enumerate(lst)]
        whole = R(lst[0][0][0], min(x[0][1] for x in lst), max(x[0][2] for x in lst))
        for i in range(0, len(lst), m):
            mms(lst[i:i + m])
            ops[-1].update(group=int(i == 0), starts=i == 0, wr=[whole])
            if i == 0:
                ops[-1]["rd"] = ops[-1]["rd"] + [x[j] for x in lst for j in (1, 2)]

    def close():
        ops[-1]["group"] = -1

    def giota(o, pat, base, cm):
        if _SB[o[0]][1] == I32:
            fn = lambda: g.iota(A(o), pat, base, cm)
        else:
            fn = lambda: g.iota(A(o), pat, base, cm, allow_small_or_imprecise_dtypes=True)
        op("g", fn, [], [o], ("pool", 130 + 2 * width(o) * CYC))

    def gsel(o, i, pat, cmp_, base, cm):
        op("g", lambda: g.affine_select(A(o), A(i), pat, cmp_, 0.0, base, cm), [i], [o],
           ("pool", 170 + 2 * width(o) * CYC))

    def diagonal(o, c):
        if o[0] in CFG["ga"]:
            giota(o, [[0, 128]], c, 0)
            gsel(o, o, [[-1, 128]], ALU.is_equal, 0, 1)
        else:
            act(o, R("IB"), ACT.Copy, scale=float(c))

    ndma = [0]

    def dmas(q, pairs, rd, wr, after=()):
        k = ndma[0]
        ndma[0] += 1
        eng = {"y": SY, "s": SE, "g": g}[q]

        def fn():
            for out, in_ in pairs:
                eng.dma_start(out(), in_()).then_inc(T.sem["dm%d" % k], 16)
        sides = wr or rd
        size = sum(width(r) * len(range(r[4], r[5], r[6])) * (2 if two_byte(r) else 4) for r in sides)
        rows = sum(8 if r[6] < 16 else 1 for r in sides)
        op(q, fn, rd + list(after), wr, ("dma", len(pairs), rows, size), "dma", ("dm%d" % k, 16 * len(pairs)))

    def load(q, o, src, lo, hi, after=()):
        dmas(q, [(lambda: A(o), lambda: T[src][:, lo:hi])], [], [o], after)

    def copies(pairs, after=()):
        dmas("y", [((lambda r=o: A(r)), (lambda r=i: A(r))) for o, i in pairs], [i for o, i in pairs],
             [o for o, i in pairs], after)

    mask, neng = few_engines(topo, core, far_core(T, topo, core))
    n = len(T.cores)

    def send(t, kind, src):
        dst, via = route(T, topo, rank, t)
        to = dst if via is None else via
        rid, pid = topo.addr(to, core)
        sem, sent = T.sem[("g%s%d" if via is None else "h%s%d") % (kind, t)], "s%s%d" % (kind, t)
        land = landing(kind, t)
        op("g", lambda: g.remote_dma(A(land), A(src), sem, T.sem[sent], pid, rid, mask), [src], [],
           ("send", 1500 if kind == "e" else 500), "dma", (sent, neng))
        me = len(ops) - 1
        frm = (rank - 1 - t % (n - 1)) % n
        _, v2 = route(T, topo, frm, t)
        if v2 is None:
            cnt = few_engines(topo, T.cores[frm], far_core(T, topo, T.cores[frm]))[1]
        else:
            cnt = few_engines(topo, v2, core)[1]
        op(None, None, [], [land], ("arrive", 2 - t), "arr", ("g%s%d" % (kind, t), cnt, me))

    def xs(t, a, b):
        return R("XS", X0 + S * t + a, X0 + S * t + b)

    def scans(nm, c):
        return 128 * c + 384 * ["MN", "MB", "MX"].index(nm)

    load("y", R("STI"), "st", 0, 16)
    load("s", R("NBI"), "nb", 0, Q0)
    load("y", xs(0, 0, S), "xs", 0, S)
    load("s", R("KK", 0, Q0), "kq", 0, Q0)
    later = [R("STI")] if CFG["stage"] else []
    load("y", xs(1, 0, 3 * S), "xs", S, 768)
    load("y", R("DLI"), "dl", 0, Q0, later)
    load("y", R("CE", C0, C0 + CN), "cc", 0, CN, later)
    load("g", R("AC", C0, C0 + CN), "aa", 0, CN, later)
    load("y", R("YS"), "ys", 0, 768, later)
    for t in range(3):
        load("y", R("KK", Q0 + NEW[t], Q0 + NEW[t] + S), "xs", S * t, S * t + S, later)

    zm = R("XS", 0, X0)
    vset(zm, 0.0)
    for t in range(2):
        send(t, "e", xs(t, 0, S))
    vset(R("ONE2"), 1.0)
    if "AC" in CFG["sa"]:
        for a in range(0, C0, 128):
            act(R("AC", a, a + 128), zm, ACT.Copy)
    else:
        vset(R("AC", 0, C0), 0.0)
    for t in range(3):
        copies([(R("IOM", LN * t, LN * t + LN), R("AC", 0, LN))]
               + ([(R("GI", GW * t, GW * t + H), R("XS", 0, H))] if t < 2 else [])
               + ([(R("AC", C0 + CN + NEW[t] + S, C0 + CN + NEW[t + 1]), R("AC", 0, H))] if t else []), later)
    vset(R("CUM"), 0.0)
    vset(R("NW"), 1.0)
    vset(R("RI"), 0)
    vset(R("MCOL", 0, 1), 84.0)
    vset(R("RB"), -8192.0)
    giota(R("PI", 0, 1), [[0, 1]], 0, 1)
    giota(R("IOTA", 0, 72), [[1, 72]], 0, 0)
    giota(R("IOTA", 72, Q0), [[1, Q0 - 72]], 72, 0)
    giota(R("KPAT", 0, 128), [[0, 8], [1, 16]], 0, 0)
    giota(R("GPAT"), [[1, 8], [0, 16]], 0, 0)
    copies([(R("KPAT", a, a + 128), R("KPAT", 0, 128)) for a in ([128, 256] if CFG["g3"] else [128])]
           + [(R("M", CFG["cut"][0] // 128 * 128, 384), R("IOTA", CFG["cut"][0] // 128 * 128, 384))])
    copies([(R("M", 384), R("AC", C0, C0 + 768))])
    for t in range(RO - 1):
        a, w = Q0 + NEW[t], NEW[t + 1] - NEW[t]
        giota(R("IOTA", a, a + w), [[1, w]], a, 0)
        copies([(R("IOM", LN * t, LN * t + w, 1, 8 + t, 128, 16), R("IOTA", a, a + w, 1, 8 + t, 128, 16))])
    md = {}
    for l0, cnt in sorted(set(ch for t in range(RO - 1) for ch in chunks(t)), reverse=True):
        if l0 not in md:
            md[l0] = 128 * len(md)
            gsel(R("MD", md[l0], md[l0] + cnt), R("IOTA", l0, l0 + cnt), [[-1, cnt]], ALU.is_equal, 0, 1)
    vts(R("PI", 1, 2), R("PI", 0, 1), 15, None, ALU.bitwise_and)
    vts(R("PI", 2, 3), R("PI", 0, 1), 4, None, ALU.arith_shift_right)
    vcopy(R("CF", 0, 3), R("PI", 0, 3))
    p_, pm, pg, g8 = R("CF", 0, 1), R("CF", 1, 2), R("CF", 2, 3), R("CF", 4, 5)
    affine(g8, pg, 8.0, 7.0)
    kpat = R("KPAT", 0, 128)
    for nm, c, step, add, off in (("KC1", 5, 4096.0, 4096.0, B1), ("KC2", 9, 2048.0, 0.0, B2)):
        affine(R("CF", c, c + 1), p_, -step, step)
        affine(R("CF", c + 1, c + 2), p_, -off - add, add)
        affine(R(nm), kpat, R("CF", c, c + 1), R("CF", c + 1, c + 2))
    vts(R("DM"), kpat, pm, None, ALU.is_equal)
    vts(R("OBD"), R("GPAT"), pg, None, ALU.is_equal)
    vts(R("BSEL"), R("IOTA", 0, 8), pg, None, ALU.is_equal)
    gsel(R("IB"), R("ONE2", 0, 128), [[-1, 128]], ALU.is_equal, 0, 1)
    vcopy(R("IH"), R("IB"))
    diagonal(R("IDF"), 1)
    diagonal(R("TRB"), -1024)
    diagonal(R("NIB"), -1)
    for t in range(RO - 1):
        diagonal(R("MT", 128 * t, 128 * t + 128), CN + NEW[t])
    vts(R("SL"), R("IOTA", 0, 72), g8, 65536.0, ALU.is_equal, ALU.mult)
    gsel(R("TRI"), R("OBD"), [[1, 128]], ALU.is_gt, 0, -1)
    act(R("NBD"), R("OBD"), ACT.Copy, scale=-1.0)
    vset(R("Z4", 0, 16), 0.0)
    gsel(R("Z4", 16), R("OBD"), [[0, 32], [1, 4]], ALU.is_equal, 0, 0)
    act(R("NZ4"), R("Z4"), ACT.Copy, scale=-1.0)
    vts(R("RMIN"), kpat, 0.0, 2.0 ** 25, ALU.is_equal, ALU.mult)
    affine(R("RMAX"), R("RMIN"), -1.0, 4096.0)
    affine(R("RMC"), R("RMIN"), 0.625, -2.0 ** 24)
    vcopy(R("IU"), R("IOTA", 0, 24))
    vts(R("BL"), R("IOTA", 0, 8), 16.0, 15.0, ALU.mult, ALU.add)
    affine(R("LANEL"), R("IOTA", 0, 16), 16.0, pm)
    affine(R("LX", 0, 12), R("LANEL", 0, 12), 1.0, 2.0 ** 23 + H - C0)
    affine(R("LX", 12, 16), R("LANEL", 12, 16), 1.0, 2.0 ** 23 - S - C0)
    affine(R("LG"), R("LANEL"), 1.0, float(LN - 1024))
    affine(R("LV2", 0, 4), R("LANEL", 0, 4), 1.0, pm)
    act(R("WL"), R("LANEL"), ACT.Exp, bias=R("MCOL", 0, 1), scale=-LNR, first=1400)
    gsel(R("ZS"), R("ONE2"), [[1, 144]], ALU.is_equal, -15, -1)
    vts(R("CF", 8, 9), pm, 0.0, None, ALU.is_equal)
    act(R("ZS"), R("ZS"), ACT.Copy, scale=R("CF", 8, 9))
    act(R("THL"), R("WL"), ACT.Copy, scale=2.5)
    act(R("THX", 0, 12), R("WL", 0, 12), ACT.Copy, scale=2.5)
    vcopy(R("ST16"), R("STI"))
    vcopy(R("NL", LN, LN + Q0), R("NBI"))
    vcopy(R("NL", LO, LO + Q0), R("DLI"))
    vcopy(R("QL0", 12, 16), R("STI", 12, 16))
    vts(R("CLF", 0, 4), R("STI", 12, 16), float(LN), None, ALU.add)

    def repeat(eng, a, b, m):
        o, i, w = (lambda: T.X3[:, a:b, m:2 * m]), (lambda: T.X3[:, a:b, 0:m]), (b - a) * m
        fn = {"g": lambda: g.affine_select(o(), i(), [[0, b - a], [0, m]], ALU.is_ge, 0.0, 0, 0),
              "v": lambda: V.tensor_copy(o(), i()), "s": lambda: SE.activation(o(), i(), ACT.Copy)}[eng]
        op(eng, fn, [R("X3", 16 * a + k, 16 * b, 16) for k in range(m)],
           [R("X3", 16 * a + k, 16 * b, 16) for k in range(m, 2 * m)],
           {"g": ("pool", 170 + 2 * w * CYC), "v": ("plain", w / 2), "s": ("plain", w)}[eng])
        if m == 8:
            copies([(R("XREP", 16 * a, 16 * b), R("X3", 16 * a, 16 * b))])

    for t in range(RO):
        for a, b, who in CFG["xr"][t]:
            a, b = S * t + a, S * t + min(b, xlanes(t))
            single, double = who.split("+")
            for k, eng in enumerate(single if a < b else ""):
                o, i = R("X3" if double else "XREP", 16 * a + k, 16 * b, 16), xs(0, a, b)
                if eng == "g":
                    gsel(o, i, [[0, b - a]], ALU.is_ge, 0, 0)
                elif eng == "v":
                    vcopy(o, i)
                else:
                    act(o, i, ACT.Copy)
            for j, eng in enumerate(double if a < b else ""):
                repeat(eng, a, b, len(single) << j)

    def lists(t, ph, o16, of, win, lst, want_f):
        vgather(o16, R(["NBI", "DLI"][ph - 1]) if t == 0 else win, lst)
        if want_f:
            vts(of, o16, float(LN if ph == 1 else 0), None, ALU.add)

    def diffs(t, ph, l0, CH, dname, win, oname):
        u, u1 = l0 // 32, (l0 + CH) // 32
        have = u
        off = lambda v: v < u1 and (32 * v >= S or (t, ph, v) in CFG["off"])
        while u < u1:
            a = 32 * u
            if off(u):
                fb = lease("F1" if (t, ph, u) in CFG["f1"] else "F0")
                d = R(dname, a * 16, (a + 32) * 16)
                if have <= u:
                    have = u + (2 if off(u + 1) and (t, ph, u) in CFG["gm"] else 1)
                    sgather(R(dname, a * 16, 512 * have), win, R(oname, a, 32 * have))
                if a >= xlanes(t):
                    g0 = (t - 1) * GW + a - S
                    x = R("GI", g0, g0 + 32) if a >= S else xs(t, a, a + 32)
                    mms([(R(fb), R("IB"), d, True, False)]
                        + [(R(fb, k, 512, 16), R("NIB"), x, False, k == 15) for k in range(16)])
                else:
                    x = R("XREP", (S * t + a) * 16, (S * t + a + 32) * 16)
                    mms([(R(fb), R("IB"), d, True, False), (R(fb), R("NIB"), x, False, True)])
                ops[-1]["group"] = 1
                act(d, R(fb), ACT.Abs)
                close()
                u += 1
                continue
            m = 2 if (t, ph, u) in CFG["vm"] and u + 1 < u1 and not off(u + 1) else 1
            vgtt(R(dname, a * 16, (a + 32 * m) * 16), win, R(oname, a, a + 32 * m),
                 R("XREP", (S * t + a) * 16, (S * t + a + 32 * m) * 16), ALU.subtract)
            for v in range(u, u + m):
                act(R(dname, 512 * v, 512 * v + 512), R(dname, 512 * v, 512 * v + 512), ACT.Abs)
            u += m

    def keys(c, CH, l0, num, kc, dname):
        bank = "K%d" % c if c < 2 else lease("R1")
        full = R(bank, 0, 128, 1, 0, CH)
        mms([(full, R(num, l0, l0 + CH), R("IH"), True, False),
             (full, R("ONE2", 0, CH, 1, 0, 2), R(kc, 0, 128, 1, 0, 2), False, False)])
        mms([(R(bank, k % 2, 128, 2, 0, CH), R(dname, l0 * 16 + k, (l0 + CH) * 16, 16),
              R("SL", 7 - k // 2, 71 - k // 2), False, k == 15) for k in range(16)])
        if c == 2:
            ops[-1]["group"] = 0
            ops[-2]["rd"] = ops[-2]["rd"] + ops[-1]["rd"]
        return full

    def to_list(out, tile, m0, c, CH):
        x = R(tile, 128 * c, 128 * c + 128)
        vgtt(x, R("M", m0, m0 + 128), R("BL"), R("DM"), ALU.mult)
        mms([(out, x[:4] + (0, CH, 1), R("BSEL", 0, CH // 16, 1, 0, CH), True, True)])

    def pick_lists(out, src, w):
        mms([(out, R("ZS", 15 - l, 143 - l), R(src[0], src[1] + l, src[1] + w, 16), l == 0, l == 15) for l in range(16)])

    def predict(t, a, cnt, form):
        last = t == RO - 1
        lo = CN + NEW[t]
        O2, D2, rr, w4 = "O2%d" % (t % 2), "D2%d" % (t % 2), "RR%d" % (t % 2), "W4%d" % (t % 2)
        b = a + cnt
        yo = R("YO", S * t + a, S * t + b)
        reset = lambda bank, w: (R(bank, 0, w, 16), R("ONE2", 0, 128, 1, 0, 2), R("RB", 0, w // 16, 1, 0, 2))
        if form == "r":
            w = 4 * cnt if cnt <= 128 else 2 * cnt
            for c in range(0, 4 * cnt, w):
                wb, lst = lease("R%d" % (c // w)), []
                for j in range(4):
                    x = 16 * a + 4 * cnt * j + c
                    lst += [(R(wb, 0, w), R("Z4", 16 - j, 144 - j), R(D2, x, x + w)),
                            (R(wb, 1, w), R("NZ4", 16 - j, 144 - j), R(D2, x, x + w - 1))]
                held(lst + [reset(wb, w)], CFG["hm"])
                act(R(w4, 4 * a + c, 4 * a + c + w), R(wb, 0, w), ACT.Exp, scale=1.0 / 64)
                close()
            copies([(R(rr, 16 * a, 16 * b, 1, r, 128, 4), R(w4, 4 * a, 4 * b)) for r in range(4)])
        have = 0
        if form == "e":
            for j in range(a // 32, b // 32):
                bank, cols = lease("R%d" % (j % 2)), lambda nm: R(nm, 512 * j, 512 * j + 512)
                held([(R(bank), R("OBD"), cols(D2))], 1)
                act(cols(rr), R(bank), ACT.Exp, scale=-1.0 / 64)
                close()
                vgtt(cols("AG"), R("AC", C0, C0 + lo), R(O2, 32 * j, 32 * j + 32), cols(rr), ALU.mult)
            acc = lease("F1")
            held([(R(acc, 0, cnt), R("IDF"), R("AG", 16 * a + k, 16 * b, 16)) for k in range(16)], CFG["pm"])
            act(yo, R(acc, 0, cnt), ACT.Copy)
            close()
            dmas("y", [(lambda: T.yp[:, yo[1]:yo[2]], lambda: A(yo))], [yo], [])
            return
        for j in range(a // 32, b // 32):
            x, cols = 512 * j, lambda nm: R(nm, 512 * j, 512 * j + 512)
            if form == "s":
                bank = lease("R%d" % (j % 2))
                held([(R(bank), R("OBD"), cols(D2)), (R(bank, 1), R("NBD"), R(D2, x, x + 511)), reset(bank, 512)], 3)
                act(cols(rr), R(bank), ACT.Exp, scale=1.0 / 64)
                close()
            if have <= j:
                have = j + 1
                while have < min(b // 32, j + CFG["agm"][t]) and ((t, have) in CFG["agv"]) == ((t, j) in CFG["agv"]):
                    have += 1
                (vgather if (t, j) in CFG["agv"] else sgather)(R("AG", x, 512 * have), R("AC", C0, C0 + lo),
                                                               R(O2, 32 * j, 32 * have))
            vscan(cols("SC"), cols(rr), cols("AG"), ALU.mult, ALU.add)
        wb = R("TR", 64 + a, 64 + b)
        mms([(wb, R("OBD"), R(D2, 15 + a * 16, b * 16, 16), True, True)])
        act(wb, wb, ACT.Exp, scale=-1.0 / 64)
        vtt(yo, R("SC", 16 * a + 15, 16 * b, 16), wb, ALU.mult)
        if not last:
            xb = R("CM", 256 + a, 256 + b)
            mms([(xb, R("NIB"), R("YS", S * t + a, S * t + b), True, False), (xb, R("IDF"), R("GG", a, b), False, False),
                 (xb, R("IDF"), yo, False, True)])
            act(R("AC", C0 + lo + a, C0 + lo + b), xb, ACT.Copy, scale=-0.25)
        if last or b == S:
            yo = yo if last else R("YO", S * t, S * t + S)
            dmas("y", [(lambda: T.yp[:, yo[1]:yo[2]], lambda: A(yo))], [yo], [])

    def nearest(t, c):
        l0, CH = chunks(t)[c]
        b0, b1, m0, qf = l0 // 16, (l0 + CH) // 16, scans("MN", c), "QF%d" % (t % 2)
        old = R("NL", LN, LN + Q0 + NEW[max(t - 1, 0)])
        lists(t, 1, R("O1", l0, l0 + CH), R("CAND", l0, l0 + CH), old, R(["ST16", "QL0", "QL1", "QL2"][t], b0, b1), True)
        diffs(t, 1, l0, CH, "D1", R("KK", 0, Q0 + NEW[t]), "O1")
        kb = keys(c, CH, l0, "CAND", "KC1", "D1")
        vscan(R("M", m0, m0 + 128, 1, 0, CH), R("RMIN", 0, 128, 1, 0, CH), kb, ALU.add, ALU.min)
        if c == 2:
            close()
        to_list(R("TR", b0, b1), "XP", m0, c, CH)
        vts(R("K1R", b0, b1), R("TR", b0, b1), MAGIC, -MAGIC, ALU.add, ALU.add)
        vtt(R(qf, b0, b1), R("TR", b0, b1), R("K1R", b0, b1), ALU.subtract)
        vts(R("QL%d" % t, b0, b1), R(qf, b0, b1), -float(LN), None, ALU.add)

    def winners(t, c0, c1):
        l0, l1 = chunks(t)[c0][0], sum(chunks(t)[c1 - 1])
        b0, b1, qf = l0 // 16, l1 // 16, "QF%d" % (t % 2)
        ql, lst, nb_ = Q0 + NEW[t], R("QL%d" % t, b0, b1), lambda nm: R(nm, b0, b1)
        sgather(R("NL", LN + ql + l0, LN + ql + l1), R("NL", LN, LN + ql), lst)
        if t in CFG["rq"]:
            vgadd(R("RQ16", l0, l1), R("IOTA", 0, ql), lst, float(LN))
        if t < 2 or t not in CFG["rq"]:
            sgather(R("RQF", l0, l1), R("IOTA", 0, ql), lst)
        if t not in CFG["rq"]:
            vts(R("RQ16", l0, l1), R("RQF", l0, l1), float(LN), None, ALU.add)
        e = lambda b: R("E", LN * b + max(16 * b, l0), LN * b + l1)
        for b in range(b1):
            vts(e(b), R("RQ16", max(16 * b, l0), l1), R(qf, b, b + 1), R("WL", b, b + 1), ALU.is_equal, ALU.mult)
        for a in range(0, b1, CFG["eg"]):
            mms([(R("CM", max(16 * b, l0), l1), R("OBD"), e(b), b == 0, b == b1 - 1)
                 for b in range(a, min(b1, a + CFG["eg"]))])
        act(R("CMB", l0, l1), R("CM", l0, l1), ACT.Copy)
        pick_lists(R("TR", 48 + b0, 48 + b1), R("CMB", l0), l1 - l0)
        vtt(nb_("WINF"), R("TR", 48 + b0, 48 + b1), nb_("THX"), ALU.is_lt)
        vtt(nb_("HD"), nb_(qf), nb_("WINF"), ALU.mult)
        vtt(nb_("HF"), nb_("HD"), nb_("K1R"), ALU.min)

    def dictionary(t, c):
        l0, CH = chunks(t)[c]
        b0, b1, mb, mx = l0 // 16, (l0 + CH) // 16, scans("MB", c), scans("MX", c)
        O2, D2 = "O2%d" % (t % 2), "D2%d" % (t % 2)
        lists(t, 2, R(O2, l0, l0 + CH), R("LI", l0, l0 + CH), R("NL", LO, LO + Q0 + NEW[t]), R("QL%d" % t, b0, b1),
              t < RO - 1)
        diffs(t, 2, l0, CH, D2, R("CE", C0, C0 + CN + NEW[t]), O2)
        if t == RO - 1:
            return
        kb = keys(c, CH, l0, "LI", "KC2", D2)
        vscan(R("M", mb, mb + 128, 1, 0, CH), R("RMC", 0, 128, 1, 0, CH), kb, ALU.max, ALU.min)
        vscan(R("M", mx, mx + 128, 1, 0, CH), R("RMAX", 0, 128, 1, 0, CH), kb, ALU.add, ALU.max)
        if c == 2:
            ops[-1]["rd"].append(R("M", mb, mb + 128))
            close()
        to_list(R("TR", 16 + b0, 16 + b1), "XQ", mb, c, CH)

    def forks(t, c0, c1):
        l0, l1 = chunks(t)[c0][0], sum(chunks(t)[c1 - 1])
        ql, nb_ = Q0 + NEW[t], lambda nm: R(nm, l0 // 16, l1 // 16)
        nnew = R("NL", LN + ql + l0, LN + ql + l1)
        vtt(nb_("YY"), R("TR", 16 + l0 // 16, 16 + l1 // 16), nb_("HF"), ALU.min)
        vtt(nb_("TA1"), nb_("YY"), nb_("LANEL"), ALU.max)
        vcopy(nb_("TA16"), nb_("TA1"))
        vscat2(R("NL", 0, LN + ql), nb_("TA16"), nnew, R("IOM", LN * t + l0, LN * t + l1), ALU.max)
        if t < 2:
            copies([(nnew[:4] + (t, 128, 16), R("RQF", l0, l1, 1, t, 128, 16))])

    def entries(t, c0, c1):
        l0, l1 = chunks(t)[c0][0], sum(chunks(t)[c1 - 1])
        np_, ql, nb_ = chunks(t)[c0][1], Q0 + NEW[t], lambda nm: R(nm, l0 // 16, l1 // 16)
        e8 = lambda nm: R(nm, 8 * c0, 8 * c1, 1, 0, np_)
        ends = lambda nm: R("M", scans(nm, c0) + 15, scans(nm, c0) + 128 * (c1 - c0), 16, 0, np_)
        vts(e8("TI"), ends("MX"), -1.0, float(30 * 2048 + 2047), ALU.mult, ALU.add)
        vts(e8("T2"), e8("TI"), 32767, None, ALU.bitwise_and)
        vtt(e8("SEL"), ends("MB"), e8("T2"), ALU.min)
        vts(e8("RI"), e8("SEL"), 11, 15, ALU.arith_shift_right, ALU.bitwise_and)
        vgtt(R("OHT", 128 * c0, 128 * c1), R("RI", 8 * c0, 8 * c1), R("IU", 0, 8 * (c1 - c0)),
             R("KPAT", 0, 128 * (c1 - c0)), ALU.is_equal)
        for c in range(c0, c1):
            a, cnt = chunks(t)[c]
            oh, oht = R("TR", 256 + a, 256 + a + cnt), R("OHT", 128 * c, 128 * c + 128, 1, 0, cnt)
            mms([(oh, oht, R("MD", md[a], md[a] + cnt, 1, 0, cnt), True, False),
                 (oh, oht, R("MT", 128 * t, 128 * t + cnt, 1, 0, cnt), False, True)])
        dnew = R("NL", LO + ql + l0, LO + ql + l1)
        vtt(nb_("HM"), nb_("HD"), nb_("LANEL"), ALU.max)
        vtt(nb_("HM2"), nb_("HM"), nb_("LANEL"), ALU.add)
        vtt(nb_("TB1"), nb_("HM2"), nb_("TA1"), ALU.subtract)
        vcopy(nb_("TB16"), nb_("TB1"))
        vtt(dnew, R("TR", 256 + l0, 256 + l1), R("LI", l0, l1), ALU.max)
        vscat(R("NL", LO - LN, LO + ql), nb_("TB16"), dnew)

    def centres(t, c0, c1):
        l0, l1 = chunks(t)[c0][0], sum(chunks(t)[c1 - 1])
        b0, lo, nb_ = l0 // 16, CN + NEW[t], lambda nm: R(nm, l0 // 16, l1 // 16)
        w0 = H if l1 <= S else 0
        vcopy(nb_("SI"), R("TR", 16 + b0, 16 + l1 // 16))
        vts(nb_("CI"), nb_("SI"), 2 ** 23 + 2047, None, ALU.bitwise_and)
        vtt(nb_("U4"), nb_("CI"), nb_("LX"), ALU.max)
        vts(nb_("CN16"), nb_("U4"), float(C0 - w0 - 2 ** 23), None, ALU.add)
        sgather(R("CE", C0 + lo + l0, C0 + lo + l1), R("CE", w0, C0 + lo), nb_("CN16"))
        if l0 < S:
            sgather(R("GG", l0, min(l1, S)), R("AC", w0, C0 + lo), R("CN16", b0, min(l1, S) // 16), -4.0)

    def guests_in(t):
        ql, lu, g0 = Q0 + NEW[t], "LU%d" % (t - 1), (t - 1) * GW
        vscat(R("GI", g0, g0 + GW), R(lu, 0, 12), landing("e", t - 1))
        copies([(R("KK", ql + S, ql + LN), R("GI", g0, g0 + H)), (R("CE", 0, H), R("GI", g0, g0 + H))])
        vcopy(R("CF", 10 + t, 11 + t), R(lu, 12, 13))
        vts(R("LVF", 12, 16), R("LV2", 0, 4), R("CF", 10 + t, 11 + t), None, ALU.is_lt)
        vtt(R("THX", 12, 16), R("THL", 12, 16), R("LVF", 12, 16), ALU.mult)

    def guests_out(t):
        sx = R("SX%d" % t, 0, 13)
        affine(R("WTH", 0, 12), R("WINF", 0, 12), -2.0 ** 23, 2.0 ** 23)
        vtt(R("NW", 0, 12), R("TR", 16, 28), R("WTH", 0, 12), ALU.is_gt)
        vscan(R("CUM", 1, 13), R("ONE2", 0, 12), R("NW", 0, 12), ALU.mult, ALU.add)
        mms([(R("TR", 32, 45), R("TRI"), R("NW", 0, 13), True, False),
             (R("TR", 32, 45), R("TRB"), R("NW", 0, 13), False, False),
             (R("TR", 32, 45), R("OBD"), R("CUM", 0, 13), False, True)])
        vtt(R("GP", 0, 13), R("TR", 32, 45), R("LG", 0, 13), ALU.min)
        vts(sx, R("GP", 0, 13), 1024.0, None, ALU.add)
        send(t, "x", sx)

    early = set()
    for t in range(RO):
        last, nc = t == RO - 1, len(chunks(t))
        groups = lambda key: list(zip(CFG[key][t], CFG[key][t][1:] + [nc]))
        if not last:
            load("y", R("CE", H, LN), "xs", S * t, S * t + S)
        if t in (1, 2):
            guests_in(t)
        for c in range(nc):
            if (t, c) not in early:
                nearest(t, c)
        for c0, c1 in ([] if last else groups("gw")):
            winners(t, c0, c1)
        for c in range(nc):
            dictionary(t, c)
        if t == 1:
            vtt(R("PU1", 0, 4), R("QF1", 12, 16), R("CLF", 0, 4), ALU.subtract)
            vtt(R("PU2", 0, 4), R("PU1", 0, 4), R("LVF", 12, 16), ALU.mult)
            vtt(R("PU3", 0, 4), R("PU2", 0, 4), R("CLF", 0, 4), ALU.add)
            vts(R("QL1", 12, 16), R("PU3", 0, 4), -float(LN), None, ALU.add)
        if t < 2:
            guests_out(t)
        if not last:
            for c0, c1 in groups("gf"):
                forks(t, c0, c1)
                for c in range(c0, c1):
                    if c == 0 or (c == 1 and c1 < nc and sum(chunks(t + 1)[1]) == S):
                        nearest(t + 1, c)
                        early.add((t + 1, c))
            for c0, c1 in groups("ge"):
                entries(t, c0, c1)
            for c0, c1 in groups("gc"):
                centres(t, c0, c1)
        for a, cnt, form in CFG["pieces"][t]:
            predict(t, a, cnt, form)
        if t < 2:
            a, b = C0 + CN + NEW[t], C0 + CN + NEW[t + 1] + S
            send(t, "a", R("AC", a, a + S))
            vscat(R("AC", b, b + GW), R("LU%d" % t, 0, 12), landing("a", t))
    return ops


def price(ops, c):
    out = []
    for o in ops:
        w = o["work"]
        if w[0] == "plain":
            out.append((c["ov"] + max(64, w[1]) * CYC * c["f"], 0.0))
        elif w[0] == "gather":
            out.append(((50 if o["eng"] == "v" else 65) + w[1] * c["gc"] * CYC, 0.0))
        elif w[0] == "scatter":
            out.append((50 + w[1] * c["sc"] * CYC, 0.0))
        elif w[0] == "tensor":
            out.append((w[1] * c["pe"], 40.0))
        elif w[0] == "pool":
            out.append((w[1] * c["f"] * c.get("gp", 1.0), 0.0))
        elif w[0] == "dma":
            move = w[2] * c["dl"] / 40 + w[3] / 600
            if o["eng"] == "y":
                out.append((max(60 * w[1], move), c["dl"] - 100))
            else:
                out.append((1000 * c.get("fs", 1.0) if o["eng"] == "g" else 60, c["dl"] + move))
        elif w[0] == "send":
            out.append((w[1] * c.get("fs", 1.0), 0.4 * c["rl"]))
        else:
            out.append((0.0, c["rl"] * (w[1] - 0.4)))
    return out


def dependences(ops):
    hist = {}
    for i, o in enumerate(ops):
        deps = {}
        acc = [(r, False) for r in o["rd"]] + [(r, True) for r in o["wr"]]
        for r, w in acc:
            for (j, r2, w2) in hist.get(r[0], []):
                if j != i and (w or w2) and overlap(r, r2):
                    inorder = w and ops[j]["eng"] == o["eng"] == "t"
                    deps[j] = deps.get(j, False) or not inorder
        for r, w in acc:
            lst = hist.setdefault(r[0], [])
            if w and r[3] == 1 and r[4] == 0 and r[5] == 128 and r[6] == 1 and not psum(r):
                lst[:] = [e for e in lst if not (r[1] <= e[1][1] and e[1][2] <= r[2])]
            lst.append((i, r, w))
        if o["kind"] == "arr":
            deps[o["x"][2]] = False
        o["deps"] = deps


def one_pass(ops, cost, preds, succ, pri, back):
    n = len(ops)
    sem, look = CFG["cost"]["sem"], CFG["look"]
    left = [len(p) for p in preds]
    rdy = [cost[i][1] if back else 0.0 for i in range(n)]
    fin = [0.0] * n
    free, used, opened = {}, {b: {} for b in LINES}, set()
    ready = [i for i in range(n) if left[i] == 0]
    order = []
    while ready:
        est = {}
        for i in ready:
            o = ops[i]
            if back or not (o["starts"] and o["banks"][0] in opened):
                est[i] = max([rdy[i], free.get(o["eng"], 0.0)]
                             + [x + sem for b in o["banks"] for e, x in used[b].items() if e != o["eng"]])
        first = min(est, key=lambda i: (est[i] + look * cost[i][0], -pri[i]))
        e = ops[first]["eng"]
        pick = max([i for i in est if ops[i]["eng"] == e and est[i] <= est[first] + look * cost[first][0]],
                   key=lambda i: (pri[i], -i))
        ready.remove(pick)
        order.append(pick)
        end = est[pick] + cost[pick][0]
        if e:
            free[e] = end
        fin[pick] = end + (0.0 if back else cost[pick][1])
        for b in ops[pick]["banks"]:
            used[b][e] = fin[pick]
        if ops[pick]["group"] > 0:
            opened.add(ops[pick]["banks"][0])
        elif ops[pick]["group"] < 0:
            opened.discard(ops[pick]["banks"][0])
        for k in succ[pick]:
            hard = ops[pick]["deps"].get(k, True) if back else ops[k]["deps"].get(pick, True)
            rdy[k] = max(rdy[k], fin[pick] + (sem if hard else 0.0) + (cost[k][1] if back else 0.0))
            left[k] -= 1
            if left[k] == 0:
                ready.append(k)
    return order, fin


def improve(ops, order, moves, slack):
    n = len(ops)
    order = list(order)
    eng = ["vstgy".index(o["eng"]) if o["eng"] else 5 + i for i, o in enumerate(ops)] + [-99]
    lines = [[eng[i]] + [-1 - LINES.index(b) for b in o["banks"]] for i, o in enumerate(ops)]
    banked = [l[1:] for l in lines]
    preds, above = [], []
    for o in ops:
        far = 0
        for j in o["deps"]:
            far |= above[j]
        preds.append(set(j for j in o["deps"] if not far >> j & 1))
        above.append(far | sum(1 << j for j in preds[-1]))
    starts, group = [o["starts"] for o in ops], [o["group"] for o in ops]
    special = set(i for i in range(n) if starts[i] or group[i])
    pos = [0] * n + [-1]
    before, after = [{} for _ in range(n + 1)], [{} for _ in range(n + 1)]

    def link(seg, p0, first, final):
        last = dict(first)
        for p, i in enumerate(seg):
            pos[i] = p0 + p
            for l in lines[i]:
                j = last.get(l, n)
                before[i][l], after[j][l], last[l] = j, i, i
        for l, j in last.items():
            k = final.get(l, n)
            after[j][l], before[k][l] = k, j

    win, figs = [0, n], []
    for c in CFG["figs"]:
        pr = price(ops, c)
        cost, lat = [x[0] for x in pr] + [0.0], [x[1] for x in pr] + [0.0]
        ins = [[(j, lat[j] + (c["sem"] if ops[i]["deps"][j] else 0.0)) for j in sorted(preds[i])] for i in range(n)]
        outs = [[] for _ in range(n)]
        for i in range(n):
            for j, y in ins[i]:
                outs[j].append((i, y))
        figs.append((cost, lat, ins, outs, [y + c["sem"] for y in lat[:n]] + [0.0], [0.0] * (n + 1), [0.0] * (n + 1)))

    def heads(f, p, stop):
        cost, lat, ins, outs, hand, end, rest = f
        top = win[1]
        while p < top and p <= stop:
            i = order[p]
            p += 1
            e, b = eng[i], before[i]
            r = end[b[e]]
            for j, y in ins[i]:
                y += end[j]
                if y > r:
                    r = y
            for l in banked[i]:
                j = b[l]
                if eng[j] != e and end[j] + hand[j] > r:
                    r = end[j] + hand[j]
            r += cost[i]
            if r != end[i]:
                end[i] = r
                for k, y in outs[i]:
                    if pos[k] > stop:
                        stop = pos[k]
                for k in after[i].values():
                    if pos[k] > stop:
                        stop = pos[k]

    def tails(f, p, stop):
        cost, lat, ins, outs, hand, end, rest = f
        low = win[0]
        while p >= low and p >= stop:
            i = order[p]
            p -= 1
            e, a = eng[i], after[i]
            r = rest[a[e]]
            if lat[i] > r:
                r = lat[i]
            for k, y in outs[i]:
                y += rest[k]
                if y > r:
                    r = y
            for l in banked[i]:
                k = a[l]
                if k < n and eng[k] != e and rest[k] + hand[i] > r:
                    r = rest[k] + hand[i]
            r += cost[i]
            if r != rest[i]:
                rest[i] = r
                for j, y in ins[i]:
                    if pos[j] < stop:
                        stop = pos[j]
                for j in before[i].values():
                    if j < n and pos[j] < stop:
                        stop = pos[j]

    tmp = [0.0] * (n + 1)

    def through(f, seg, pa, pb, first, final, limit):
        cost, lat, ins, outs, hand, end, rest = f
        last, top = {}, 0.0
        for i in seg:
            e = eng[i]
            r = tmp[last[e]] if e in last else end[first[e]]
            last[e] = i
            for j, y in ins[i]:
                y += tmp[j] if pos[j] >= pa else end[j]
                if y > r:
                    r = y
            for l in banked[i]:
                if l in last:
                    j = last[l]
                    y = tmp[j]
                else:
                    j = first[l]
                    y = end[j]
                last[l] = i
                if eng[j] != e and y + hand[j] > r:
                    r = y + hand[j]
            r += cost[i]
            tmp[i] = r
            z = lat[i]
            for k, y in outs[i]:
                if pos[k] > pb and y + rest[k] > z:
                    z = y + rest[k]
            if r + z > top:
                top = r + z
                if top > limit:
                    return None
        for l, j in last.items():
            k = final[l]
            y = tmp[j] + rest[k] + (hand[j] if l < 0 and k < n and eng[k] != eng[j] else 0.0)
            if y > top:
                top = y
        return None if top > limit else top

    def waits(m, part):
        cost, lat, ins, outs, hand, end, rest = figs[m]
        out, total = [], span[m] - 0.01
        for i in [i for i in part if end[i] - cost[i] + rest[i] > total]:
            r = end[i] - cost[i] - 0.01
            for l, j in before[i].items():
                if (pos[j] >= win[0] and j not in preds[i]
                        and end[j] + (hand[j] if l < 0 and eng[j] != eng[i] else 0.0) > r):
                    out.append((j, i, m))
        return out

    def pause(f, total, i, back):
        cost, lat, ins, outs, hand, end, rest = f
        e, out, k, need = eng[i], [], i, cost[i] * draw(100) / 100.0
        if back:
            late = total - max([y + rest[j] for j, y in outs[i]] + [lat[i]]) - cost[i]
            for _ in range(CFG["far"]):
                k = after[k][e]
                if k == n or end[k] > late + cost[i]:
                    break
                j = after[k][e]
                if j < n and end[j] - cost[j] - end[k] >= need:
                    out.append(k)
        else:
            soon = max([y + end[j] for j, y in ins[i]] + [0.0])
            for _ in range(CFG["far"]):
                k = before[k][e]
                if k == n or end[k] < soon:
                    break
                if end[k] - cost[k] - max(end[before[k][e]], soon) >= need:
                    out.append(k)
        return out[draw(len(out))] if out else None

    def nests(seg, first):
        opened = {}
        for i in seg:
            if i in special:
                l = lines[i][1]
                if l not in opened:
                    j = first[l]
                    while j < n and not (group[j] and lines[j][1] == l):
                        j = before[j][l]
                    opened[l] = j < n and group[j] > 0
                if starts[i] and opened[l]:
                    return False
                if group[i]:
                    opened[l] = group[i] > 0
        return True

    x = [CFG["seed"]]

    def draw(m):
        x[0] = (x[0] * 1103515245 + 12345) % 2147483648
        return (x[0] >> 8) % m

    def longest():
        part = order[win[0]:win[1]]
        span[:] = [max([end[i] - cost[i] + rest[i] for i in part]) for cost, lat, ins, outs, hand, end, rest in figs]
        return sum(y * z for y, z in zip(span, scale)), sum([waits(m, part) for m in range(len(figs))], [])

    def afresh():
        link(order, 0, {}, {})
        win[:] = [0, n]
        for f in figs:
            heads(f, 0, n)
            tails(f, n - 1, 0)

    scale = [0.9 / sum(f[0][i] for i in range(n) if eng[i] == 0) for f in figs]
    reach, cap, it, edges, kept, span = CFG["reach"], CFG["cap"], 0, [], None, []
    while it < moves:
        if it % CFG["stay"] < CFG["tries"] or not edges:
            if kept:
                order[win[0]:win[1]] = kept
            afresh()
            win[0] = max(0, min(n - CFG["window"], draw(n) - CFG["window"] // 2))
            win[1] = min(n, win[0] + CFG["window"])
            best, edges = longest()
            kept = order[win[0]:win[1]]
            it += CFG["tries"]
            continue
        allow = slack * draw(1000) / 1000.0 * (1.0 - it % CFG["stay"] / CFG["stay"]) * (1.2 - it / moves)
        pick = None
        for _ in range(CFG["tries"]):
            it += 1
            a, b, m = edges[draw(len(edges))]
            pa, pb = pos[a], pos[b]
            kind = draw(3)
            if draw(100) < CFG["aim"]:
                k = pause(figs[m], span[m], a, draw(2))
                if k is None or not win[0] <= pos[k] < win[1]:
                    continue
                if pos[k] < pa:
                    kind, b, pb, pa = 3, a, pa, pos[k]
                else:
                    kind, b, pb = -1, n, pos[k]
            if kind > 0:
                if kind == 3:
                    pass
                elif kind == 2:
                    b, pb, pa = a, pa, max(win[0], pa - 1 - draw(reach))
                else:
                    pa = max(win[0], pa - (draw(12) if draw(3) == 0 else 0))
                moved, need, old = {b}, set(preds[b]), order[pa:pb + 1]
                for k in reversed(old):
                    if k in need:
                        moved.add(k)
                        need |= preds[k]
                if a in moved and kind == 1:
                    continue
                seg = [k for k in old if k in moved] + [k for k in old if k not in moved]
            else:
                pb = min(win[1] - 1, pb + (draw(reach) if draw(2) and kind == 0 else 0))
                old, moved = order[pa:pb + 1], {a}
                for k in old:
                    if preds[k] & moved:
                        moved.add(k)
                if b in moved:
                    continue
                seg = [k for k in old if k not in moved] + [k for k in old if k in moved]
            first, final = {}, {}
            for k in old:
                for l in lines[k]:
                    if l not in first:
                        first[l] = before[k][l]
                    final[l] = after[k][l]
            if moved & special and not nests(seg, first):
                continue
            s = 0.0
            for f, y, z in zip(figs, span, scale):
                top = through(f, seg, pa, pb, first, final, y + (allow + cap) / z)
                if top is None:
                    break
                s += max((top - y) * z, -cap)
            else:
                if s < allow:
                    allow, pick = s, (seg, pa, pb, first, final)
        if pick:
            seg, pa, pb, first, final = pick
            order[pa:pb + 1] = seg
            link(seg, pa, first, final)
            far = max(pos[k] for k in final.values())
            near = min(pos[k] if k < n else pa for k in first.values())
            for f in figs:
                heads(f, pa, max(pb, far))
                tails(f, pb, min(pa, near))
            s, edges = longest()
            if s < best:
                best, kept = s, order[win[0]:win[1]]
    order[win[0]:win[1]] = kept
    afresh()
    return longest()[0], order, figs[0][5]


PLAN = []


def schedule(ops):
    n = len(ops)
    if not PLAN:
        cost = price(ops, CFG["cost"])
        preds = [list(o["deps"]) for o in ops]
        succ = [[] for _ in ops]
        for i in range(n):
            for j in preds[i]:
                succ[j].append(i)
        pri = [0.0] * n
        for i in range(n - 1, -1, -1):
            pri[i] = sum(cost[i]) + CFG["cost"]["sem"] + max([pri[k] for k in succ[i]] + [0.0])
        plans = []
        for it in range(CFG["iters"]):
            order, fin = one_pass(ops, cost, preds, succ, pri, False)
            plans = sorted(plans + [(max(fin), order)])
            if max(fin) < plans[0][0] * (1 + CFG["back"]):
                base = fin
            pri = one_pass(ops, cost, succ, preds, base, True)[1]
            x = CFG["seed"] * 7919 + it
            for i in range(n):
                x = (x * 1103515245 + 12345) % 2147483648
                pri[i] += CFG["noise"] * x / 2147483648
        for keep, moves, slack in CFG["rounds"]:
            plans = sorted([improve(ops, p[1], moves, slack) for p in plans[:keep]] + [p for p in plans if len(p) > 2])
        PLAN.extend(plans[0][1:])
    seen = {b: {} for b in LINES}
    for i in PLAN[0]:
        o = ops[i]
        o["t0"] = PLAN[1][i]
        for b in o["banks"]:
            for e, j in seen[b].items():
                if e != o["eng"]:
                    o["deps"][j] = True
            seen[b][o["eng"]] = i
    return PLAN[0]


def emit(g, T, ops, order):
    queue = {"v": g.vector, "s": g.scalar, "t": g.tensor, "g": g, "y": g.sync}
    csem = {"v": "sv", "s": "ss", "t": "st_", "g": "sg"}
    needed = set()
    for o in ops:
        if o["kind"] != "arr":
            needed.update(j for j in o["deps"] if o["deps"][j])
    count = {}
    known = {e: {} for e in queue}
    totals = {}
    for i in order:
        o = ops[i]
        if o["kind"] == "arr":
            o["tok"] = (o["x"][0], o["x"][1])
            o["clock"] = {o["x"][0]: o["x"][1]}
            totals[o["x"][0]] = o["x"][1]
            continue
        e = o["eng"]
        kn = known[e]
        want = sorted([j for j in o["deps"] if o["deps"][j]], key=lambda j: -ops[j]["t0"])
        for j in want:
            s, v = ops[j]["tok"]
            if kn.get(s, 0) >= v:
                continue
            v = max(ops[k]["tok"][1] for k in want if ops[k]["tok"][0] == s)
            queue[e].wait_ge(T.sem[s], v)
            for k in want:
                if ops[k]["tok"][0] == s:
                    for s2, v2 in ops[k]["clock"].items():
                        kn[s2] = max(kn.get(s2, 0), v2)
        ins = o["fn"]()
        if o["kind"] == "dma":
            o["tok"] = o["x"]
        elif i in needed:
            count[e] = count.get(e, 0) + 1
            ins.then_inc(T.sem[csem[e]], 1)
            o["tok"] = (csem[e], count[e])
        else:
            continue
        o["clock"] = dict(kn)
        o["clock"][o["tok"][0]] = o["tok"][1]
        totals[o["tok"][0]] = o["tok"][1]
    for s in totals:
        if not any(known[e].get(s, 0) >= totals[s] for e in known):
            g.wait_ge(T.sem[s], totals[s])


def rank_program(g, core, T, topo):
    rank = T.rank_of(core)
    if rank is None:
        relay_program(g, core, T, topo)
        return
    ops = build(g, core, T, topo, rank)
    dependences(ops)
    emit(g, T, ops, schedule(ops))
